import numpy as np, ml_dtypes
CORES = [242,247,114,119]
N = 4
BF = ml_dtypes.bfloat16
W, C, M, V, D, Q = 2048, 256, 5, 4, 1, 9
LM = 127
def parts(rng):
    return (rng.integers(0, 256, (N, 8, 16, W)), rng.integers(0, W, (N, 8, 16, C)), rng.integers(0, 256, (N, 8, 16, C)),
            rng.integers(0, 16, (N, 8, 16, 1)), rng.integers(48, 81, (N, 8, 16, 1)))
def pack(x, f, z, w, lm):
    return {"rock": x.reshape(N, 128, W).astype(np.float32).astype(BF), "front": np.ascontiguousarray(f.reshape(N, 128, C)).astype(np.int32),
            "vein": z.reshape(N, 128, C).astype(np.float32).astype(BF), "w": w.reshape(N, 128, 1).astype(np.int32), "lim": lm.reshape(N, 128, 1).astype(np.int32)}
def setup_inputs(rng):
    return pack(*parts(rng))
def setup_inputs_alike(rng):
    x, f, z, w, lm = parts(rng); lm = rng.integers(10, 41, (N, 8, 16, 1)); rec = rng.integers(100, 156, (N, 8, 16, 4))
    x = np.take_along_axis(rec, rng.integers(0, 4, (N, 8, 1, W)), 3)
    far = lm + rng.choice(np.array([-1, 0, 0, 0, 1, 2, 3, 4]), (N, 8, 16, C))
    z = np.take_along_axis(rec, rng.integers(0, 4, (N, 8, 1, C)), 3) + rng.choice(np.array([-1, 1]), (N, 8, 16, C)) * far
    f[:, ::2] = rng.choice(np.array([0, W - 1, W // 2, 3]), (N, 4, 16, C))
    f[:, 1] = f[:, 1][..., rng.integers(0, 4, C)]
    return pack(x, f, z, w, lm)
def setup_inputs_corners(rng):
    x, f, z, w, lm = parts(rng); end = np.array([0, 1, 14, 15]); P = C // 2; h = np.arange(P)
    for a in range(N):
        o = [int(b) for b in rng.permutation(8)]
        for g in range(8):
            v = o[g]
            if v == 0:
                lm[a, g] = 0; w[a, g] = 0
            elif v == 1:
                lm[a, g] = LM; w[a, g] = 15
            elif v in (2, 3, 4):
                x[a, g] = rng.integers(200, 256, (16, W)); z[a, g] = rng.integers(0, 61, (16, C)); lm[a, g] = rng.integers(0, 101, (16, 1))
                s = np.arange(16)[:, None] * (W // 32) + rng.integers(0, W // 32, (16, P)); j = rng.integers(W // 2, W, (16, P))
                if v == 2:
                    k = rng.choice(end, P); l = rng.choice(end, P); k[:16] = np.repeat(end, 4); l[:16] = np.tile(end, 4)
                    s[np.maximum(l, rng.integers(0, 16, P)), h] = s[l, h]
                    j[k, h] = (s[l, h] & -8) + rng.integers(0, 8, P)
                    j[np.maximum(k, rng.integers(0, 16, P)), h] = j[k, h]
                if v == 4:
                    s[:] = W - 1; j[:] = W - 1; s[:, :P // 2] = 0; j[:, :P // 2] = 0
                    s[1:, P // 2:3 * P // 4] = W - 21; j[1:, P // 2:3 * P // 4] = W - 3
                f[a, g][:, 0::2] = s; f[a, g][:, 1::2] = j
            elif v == 5:
                r = rng.integers(64, 192, (16, 1)); x[a, g] = r; lm[a, g] = 0
                off = np.argsort(rng.random((16, C)), axis=0) >= rng.integers(Q - 2, Q + 2, C)[None, :]
                z[a, g] = r + np.where(off, rng.choice(np.array([-40, -4, 4, 40]), (16, C)), 0)
            elif v == 6:
                f[a, g] = (W - 1) * rng.integers(0, 2, (16, C)); w[a, g] = 15 * rng.integers(0, 2, (16, 1)); lm[a, g] = LM * rng.integers(0, 2, (16, 1))
            else:
                w[a, g, 0] = 15; w[a, g, 1] = 1; z[a, g][:, ::2] = 0; z[a, g, 0, ::2] = 136; z[a, g, 1, ::2] = 7; f[a, g][:, ::4] = W - 1
                for i, n, u, m in ((2, W - 3, 2037, 0), (6, W - 15, 2039, 2)):
                    z[a, g, 0, i::8] = 135; z[a, g, 1, i::8] = u - 2025; f[a, g][:, i::8] = n
                    x[a, g][:, (((n * (2 * u + 1)) >> (5 + m)) + n + 613 * m + 37 * np.arange(16)) & (W - 1)] = z[a, g][:, i][:, None]
    return pack(x, f, z, w, lm)
def setup_inputs_ends(rng):
    x, f, z, w, lm = parts(rng)
    x = 255 * np.where(rng.random((N, 8, 1, W)) < 0.4, rng.integers(0, 2, (N, 8, 1, W)), rng.integers(0, 2, (N, 8, 16, W)))
    z = 255 * np.where(rng.random((N, 8, 1, C)) < 0.4, rng.integers(0, 2, (N, 8, 1, C)), rng.integers(0, 2, (N, 8, 16, C)))
    f = (W - 1) * rng.integers(0, 2, f.shape); w = 15 * rng.integers(0, 2, w.shape); lm = LM * rng.integers(0, 2, lm.shape)
    for a, g in ((N - 1, 7), (0, 0)):
        w[a, g] = 15; z[a, g][:, [0, C - 2, C - 1]] = 255; z[a, g][:, [3, C - 3]] = 0
        z[a, g][:, [5, C - 4]] = rng.permutation(np.array([255] * 9 + [26] + [0] * 6))[:, None]
        f[a, g, 15][[0, 3, 5, C - 4, C - 3, C - 2, C - 1]] = W - 1
        for u in ((16 * 15 * 255) & 2047, 0):
            x[a, g][:, ((((W - 1) * (2 * u + 1)) >> (5 + np.arange(M))) + W - 1 + 613 * np.arange(M) + 37 * 15) & (W - 1)] = 0
    return pack(x, f, z, w, lm)
def setup_inputs_full(rng):
    x, f, z, w, lm = parts(rng); P = C // 2; h = np.arange(P); n = W // C
    b = int(rng.integers(0, N)); g = int(rng.integers(0, 8)); rest = [q for q in range(N) if q not in (b, (b - D) % N)]; a = rest[int(rng.integers(0, len(rest)))]
    for q in range(N):
        if q != a:
            x[q, g] = rng.integers(200, 256, (16, W)); z[q, g] = rng.integers(0, 61, (16, C)); lm[q, g] = 0
            f[q, g] = n * rng.permutation(C)[None, :] + rng.integers(0, n, (16, C))
    i = np.array([P - 1, 0, P // 2])[:int(rng.integers(1, 4))]
    f[b, g, 15, 2 * i + 1] = (f[b, g, rng.integers(0, 16, len(i)), 2 * i] & -8) + rng.integers(0, 8, len(i))
    x[a] = rng.integers(200, 256, (8, 16, W)); z[a] = rng.integers(0, 61, (8, 16, C)); lm[a] = rng.integers(80, 121, (8, 16, 1))
    k = rng.integers(0, 16, (8, P)); l = rng.integers(0, 16, (8, P)); gr = np.arange(8)[:, None]; fa = f[a]
    fa[gr, k, 2 * h + 1] = (fa[gr, l, 2 * h] & -8) + rng.integers(0, 8, (8, P))
    o = [int(c) for c in rng.permutation(8)]
    f[a, o[0]] = 0; w[a, o[0]] = 0
    f[a, o[1]] = W - 1; w[a, o[1]] = 0; w[a, o[1], 0] = W >> 9; z[a, o[1], 0] = 32
    return pack(x, f, z, w, lm)
def setup_inputs_spread(rng):
    x = np.minimum((np.exp2(8 * rng.random((N, 8, 1, W))) * rng.random((N, 8, 16, W))).astype(np.int64), 255)
    z = np.minimum((np.exp2(8 * rng.random((N, 8, 1, C))) * rng.random((N, 8, 16, C))).astype(np.int64), 255)
    f = np.minimum((W * rng.random((N, 8, 16, C)) ** 3).astype(np.int64), W - 1)
    return pack(x, f, z, rng.integers(0, 16, (N, 8, 16, 1)), np.minimum((128 * rng.random((N, 8, 16, 1)) ** 2).astype(np.int64), LM))
def check_inputs(d):
    bad = []
    for k, hi in (("rock", 255), ("front", W - 1), ("vein", 255), ("w", 15), ("lim", LM)):
        v = np.asarray(d[k]).astype(np.float64)
        if not (np.min(v) >= 0 and np.max(v) <= hi): bad.append("range of " + k)
        elif np.any(v != np.floor(v)): bad.append("whole numbers in " + k)
    return bad
def reference(rock, front, vein, w, lim):
    x = rock.astype(np.float32).astype(np.int64).reshape(N, 8, 16, W)
    f = front.astype(np.int64).reshape(N, 8, 16, C)
    z = vein.astype(np.float32).astype(np.int64).reshape(N, 8, 16, C)
    wt = w.astype(np.int64).reshape(N, 8, 16, 1); lm = lim.astype(np.int64).reshape(N, 8, 16, 1)
    place = np.arange(16)[:, None]; ci = np.arange(C); met = np.zeros(N, np.int64)
    for t in range(V):
        if t > 0:
            f = np.roll(f, D, axis=0); z = np.roll(z, D, axis=0)
        u = np.add.reduce(wt * z, axis=2) & 2047
        dig = np.add.reduce(z, axis=2) & 15
        top = (lm + (met & 3)[:, None, None, None])[..., None]
        for m in range(M):
            c = (((f * (2 * u[:, :, None, :] + 1)) >> (5 + m)) + f + 613 * m + 37 * place) & (W - 1)
            v = np.take_along_axis(x, c.reshape(N, 8, 1, 16 * C), 3).reshape(N, 8, 16, 16, C)
            dif = np.abs(v - z[:, :, :, None, :])
            score = np.add.reduce(dif, axis=2); near = np.count_nonzero(dif <= top, axis=2)
            if m == 0:
                bs, bc, bn = score, c, near
            else:
                less = score < bs; bs = np.where(less, score, bs); bc = np.where(less, c, bc); bn = np.where(less, near, bn)
        f = np.where(bn >= Q, bc, f)
        sen = ci[((ci >> t) & 1) == 0]; jun = sen + (1 << t)
        fs = f[..., sen]; fj = f[..., jun]
        eq = ((fj[:, :, :, None, :] >> 3) == (fs[:, :, None, :, :] >> 3)).reshape(N, 8, 256, C // 2)
        meet = np.any(eq, axis=2)[:, :, None, :]; first = np.argmax(eq, axis=2)[:, :, None, :]
        k = first >> 4; l = first & 15
        met = np.count_nonzero(meet, axis=(1, 2, 3))
        src = place - l + k
        ns = np.where(meet & (place > l) & (src <= 15), np.take_along_axis(fj, np.minimum(np.maximum(src, 0), 15), 2), fs)
        nj = np.where(meet & (place >= k), (((fj * fs) >> 5) + fj + u[..., jun][:, :, None, :]) & (W - 1), fj)
        f = f.copy(); f[..., sen] = ns; f[..., jun] = nj
        e = np.take_along_axis(f, dig[:, :, None, :], 2)
        old = np.take_along_axis(x, e, 3)
        lo = np.full((N, 8, W), C)
        np.minimum.at(lo, (np.arange(N)[:, None, None], np.arange(8)[None, :, None], e[:, :, 0]), np.broadcast_to(ci, (N, 8, C)))
        zl = np.take_along_axis(z, np.minimum(lo, C - 1)[:, :, None, :], 3)
        x = np.where((lo < C)[:, :, None, :], np.maximum(x - (zl >> 2), 0), x)
        z = (z + old) >> 1
    return {"yx": x.reshape(N, 128, W).astype(np.float32).astype(BF), "yf": f.reshape(N, 128, C).astype(np.float32), "yz": z.reshape(N, 128, C).astype(np.float32).astype(BF)}

@@ -1,0 +1,574 @@
+from concourse.mybir import dt, AluOpType as Op, AxisListType, ActivationFunctionType as Act
+
+NEXT = 1
+CH = [("S", 0, 64), ("V", 64, 128), ("S", 128, 192), ("S", 192, 256)]
+GR = [(0, 128), (128, 256)]
+NV = [b - a for k, a, b in CH if k == "V"][0]
+SUB = 16
+KN = 2956 * 10240 - (1 << 24)
+
+f32, bf, f16, i32, u16 = "float32", "bfloat16", "float16", "int32", "uint16"
+SCRATCH = {
+    "X": ("sbuf", [128, 2560], bf), "fin": ("sbuf", [128, 256], i32), "win": ("sbuf", [128, 1], i32), "lin": ("sbuf", [128, 1], i32),
+    "A": ("sbuf", [128, 20480], bf), "D": ("sbuf", [128, 80 * NV], bf), "NR": ("sbuf", [128, 20480], bf), "Zx": ("sbuf", [128, 16 * NV], bf),
+    "off6": ("sbuf", [128, 1536], u16), "offV": ("sbuf", [128, 5 * NV], u16), "c16": ("sbuf", [128, 1280], f16),
+    "usi": ("sbuf", [128, 512], i32), "u2": ("sbuf", [128, 256], i32), "si": ("sbuf", [128, 256], i32),
+    "zq": ("sbuf", [128, 256], f16), "P": ("sbuf", [128, 256], f32), "Q": ("sbuf", [128, 1280], i32), "C": ("sbuf", [128, 1280], i32),
+    "Kn": ("sbuf", [128, 256], f32), "KB": ("sbuf", [128, 256], f32), "EQm": ("sbuf", [128, 1280], bf), "TT": ("sbuf", [128, 1280], bf),
+    "KF": ("sbuf", [128, 256], f32), "K1": ("sbuf", [128, 256], f32), "K2": ("sbuf", [128, 256], f32), "KI": ("sbuf", [128, 256], i32),
+    "SJ": ("sbuf", [128, 256], f16), "Hh": ("sbuf", [128, 256], f16), "EQ2": ("sbuf", [128, 2048], bf), "MK": ("sbuf", [128, 2048], f16),
+    "PJ": ("sbuf", [128, 2048], f16), "LT": ("sbuf", [128, 128], bf), "KX": ("sbuf", [128, 16], f32), "ph": ("sbuf", [128, 768], f16),
+    "pb": ("sbuf", [128, 512], bf), "JS": ("sbuf", [128, 128], f32), "JQ": ("sbuf", [128, 128], i32), "Jn": ("sbuf", [128, 128], i32),
+    "metc": ("sbuf", [128, 4], f32), "Er": ("sbuf", [128, 256], f16), "Ouf": ("sbuf", [128, 16], f32), "Ol": ("sbuf", [128, 16], u16),
+    "Y": ("sbuf", [128, 256], bf), "zt": ("sbuf", [128, 256], f16), "R1": ("sbuf", [128, 256], f16), "R2": ("sbuf", [128, 256], bf),
+    "EQW": ("sbuf", [128, 16, 256], bf), "lo": ("sbuf", [128, 256], bf), "LO": ("sbuf", [128, 16], f32),
+    "Ls": ("sbuf", [128, 16], u16), "yo": ("sbuf", [128, 256], f32),
+    "one": ("sbuf", [128, 512], bf), "BD": ("sbuf", [128, 128], bf), "BD1": ("sbuf", [128, 128], bf), "I": ("sbuf", [128, 128], bf),
+    "I25": ("sbuf", [128, 128], bf), "c85": ("sbuf", [128, 128], bf), "c16k": ("sbuf", [128, 128], bf), "I32": ("sbuf", [128, 128], bf), "Ihalf": ("sbuf", [128, 128], bf), "q9": ("sbuf", [128, 128], bf),
+    "I5": ("sbuf", [128, 640], bf), "E": ("sbuf", [128, 2048], bf), "ES": ("sbuf", [128, 2048], bf), "B": ("sbuf", [128, 2048], bf),
+    "Q4": ("sbuf", [128, 2048], bf), "W2": ("sbuf", [128, 128], bf), "W32": ("sbuf", [128, 128], bf), "BM": ("sbuf", [128, 128], bf),
+    "BN": ("sbuf", [128, 128], bf), "S15": ("sbuf", [128, 128], bf), "KC": ("sbuf", [128, 128], bf), "MCS": ("sbuf", [128, 480], bf),
+    "MCV": ("sbuf", [128, 480], bf), "RC": ("sbuf", [128, 128], f16), "RM": ("sbuf", [128, 480], f16), "io": ("sbuf", [128, 16], f32),
+    "OH": ("sbuf", [128, 16], f32), "PW": ("sbuf", [128, 48], f32), "PT": ("sbuf", [128, 48], f32), "DMi": ("sbuf", [128, 16, 16], f32),
+    "DM": ("sbuf", [128, 16, 16], bf), "IO": ("sbuf", [128, 16], f16),
+}
+COLS = {}
+for _b, _d, _ns in (("colf", f32, ("kc", "kx", "w2c", "p32", "p4", "limf", "top", "mets")), ("coli", i32, ("pi", "pk", "meti", "mete"))):
+    SCRATCH[_b] = ("sbuf", [128, len(_ns)], _d)
+    for _i, _n in enumerate(_ns):
+        COLS[_n] = (_b, _i)
+for _t in range(4):
+    SCRATCH["F%d" % _t] = ("sbuf", [128, 256], f16)
+    SCRATCH["Z%d" % _t] = ("sbuf", [128, 256], bf)
+    SCRATCH["Zo%d" % _t] = ("sbuf", [128, 256], bf)
+    for _n, _d in (("UH", f16), ("OP", f16), ("FI", i32), ("FO", f16), ("Fm", f16)):
+        SCRATCH["%s%d" % (_n, _t)] = ("sbuf", [128, 128 >> _t, 2, 1 << _t], _d)
+BANKS = ["pU", "pR", "pS", "pN", "pA", "pB", "p1", "p2"]
+for _n in BANKS:
+    SCRATCH[_n] = ("psum", [128, 512], f32)
+SEMAPHORES = ["sg", "sv", "ss", "st", "loc"] + ["d%d" % i for i in range(5)] + ["o%s%d" % (c, h) for c in "FZ" for h in range(len(GR))] + \
+    ["r%s%d%d" % (c, t, h) for c in "FZ" for t in (1, 2, 3) for h in range(len(GR))]
+
+CYC, TCYC, GATH, WAKE, WIRE = 1.04e-3, 0.52e-3, 1.56, 0.22, 3.0
+
+
+def rank_program(g, core, T, topo):
+    rank = T.rank_of(core)
+    if rank is None:
+        return
+    nrank = len(T.cores)
+    eng = {"g": g, "v": g.vector, "s": g.scalar, "t": g.tensor, "y": g.sync}
+    semof = {"g": "sg", "v": "sv", "s": "ss", "t": "st"}
+    ops = []
+    hist = {}
+
+    def op(q, fn, outs, ins, cost=0.1, sem=None, inc=1):
+        me, deps = len(ops), {}
+        for accs, wr in ((ins, False), (outs, True)):
+            for acc in accs:
+                for w, lo, hi, i in hist.get(acc[1], ()):
+                    own = ops[i][0] == q
+                    if acc[1] in BANKS:
+                        if not own or (acc[2] < hi and lo < acc[3] and (w or wr)):
+                            deps[i] = deps.get(i, False) or not own
+                    elif acc[2] < hi and lo < acc[3] and (w or wr):
+                        deps[i] = deps.get(i, False) or w or not own
+        ops.append([q, fn, cost, deps, sem or semof[q], inc])
+        for accs, wr in ((ins, False), (outs, True)):
+            for acc in accs:
+                mark(acc[1], acc[2], acc[3], wr, me)
+        return me
+
+    def mark(name, lo, hi, wr, me):
+        h = hist.setdefault(name, [])
+        if wr and name not in BANKS:
+            h[:] = [a for a in h if not (lo <= a[1] and a[2] <= hi)]
+        elif wr:
+            h[:] = [a for a in h if not (lo <= a[1] and a[2] <= hi and ops[a[3]][0] == ops[me][0])]
+        h.append((wr, lo, hi, me))
+
+    def v(name, lo=0, hi=None, st=1, r=128):
+        if name in COLS:
+            name, lo = COLS[name]
+            hi = lo + 1
+        hi = SCRATCH[name][1][1] if hi is None else hi
+        ap = T[name][0:r, lo:hi:st] if st > 1 else T[name][0:r, lo:hi]
+        return (ap, name, lo, hi, (hi - lo + st - 1) // st)
+
+    def v4(base, t, a, b, which=None):
+        name, w = "%s%d" % (base, t), 2 << t
+        ap = T[name][:, a // w:b // w, :, :] if which is None else T[name][:, a // w:b // w, which, :]
+        return (ap, name, a, b, b - a if which is None else (b - a) // 2)
+
+    def vcost(o, *ins):
+        two = all(x[1] not in BANKS and SCRATCH[x[1]][2] in (bf, f16, u16) for x in (o,) + ins[:1])
+        if len(ins) == 2:
+            return max(64, o[4] * (1 if ins[0][1] in BANKS or ins[1][1] in BANKS else 2)) * CYC
+        return max(64, o[4] * (0.5 if two else 1)) * CYC
+
+    def tt(o, a, b, f):
+        op("v", lambda: g.vector.tensor_tensor(o[0], a[0], b[0], f), [o], [a, b], vcost(o, a, b))
+
+    def ts(o, a, s1, f1, s2=None, f2=None):
+        ins = [a] + [s for s in (s1, s2) if isinstance(s, tuple)]
+        x1 = s1[0] if isinstance(s1, tuple) else s1
+        x2 = s2[0] if isinstance(s2, tuple) else s2
+        if f2 is None:
+            op("v", lambda: g.vector.tensor_scalar(o[0], a[0], x1, None, f1), [o], ins, vcost(o, a))
+        else:
+            op("v", lambda: g.vector.tensor_scalar(o[0], a[0], x1, x2, f1, f2), [o], ins, vcost(o, a))
+
+    def cp(o, a):
+        op("v", lambda: g.vector.tensor_copy(o[0], a[0]), [o], [a], vcost(o, a))
+
+    def fill(o, c):
+        op("v", lambda: g.vector.memset(o[0], c), [o], [])
+
+    def red(o, a):
+        op("v", lambda: g.vector.tensor_reduce(o[0], a[0], AxisListType.X, Op.add), [o], [a])
+
+    def mm(o, l, r, start, stop):
+        me = op("t", lambda: g.tensor.matmul(o[0], l[0], r[0], start, stop), [o], [l, r], max(64, r[4]) * TCYC)
+        if start and o[1] in closed:
+            ops[me][3].setdefault(closed[o[1]], False)
+        if stop:
+            closed[o[1]] = me
+
+    def act(o, a, func, **kw):
+        op("s", lambda: g.scalar.activation(o[0], a[0], func, **kw), [o], [a], max(64, o[4]) * CYC)
+
+    def asel(o, a, pat, cop, base, cm):
+        op("g", lambda: g.affine_select(o[0], a[0], pat, cop, 0.0, base, cm), [o], [a], 0.17 + 2 * o[4] * CYC)
+
+    def iota(o, pat, base, cm, small=True):
+        if small:
+            op("g", lambda: g.iota(o[0], pat, base, cm, allow_small_or_imprecise_dtypes=True), [o], [])
+        else:
+            op("g", lambda: g.iota(o[0], pat, base, cm), [o], [])
+
+    def mat(name, k):
+        return v(name, 128 * k, 128 * k + 128)
+
+    lists, closed = {}, {}
+    X = (T.X[:, 0:2048], "X", 0, 2048)
+
+    op("y", lambda: g.sync.dma_start(T.Z0[:], T.vein[:]), [v("Z0")], [], 2.0, "d0", 16)
+    op("y", lambda: g.sync.dma_start(T.win[:], T.w[:]), [v("win")], [], 2.0, "d1", 16)
+    op("y", lambda: g.sync.dma_start(T.fin[:], T.front[:]), [v("fin")], [], 2.0, "d2", 16)
+    op("y", lambda: g.sync.dma_start(T.X[:, 0:2048], T.rock[:]), [X], [], 2.0, "d3", 16)
+    op("y", lambda: g.sync.dma_start(T.lin[:], T.lim[:]), [v("lin")], [], 2.0, "d4", 16)
+
+    fill(v("one"), 1.0)
+    iota(v("pi"), [[0, 1]], 0, 1, False)
+    asel(v("BD1"), v("one", 0, 128), [[-16, 8], [0, 16]], Op.is_ge, 0, 1)
+    asel(v("BD"), v("BD1"), [[16, 8], [0, 16]], Op.is_ge, 15, -1)
+    asel(v("I"), v("one", 0, 128), [[-1, 128]], Op.is_equal, 0, 1)
+    iota(v("RC", r=2), [[0, 8], [37, 16]], 0, 0)
+    for m in range(5):
+        fill(v("RM", 96 * m, 96 * m + 96, r=2), float(32 << m))
+        fill(v("RM", 96 * m, 96 * m + 96, r=1), float(m * (32 << m)))
+    fill(v("RC", r=1), 613.0)
+    ts(v("pk"), v("pi"), 15, Op.bitwise_and)
+    cp(v("kc"), v("pk"))
+    cp(v("F0"), v("fin"))
+    ts(v("w2c"), v("win"), 2.0, Op.mult)
+    ts(v("W2"), v("BD"), v("w2c"), Op.mult)
+    for m in range(5):
+        act(mat("I5", m), v("I"), Act.Copy, scale=float(32 << m))
+
+    def prep(t, ch):
+        kind, a, b = ch
+        n = b - a
+        F, Z = v("F%d" % t, a, b), v("Z%d" % t, a, b)
+        mm(v("pU", 0, n), v("W2"), Z, True, False)
+        mm(v("pU", 0, n), v("one", 0, 128, r=1), v("one", 0, n, r=1), False, True)
+        mm(v("pU", n, 2 * n), v("BD"), Z, True, True)
+        mm(v("pU", 2 * n, 3 * n), v("I"), F, True, True)
+        for m in range(5):
+            o = v("pR", m * n, m * n + n)
+            mm(o, v("RC", r=2), v("RM", 96 * m, 96 * m + n, r=2), True, False)
+            mm(o, mat("I5", m), F, False, True)
+        cp(v("usi", 2 * a, 2 * b), v("pU", 0, 2 * n))
+        ts(v("u2", a, b), v("usi", 2 * a, 2 * a + n), 4095, Op.bitwise_and)
+        tt(v("P", a, b), v("pU", 2 * n, 3 * n), v("u2", a, b), Op.mult)
+        for m in range(5):
+            cm = (5 * a + m * n, 5 * a + m * n + n)
+            tt(v("Q", *cm), v("pR", m * n, m * n + n), v("P", a, b), Op.add)
+            ts(v("C", *cm), v("Q", *cm), 5 + m, Op.logical_shift_right, 2047, Op.bitwise_and)
+            if kind == "S":
+                cp(v("off6", 6 * a + m, 6 * b - 5 + m, 6), v("C", *cm))
+        if kind == "V":
+            cp(v("offV", 0, 5 * n), v("C", 5 * a, 5 * b))
+        cp(v("c16", 5 * a, 5 * b), v("C", 5 * a, 5 * b))
+        ts(v("si", a, b), v("usi", 2 * a + n, 2 * b), 15, Op.bitwise_and)
+        ts(v4("OP", t, a, b), v("si", a, b), v("kc"), Op.is_equal)
+        ts(v4("UH", t, a, b), v("u2", a, b), 0.5, Op.mult, -0.5, Op.add)
+        ts(v("zq", a, b), Z, 0.25, Op.mult, 1279.625, Op.add)
+        ts(v("Kn", a, b), F, float(KN), Op.add)
+
+    def spread(t, ch):
+        kind, a, b = ch
+        for k in range(16):
+            asel(v("Zx", k, 16 * (b - a) - 15 + k, 16), v("Z%d" % t, a, b), [[0, b - a]], Op.is_gt, 1, 0)
+
+    def gather_s(t, ch):
+        for i in range(ch[1], ch[2]):
+            def one(o, f, z):
+                op("s", lambda: g.scalar.activation(o[0], X[0].indirect(f[0]), Act.Abs, bias=z[0], scale=-1.0), [o], [X, f, z], 0.065 + 80 * GATH * CYC)
+            one(v("A", 80 * i, 80 * i + 80), v("off6", 6 * i, 6 * i + 5), v("Z%d" % t, i, i + 1))
+
+    def gather_v(t, ch):
+        n = ch[2] - ch[1]
+        for m in range(5):
+            def one(o, f, z):
+                op("v", lambda: g.vector.tensor_tensor(o[0], X[0].indirect(f[0]), z[0], Op.subtract), [o], [X, f, z], 0.05 + o[4] * GATH * CYC)
+            one(v("D", 16 * n * m, 16 * n * (m + 1)), v("offV", m * n, m * n + n), v("Zx", 0, 16 * n))
+
+    def abs_v(ch):
+        n, a = ch[2] - ch[1], 80 * ch[1]
+        for m in range(5):
+            act(v("A", a + 16 * n * m, a + 16 * n * (m + 1)), v("D", 16 * n * m, 16 * n * (m + 1)), Act.Abs)
+
+    def view5(name, kind, n, m, off=0):
+        if kind == "S":
+            return v(name, off + m, off + 5 * n - 4 + m, 5)
+        return v(name, off + m * n, off + m * n + n)
+
+    def score(ch):
+        kind, a, b = ch
+        n = b - a
+        step = SUB if kind == "S" else n
+        mm(v("pS", 0, 5 * n), v("KC", r=2), v("MCS" if kind == "S" else "MCV", 0, 5 * n, r=2), True, False)
+        for m in range(5):
+            mm(view5("pS", kind, n, m), v("I"), v("c16", 5 * a + m * n, 5 * a + m * n + n), False, False)
+        for p in range(a, b, step):
+            w, off = step, 5 * (p - a)
+            o, on = v("pS", off, off + 5 * w), v("pN", off, off + 5 * w)
+            for k in range(16):
+                mm(o, mat("ES", k), v("A", 80 * p + k, 80 * (p + w) - 15 + k, 16), False, k == 15 and p + w == b)
+            pieces = 1 if kind == "S" else 5
+            for c in range(pieces):
+                x = (80 * p + c * 80 * w // pieces, 80 * p + (c + 1) * 80 * w // pieces)
+                ts(v("NR", *x), v("A", *x), v("top"), Op.is_le)
+            for k in range(16):
+                mm(on, mat("E", k), v("NR", 80 * p + k, 80 * (p + w) - 15 + k, 16), k == 0, k == 15)
+
+    def choose(t, ch):
+        kind, a, b = ch
+        n = b - a
+        KB = v("KB", a, b)
+        K1, K2 = v("K1", a, b), v("K2", a, b)
+        tt(K1, view5("pS", kind, n, 0), v("Kn", a, b), Op.min)
+        tt(K2, view5("pS", kind, n, 1), v("Kn", a, b), Op.min)
+        tt(K1, view5("pS", kind, n, 2), K1, Op.min)
+        tt(K2, view5("pS", kind, n, 3), K2, Op.min)
+        tt(K1, view5("pS", kind, n, 4), K1, Op.min)
+        tt(KB, K1, K2, Op.min)
+        for m in range(5):
+            tt(view5("EQm", kind, n, m, 5 * a), view5("pS", kind, n, m), KB, Op.is_equal)
+        tt(v("TT", 5 * a, 5 * b), v("EQm", 5 * a, 5 * b), v("pN", 0, 5 * n), Op.mult)
+        cnt = v("pN", 416, 416 + n)
+        for m in range(5):
+            mm(cnt, v("I25"), view5("TT", kind, n, m, 5 * a), m == 0, False)
+        mm(cnt, v("c85", r=1), v("one", 0, n, r=1), False, True)
+        tt(v("KF", a, b), cnt, KB, Op.max)
+        tt(v("KI", a, b), v("KF", a, b), v("Kn", a, b), Op.min)
+        ts(v4("FI", t, a, b), v("KI", a, b), 2047, Op.bitwise_and)
+
+    def meeting(t, gi):
+        a, b = GR[gi]
+        h = (b - a) // 2
+        q0, q1 = a // 2, b // 2
+        per = max(x for x in (1, 2, 4, 8, 16) if x * h <= 512)
+        rounds = [(r, "pA" if (r // per) % 2 == 0 else "pB") for r in range(0, 16, per)]
+        S, J = v("SJ", a, a + h), v("SJ", a + h, b)
+
+        def pr(name):
+            for buf, names in (("ph", ("nv", "nvS", "t1", "t2", "ohS", "ohJ")), ("pb", ("mj", "w0", "wM", "ms"))):
+                if name in names:
+                    return v(buf, 128 * names.index(name) + q0, 128 * names.index(name) + q1)
+            return v(name, q0, q1)
+
+        def big(name, k, c=1):
+            return v(name, 8 * a + k * h, 8 * a + (k + c) * h)
+        G, LM, XP, SN = (v("p1", 112 * i, 112 * i + h) for i in range(4))
+        HF = v("pN", 416, 416 + h)
+        ML, MT, JN = (v("p2", 112 * i, 112 * i + h) for i in range(3))
+        ts(v("Hh", a, a + h), v4("FI", t, a, b, 0), 0.125, Op.mult, 1279.5625, Op.add)
+        ts(v("Hh", a + h, b), v4("FI", t, a, b, 1), 0.125, Op.mult, 1279.5625, Op.add)
+        cp(S, v4("FI", t, a, b, 0))
+        cp(J, v4("FI", t, a, b, 1))
+        for r, bank in rounds:
+            for l in range(per):
+                o = v(bank, l * h, l * h + h)
+                mm(o, mat("B", r + l), v("Hh", a, a + h), True, True)
+            for l in range(per):
+                tt(big("EQ2", r + l), v(bank, l * h, l * h + h), v("Hh", a + h, b), Op.is_equal)
+        for l in range(16):
+            mm(HF, v("LT"), big("EQ2", l), l == 0, l == 15)
+        for l in range(16):
+            mm(ML, mat("Q4", l), big("EQ2", l), l == 0, l == 15)
+        for l in range(16):
+            mm(G, v("W32"), big("EQ2", l), l == 0, l == 15)
+        cp(pr("ohS"), v4("OP", t, a, b, 0))
+        cp(pr("ohJ"), v4("OP", t, a, b, 1))
+        tt(pr("JS"), J, S, Op.mult)
+        jq = v("pU", 320, 320 + h)
+        mm(jq, v("I32"), J, True, False)
+        mm(jq, v("I32"), v4("UH", t, a, b, 1), False, True)
+        tt(pr("JQ"), jq, pr("JS"), Op.add)
+        ts(pr("Jn"), pr("JQ"), 5, Op.logical_shift_right, 2047, Op.bitwise_and)
+        tt(pr("t1"), pr("Jn"), J, Op.subtract)
+        ts(pr("w0"), HF, 0.0, Op.is_gt)
+        tt(pr("wM"), ML, pr("w0"), Op.mult)
+        ts(pr("mj"), G, v("p32"), Op.is_ge)
+        mm(LM, v("BD"), pr("wM"), True, True)
+        ts(pr("ms"), LM, v("p4"), Op.is_ge)
+        mm(XP, v("BM"), pr("ms"), True, False)
+        mm(XP, v("BN"), pr("mj"), False, True)
+        for r, bank in rounds:
+            for k in range(per):
+                mm(v(bank, k * h, k * h + h), mat("B", r + k), J, True, True)
+            for k in range(per):
+                ts(big("MK", r + k), XP, v("KX", r + k, r + k + 1), Op.is_equal)
+            tt(big("PJ", r, per), v(bank, 0, per * h), big("MK", r, per), Op.mult)
+        ts(pr("nv"), XP, v("KX", 15, 16), Op.is_gt)
+        tt(pr("nvS"), pr("nv"), S, Op.mult)
+        mm(SN, v("I"), pr("nvS"), True, False)
+        for k in range(16):
+            mm(SN, v("I"), big("PJ", k), False, k == 15)
+        tt(pr("t2"), pr("t1"), pr("mj"), Op.mult)
+        mm(JN, v("I"), J, True, False)
+        mm(JN, v("I"), pr("t2"), False, True)
+        mm(MT, v("S15"), pr("mj"), True, True)
+        tt(v4("Fm", t, a, b, 1), JN, pr("ohJ"), Op.mult)
+        tt(v4("Fm", t, a, b, 0), SN, pr("ohS"), Op.mult)
+        cp(v4("FO", t, a, b, 1), JN)
+        cp(v4("FO", t, a, b, 0), SN)
+        red(v("metc", gi, gi + 1), MT)
+
+    def send(t, gi, what, src):
+        dst = T.cores[(rank + NEXT) % nrank]
+        rid, pid = topo.addr(dst, core)
+        es = topo.engines(core, dst)[:8]
+        a, b = GR[gi]
+        sem = "r%s%d%d" % (what, t + 1, gi)
+
+        def call():
+            g.remote_dma(out_ap=T["%s%d" % (what, t + 1)][:, a:b], in_ap=src[0], remote_sem=T.sem[sem], local_sem=T.sem["loc"],
+                         pid=pid, routing_id=rid, dma_engine_mask=sum(1 << e for e in es))
+        me = op("g", call, [], [src], 0.4, "loc", len(es))
+        ops.append(["r", None, WIRE, {me: False}, sem, len(topo.engines(T.cores[(rank - NEXT) % nrank], core)[:8])])
+        mark("%s%d" % (what, t + 1), a, b, True, len(ops) - 1)
+
+    def mining(t, gi):
+        a, b = GR[gi]
+        n, c0, c1 = b - a, a // 16, b // 16
+        FO, Z, o, f = v4("FO", t, a, b), v("Z%d" % t, a, b), v("Y", a, b), v("Ol", c0, c1)
+        OL, ER, VN, CN, LL = v("p2", 448, 448 + n // 16), v("pA", 0, n), v("pB", 0, n), v("pA", 256, 256 + n), v("p2", 480, 480 + n // 16)
+        if t < 3:
+            send(t, gi, "F", FO)
+        else:
+            cp(v("yo", a, b), FO)
+            op("y", lambda: g.sync.dma_start(T.yf[:, a:b], T.yo[:, a:b]), [], [v("yo", a, b)], 2.0, "oF%d" % gi, 16)
+        w = 2 << t
+        for q in range(16):
+            col = (T["Fm%d" % t][:, a // w + q // w:b // w:16 // w, q % w // (w // 2), q % (w // 2)], "Fm%d" % t, a, b, n // 16)
+            mm(OL, mat("E", q), col, q == 0, q == 15)
+        mm(ER, v("BD"), v4("Fm", t, a, b), True, True)
+        cp(f, OL)
+        cp(v("Ouf", c0, c1), OL)
+        cp(v("Er", a, b), ER)
+        op("s", lambda: g.scalar.activation(o[0], X[0].indirect(f[0]), Act.Copy), [o], [X, f], 0.065 + n * GATH * CYC)
+        if gi == len(GR) - 1:
+            for x in range(gi):
+                scatter(x)
+        mm(VN, v("Ihalf"), Z, True, False)
+        mm(VN, v("q9"), v("one", 0, n), False, False)
+        mm(VN, v("Ihalf"), o, False, True)
+        ts(v("zt", a, b), VN, 1280.0, Op.add)
+        ts(v("Zo%d" % t, a, b), v("zt", a, b), -1280.0, Op.add)
+        if t < 3:
+            send(t, gi, "Z", v("Zo%d" % t, a, b))
+        else:
+            op("y", lambda: g.sync.dma_start(T.yz[:, a:b], T["Zo3"][:, a:b]), [], [v("Zo3", a, b)], 2.0, "oZ%d" % gi, 16)
+
+        def later(c):
+            lo = max(16 * c, a)
+            w = (T.EQW[:, c, lo - 16 * c:b - 16 * c], "EQW", 256 * c + lo - 16 * c, 256 * c + b - 16 * c, b - lo)
+            return lo, w
+        for c in range(c1):
+            lo, w = later(c)
+            ts(w, v("Er", lo, b), v("Ouf", c, c + 1), Op.is_equal)
+        dg = (T.EQW[:, c0:c1, 0:16], "EQW", 256 * c0, 256 * c1, n)
+        op("v", lambda: g.vector.tensor_tensor(dg[0], dg[0], T.DM[:, c0:c1, :], Op.mult), [dg], [dg, ("", "DM", 0, 256)], 2 * n * CYC)
+        for c in range(c1):
+            lo, w = later(c)
+            mm(v("pA", 256 + lo - a, 256 + n), v("BD"), w, c == 0, c == c1 - 1)
+        act(v("lo", a, b), CN, Act.Sign)
+        mm(LL, v("I"), v("IO", c0, c1), True, False)
+        mm(LL, v("c16k", r=1), v("one", 0, n // 16, r=1), False, False)
+        for q in range(16):
+            mm(LL, mat("ES", q), v("lo", a + q, b - 15 + q, 16), False, q == 15)
+        tt(v("R1", a, b), o, v("zq", a, b), Op.subtract)
+        ts(v("R2", a, b), v("R1", a, b), 1280.0, Op.add, 0.0, Op.max)
+        tt(v("LO", c0, c1), LL, v("Ouf", c0, c1), Op.max)
+        cp(v("Ls", c0, c1), v("LO", c0, c1))
+        lists[gi] = (v("Ls", c0, c1), v("R2", a, b))
+
+    def scatter(gi):
+        XW, ls, r2 = (T.X[:, 0:2560], "X", 0, 2560), lists[gi][0], lists[gi][1]
+        op("v", lambda: g.vector.tensor_copy(XW[0].indirect(ls[0]), r2[0]), [XW], [ls, r2], 0.05 + r2[4] * 3.8 * CYC)
+
+    def limits(t):
+        if t == 0:
+            cp(v("limf"), v("lin"))
+            cp(v("top"), v("limf"))
+        else:
+            red(v("mets"), v("metc", 0, len(GR)))
+            cp(v("meti"), v("mets"))
+            ts(v("mete"), v("meti"), 3, Op.bitwise_and)
+            tt(v("top"), v("limf"), v("mete"), Op.add)
+
+    def key_constants():
+        for k in range(16):
+            asel(mat("E", k), v("BD"), [[0, 8], [1, 16]], Op.is_equal, -k, 0)
+            act(mat("ES", k), mat("E", k), Act.Copy, scale=10240.0)
+        iota(v("KC", r=2), [[0, 128]], -4096, 6144)
+        iota(v("MCS", r=2), [[0, 96], [1, 5]], 0, 0)
+        iota(v("MCV", 0, 5 * NV, r=2), [[1, 5], [0, NV]], 0, 0)
+        fill(v("MCS", r=1), 4096.0)
+        fill(v("MCV", 0, 5 * NV, r=1), 4096.0)
+
+    def last_constants():
+        iota(v("io"), [[1, 16]], 0, 0)
+        op("g", lambda: g.iota(T.DMi[:], [[0, 16], [1, 16]], 0, 0, allow_small_or_imprecise_dtypes=True), [("", "DMi", 0, 256)], [])
+        act(v("I25"), v("I"), Act.Copy, scale=-float(1 << 25))
+        fill(v("c85"), 8.5 * (1 << 25))
+        fill(v("c16k"), -163840.0)
+        ts(v("I32"), v("I"), 32.0, Op.mult)
+        ts(v("Ihalf"), v("I"), 0.5, Op.mult)
+        fill(v("q9"), -(2.0 ** -9))
+        ts(v("OH"), v("io"), v("kc"), Op.is_equal)
+        for l in range(16):
+            ts(mat("B", l), v("BD"), v("OH", l, l + 1), Op.mult)
+            act(mat("Q4", l), v("I"), Act.Copy, scale=float(4 ** (15 - l)))
+        for r in range(16):
+            fill(v("PW", r, r + 1), 2.0 ** (5 * (15 - r)))
+            fill(v("PW", 16 + r, 17 + r), 2.0 ** (2 * (16 - r)))
+        for j, name in ((0, "p32"), (16, "p4")):
+            tt(v("PT", j, j + 16), v("PW", j, j + 16), v("OH"), Op.mult)
+            red(v(name), v("PT", j, j + 16))
+        asel(v("LT"), v("BD"), [[1, 128]], Op.is_gt, 0, -1)
+        ts(v("LT"), v("LT"), -32.0, Op.mult)
+        tt(v("LT"), v("LT"), v("I"), Op.add)
+        ts(v("W32"), v("BD"), v("p32"), Op.mult)
+        ts(v("BN"), v("BD"), -1.0, Op.mult)
+        ts(v("BD1"), v("I"), -64.0, Op.mult)
+        tt(v("BM"), v("BD1"), v("BD"), Op.add)
+        ts(v("S15"), v("one", 0, 128), v("OH", 15, 16), Op.mult)
+        ts(v("kx"), v("kc"), 65.0, Op.add)
+        ts(v("KX"), v("io"), v("kx"), Op.subtract)
+        op("v", lambda: g.vector.tensor_scalar(T.DM[:], T.DMi[:], v("kc")[0], None, Op.is_gt), [("", "DM", 0, 256)], [("", "DMi", 0, 256), v("kc")], 256 * CYC)
+        ts(v("PT", 16, 32), v("io"), 32.0, Op.mult, 2048.0, Op.add)
+        ts(v("PT", 32, 33), v("kc"), 2.0, Op.mult)
+        ts(v("IO"), v("PT", 16, 32), v("PT", 32, 33), Op.add)
+
+    vch = [ch for ch in CH if ch[0] == "V"][0]
+    for t in range(4):
+        if t == 0:
+            for ch in CH:
+                prep(0, ch)
+            key_constants()
+            last_constants()
+        else:
+            for ch in CH:
+                if ch[1] >= GR[-1][0]:
+                    prep(t, ch)
+        spread(t, vch)
+        for ch in CH:
+            if ch[0] == "S":
+                gather_s(t, ch)
+        gather_v(t, vch)
+        limits(t)
+        abs_v(vch)
+        for gi, (a, b) in enumerate(GR):
+            for ch in CH:
+                if a <= ch[1] < b:
+                    score(ch)
+                    choose(t, ch)
+            meeting(t, gi)
+            mining(t, gi)
+            if gi == len(GR) - 1:
+                scatter(gi)
+            elif t < 3:
+                for ch in CH:
+                    if a <= ch[1] < b:
+                        prep(t + 1, ch)
+    op("y", lambda: g.sync.dma_start(T.yx[:], T.X[:, 0:2048]), [], [X], 2.0, "d3", 16)
+
+    succ = [[] for _ in ops]
+    left = [0] * len(ops)
+    for i, o in enumerate(ops):
+        for j in o[3]:
+            succ[j].append(i)
+            left[i] += 1
+    way = [0.0] * len(ops)
+    for i in range(len(ops) - 1, -1, -1):
+        best = 0.0
+        for j in succ[i]:
+            best = max(best, way[j] + (WAKE if ops[j][3][i] else 0.0))
+        way[i] = best + ops[i][2]
+    free, ready = {}, {}
+    early = [0.0] * len(ops)
+    for i, o in enumerate(ops):
+        free[o[0]] = 0.0
+        ready.setdefault(o[0], [])
+        if not left[i]:
+            ready[o[0]].append(i)
+    order = []
+    while len(order) < len(ops):
+        pick = None
+        for q, r in ready.items():
+            if r:
+                start = max(free[q], min(early[i] for i in r))
+                if pick is None or start < pick[0]:
+                    pick = (start, q)
+        start, q = pick
+        i = max((i for i in ready[q] if early[i] <= start + 1e-9), key=lambda i: way[i])
+        ready[q].remove(i)
+        end = start + ops[i][2]
+        if q != "r":
+            free[q] = end if q != "y" else start + 0.1
+        order.append(i)
+        for j in succ[i]:
+            left[j] -= 1
+            early[j] = max(early[j], end + WAKE if ops[j][3][i] else (end if ops[j][0] == "r" else start))
+            if not left[j]:
+                ready[ops[j][0]].append(j)
+
+    count, know, value, clocks = {}, {q: {} for q in free}, {}, {}
+    for i in order:
+        q, fn, cost, deps, sem, inc = ops[i]
+        k = know[q]
+        best = {}
+        for j, wait in deps.items():
+            if wait and (ops[j][4] not in best or value[best[ops[j][4]]] < value[j]):
+                best[ops[j][4]] = j
+        for j in sorted(best.values(), key=lambda j: -len(clocks[j])):
+            if k.get(ops[j][4], 0) < value[j]:
+                eng[q].wait_ge(T.sem[ops[j][4]], value[j])
+                for s, x in clocks[j].items():
+                    if k.get(s, 0) < x:
+                        k[s] = x
+        count[sem] = value[i] = count.get(sem, 0) + inc
+        clocks[i] = {sem: value[i]}
+        if q != "r":
+            r = fn()
+            if r is not None:
+                r.then_inc(T.sem[sem], inc)
+            clocks[i] = dict(k)
+            clocks[i][sem] = value[i]
+    for s in SEMAPHORES:
+        if count.get(s):
+            g.wait_ge(T.sem[s], count[s])

@@ -1,55 +1,78 @@
 from concourse.mybir import dt, AluOpType as Op, AxisListType, ActivationFunctionType as Act
 
 NEXT = 1
-CH = [("S", 0, 64), ("V", 64, 128), ("S", 128, 192), ("S", 192, 256)]
-GR = [(0, 128), (128, 256)]
-NV = [b - a for k, a, b in CH if k == "V"][0]
+CH = [("S", 0, 64, "v"), ("S", 64, 96, "v"), ("V", 96, 128, "s")]
+GR = [(0, 128)]
+VP, NP = 16, 16
 SUB = 16
-KN = 2956 * 10240 - (1 << 24)
+VA, VB = [(a, b) for k, a, b, e in CH if k == "V"][0]
+NV = VB - VA
+KN = 13 << 20
+BIG = 4096.0
+MAGIC = 1.5 * (1 << 23)
+REST = 2048.0 * 105
 
 f32, bf, f16, i32, u16 = "float32", "bfloat16", "float16", "int32", "uint16"
-SCRATCH = {
-    "X": ("sbuf", [128, 2560], bf), "fin": ("sbuf", [128, 256], i32), "win": ("sbuf", [128, 1], i32), "lin": ("sbuf", [128, 1], i32),
-    "A": ("sbuf", [128, 20480], bf), "D": ("sbuf", [128, 80 * NV], bf), "NR": ("sbuf", [128, 20480], bf), "Zx": ("sbuf", [128, 16 * NV], bf),
-    "off6": ("sbuf", [128, 1536], u16), "offV": ("sbuf", [128, 5 * NV], u16), "c16": ("sbuf", [128, 1280], f16),
-    "usi": ("sbuf", [128, 512], i32), "u2": ("sbuf", [128, 256], i32), "si": ("sbuf", [128, 256], i32),
-    "zq": ("sbuf", [128, 256], f16), "P": ("sbuf", [128, 256], f32), "Q": ("sbuf", [128, 1280], i32), "C": ("sbuf", [128, 1280], i32),
-    "Kn": ("sbuf", [128, 256], f32), "KB": ("sbuf", [128, 256], f32), "EQm": ("sbuf", [128, 1280], bf), "TT": ("sbuf", [128, 1280], bf),
-    "KF": ("sbuf", [128, 256], f32), "K1": ("sbuf", [128, 256], f32), "K2": ("sbuf", [128, 256], f32), "KI": ("sbuf", [128, 256], i32),
-    "SJ": ("sbuf", [128, 256], f16), "Hh": ("sbuf", [128, 256], f16), "EQ2": ("sbuf", [128, 2048], bf), "MK": ("sbuf", [128, 2048], f16),
-    "PJ": ("sbuf", [128, 2048], f16), "LT": ("sbuf", [128, 128], bf), "KX": ("sbuf", [128, 16], f32), "ph": ("sbuf", [128, 768], f16),
-    "pb": ("sbuf", [128, 512], bf), "JS": ("sbuf", [128, 128], f32), "JQ": ("sbuf", [128, 128], i32), "Jn": ("sbuf", [128, 128], i32),
-    "metc": ("sbuf", [128, 4], f32), "Er": ("sbuf", [128, 256], f16), "Ouf": ("sbuf", [128, 16], f32), "Ol": ("sbuf", [128, 16], u16),
-    "Y": ("sbuf", [128, 256], bf), "zt": ("sbuf", [128, 256], f16), "R1": ("sbuf", [128, 256], f16), "R2": ("sbuf", [128, 256], bf),
-    "EQW": ("sbuf", [128, 16, 256], bf), "lo": ("sbuf", [128, 256], bf), "LO": ("sbuf", [128, 16], f32),
-    "Ls": ("sbuf", [128, 16], u16), "yo": ("sbuf", [128, 256], f32),
-    "one": ("sbuf", [128, 512], bf), "BD": ("sbuf", [128, 128], bf), "BD1": ("sbuf", [128, 128], bf), "I": ("sbuf", [128, 128], bf),
-    "I25": ("sbuf", [128, 128], bf), "c85": ("sbuf", [128, 128], bf), "c16k": ("sbuf", [128, 128], bf), "I32": ("sbuf", [128, 128], bf), "Ihalf": ("sbuf", [128, 128], bf), "q9": ("sbuf", [128, 128], bf),
-    "I5": ("sbuf", [128, 640], bf), "E": ("sbuf", [128, 2048], bf), "ES": ("sbuf", [128, 2048], bf), "B": ("sbuf", [128, 2048], bf),
-    "Q4": ("sbuf", [128, 2048], bf), "W2": ("sbuf", [128, 128], bf), "W32": ("sbuf", [128, 128], bf), "BM": ("sbuf", [128, 128], bf),
-    "BN": ("sbuf", [128, 128], bf), "S15": ("sbuf", [128, 128], bf), "KC": ("sbuf", [128, 128], bf), "MCS": ("sbuf", [128, 480], bf),
-    "MCV": ("sbuf", [128, 480], bf), "RC": ("sbuf", [128, 128], f16), "RM": ("sbuf", [128, 480], f16), "io": ("sbuf", [128, 16], f32),
-    "OH": ("sbuf", [128, 16], f32), "PW": ("sbuf", [128, 48], f32), "PT": ("sbuf", [128, 48], f32), "DMi": ("sbuf", [128, 16, 16], f32),
-    "DM": ("sbuf", [128, 16, 16], bf), "IO": ("sbuf", [128, 16], f16),
+SCRATCH = {}
+PER = {
+    "X": ([128, 2560], bf), "A": ([128, 80 * 128], bf), "D": ([128, 80 * NV], bf), "RL": ([128, 80 * NV], bf), "Zx": ([128, 16 * NV], bf),
+    "off6": ([128, 768], u16), "offV": ([128, 5 * NV], u16), "c6": ([128, 768], f16), "cV": ([128, 5 * NV], f16),
+    "P": ([128, 128], f32), "Q": ([128, 640], i32), "C": ([128, 5, 128], i32), "KS": ([128, 640], f32), "EQm": ([128, 512], bf),
+    "NR": ([128, 2048], bf), "NA": ([128, 16 * NV], bf), "EQ2": ([128, 1024], bf), "EQW": ([128, 8, 256], bf),
+    "W2": ([128, 128], bf), "W32": ([128, 128], bf),
+}
+PARTS = {
+    "h16": (f16, [("Hu", 128), ("zq", 128), ("SJ", 128), ("Hh", 128), ("T1", 256), ("T2", 320), ("L5", 320), ("t1", 64), ("Er", 256)]),
+    "b16": (bf, [("mj", 64), ("wM", 64), ("ms", 64), ("oha", 64), ("ohb", 64), ("Y", 128), ("lo", 256), ("R2", 256)]),
+    "w32": (f32, [("KF", 128), ("JS", 64), ("Ouf", 16), ("OI", 16), ("LO", 16), ("yo", 128), ("w2c", 4), ("limf", 4), ("top", 4), ("toph", 4)]),
+    "n32": (i32, [("fin", 128), ("SJi", 128), ("JQ", 64), ("Jn", 64), ("win", 4), ("lin", 4)]),
+    "u16": (u16, [("pos", 128), ("Ol", 16), ("Ls", 16)]),
 }
 COLS = {}
-for _b, _d, _ns in (("colf", f32, ("kc", "kx", "w2c", "p32", "p4", "limf", "top", "mets")), ("coli", i32, ("pi", "pk", "meti", "mete"))):
-    SCRATCH[_b] = ("sbuf", [128, len(_ns)], _d)
-    for _i, _n in enumerate(_ns):
-        COLS[_n] = (_b, _i)
-for _t in range(4):
-    SCRATCH["F%d" % _t] = ("sbuf", [128, 256], f16)
-    SCRATCH["Z%d" % _t] = ("sbuf", [128, 256], bf)
-    SCRATCH["Zo%d" % _t] = ("sbuf", [128, 256], bf)
-    for _n, _d in (("UH", f16), ("OP", f16), ("FI", i32), ("FO", f16), ("Fm", f16)):
-        SCRATCH["%s%d" % (_n, _t)] = ("sbuf", [128, 128 >> _t, 2, 1 << _t], _d)
-BANKS = ["pU", "pR", "pS", "pN", "pA", "pB", "p1", "p2"]
+for _h in range(2):
+    for _n, (_s, _d) in PER.items():
+        SCRATCH["%s%d" % (_n, _h)] = ("sbuf", _s, _d)
+    for _b, (_d, _ts) in PARTS.items():
+        _c = 0
+        for _n, _w in _ts:
+            COLS["%s%d" % (_n, _h)] = ("%s%d" % (_b, _h), _c, _w)
+            _c += _w
+        SCRATCH["%s%d" % (_b, _h)] = ("sbuf", [128, _c], _d)
+    for _t in range(4):
+        SCRATCH["F%d%d" % (_h, _t)] = ("sbuf", [128, 128], f16)
+        for _n, _d in (("Z", bf), ("KI", i32), ("FO", f16), ("Hs", f16), ("Fm", f16)):
+            SCRATCH["%s%d%d" % (_n, _h, _t)] = ("sbuf", [128, 64 >> _t, 2, 1 << _t], _d)
+    SCRATCH["Zo%d" % _h] = ("sbuf", [128, 4 * 128], bf)
+MATS = ["BD", "I", "In", "BDt", "Ih", "I4096", "I32k", "BDn", "G32", "SHB", "BN", "S15", "NOK", "NOKn", "IB", "IBn", "BD0", "BD1", "I0", "I1", "BD2", "W4D"] + \
+    ["I5_%d" % m for m in range(5)] + ["IS%d" % m for m in range(1, 5)] + ["IV%d" % m for m in range(1, 5)] + \
+    ["B%d" % l for l in range(16)] + ["Q4_%d" % l for l in range(16)] + ["Rot%d" % d for d in (1, 2, 3, 4, 8, 12)] + \
+    ["PA%d" % a for a in range(4)] + ["PB%d" % a for a in range(4)]
+SCRATCH["mats"] = ("sbuf", [128, 128 * len(MATS)], bf)
+for _i, _n in enumerate(MATS):
+    COLS[_n] = ("mats", 128 * _i, 128)
+CONST = {
+    "cb": (bf, [("one", 256), ("E", 144), ("ES", 144), ("ES2", 144), ("ESn", 144), ("E25", 144), ("E24", 144), ("RS5", 320), ("RS4", 256), ("THR", 256),
+                ("d0", 256), ("d1", 256), ("KC", 128), ("MCS", 320), ("MCV", 5 * NV), ("cU", 128), ("cS", 128), ("cP", 128), ("cN", 128), ("c85", 128),
+                ("c24", 128), ("c32", 128), ("cq", 128), ("c16k", 128)]),
+    "ch": (f16, [("RC", 128), ("RM", 640), ("b5", 128), ("b1", 128), ("IO", 16), ("oneh", 128)]),
+    "cf": (f32, [("io", 32), ("OH", 32), ("PW", 32), ("PT", 32), ("kc", 1), ("kn", 1), ("rc", 1), ("p32", 1), ("p4", 1), ("p4d", 1), ("mets", 1), ("metc", 16), ("sel", 16)]),
+    "ci": (i32, [("pi", 1), ("pk", 1), ("pj", 1), ("meti", 1), ("mete", 1)]),
+}
+for _b, (_d, _ts) in CONST.items():
+    _c = 0
+    for _n, _w in _ts:
+        COLS[_n] = (_b, _c, _w)
+        _c += _w
+    SCRATCH[_b] = ("sbuf", [128, _c], _d)
+SCRATCH["RW"] = ("sbuf", [128, 8, 32], bf)
+BANKS = ["b%d%d" % (h, i) for h in range(2) for i in range(4)]
 for _n in BANKS:
     SCRATCH[_n] = ("psum", [128, 512], f32)
-SEMAPHORES = ["sg", "sv", "ss", "st", "loc"] + ["d%d" % i for i in range(5)] + ["o%s%d" % (c, h) for c in "FZ" for h in range(len(GR))] + \
-    ["r%s%d%d" % (c, t, h) for c in "FZ" for t in (1, 2, 3) for h in range(len(GR))]
+SEMAPHORES = ["sg", "sv", "ss", "st", "loc"] + ["d%s%d" % (c, h) for c in "ZWFXL" for h in range(2)] + \
+    ["o%s%d%d" % (c, h, i) for c in "FZX" for h in range(2) for i in range(len(GR))] + \
+    ["r%s%d%d%d" % (c, h, t, i) for c in "FZ" for h in range(2) for t in (1, 2, 3) for i in range(len(GR))]
 
-CYC, TCYC, GATH, WAKE, WIRE = 1.04e-3, 0.52e-3, 1.56, 0.22, 3.0
+CYC, TCYC, GATH, WAKE, WIRE, SLACK = 0.9e-3, 0.45e-3, 1.56, 0.25, 3.0, 0.0
 
 
 def rank_program(g, core, T, topo):
@@ -62,43 +85,56 @@ def rank_program(g, core, T, topo):
     ops = []
     hist = {}
 
-    def op(q, fn, outs, ins, cost=0.1, sem=None, inc=1):
+    def meets(a, b):
+        return a[2] < b[3] and b[2] < a[3] and a[5][0] < b[5][1] and b[5][0] < a[5][1] and not (a[6][0] == b[6][0] and a[6][1] != b[6][1])
+
+    def covers(a, b):
+        return a[2] <= b[2] and b[3] <= a[3] and a[5][0] <= b[5][0] and b[5][1] <= a[5][1] and (a[6][0] == 1 or a[6] == b[6])
+
+    def op(q, fn, outs, ins, cost=0.06, sem=None, inc=1):
         me, deps = len(ops), {}
         for accs, wr in ((ins, False), (outs, True)):
             for acc in accs:
-                for w, lo, hi, i in hist.get(acc[1], ()):
+                for w, old, i in hist.get(acc[1], ()):
                     own = ops[i][0] == q
                     if acc[1] in BANKS:
-                        if not own or (acc[2] < hi and lo < acc[3] and (w or wr)):
+                        if not own or (meets(acc, old) and (w or wr)):
                             deps[i] = deps.get(i, False) or not own
-                    elif acc[2] < hi and lo < acc[3] and (w or wr):
-                        deps[i] = deps.get(i, False) or w or not own
-        ops.append([q, fn, cost, deps, sem or semof[q], inc])
+                    elif (w or wr) and meets(acc, old):
+                        deps[i] = True
+        ops.append([q, fn, cost, deps, sem or semof[q], inc, phase[0]])
         for accs, wr in ((ins, False), (outs, True)):
             for acc in accs:
-                mark(acc[1], acc[2], acc[3], wr, me)
+                mark(acc, wr, me)
         return me
 
-    def mark(name, lo, hi, wr, me):
-        h = hist.setdefault(name, [])
-        if wr and name not in BANKS:
-            h[:] = [a for a in h if not (lo <= a[1] and a[2] <= hi)]
+    def mark(acc, wr, me):
+        h = hist.setdefault(acc[1], [])
+        if wr and acc[1] not in BANKS:
+            h[:] = [a for a in h if not covers(acc, a[1])]
         elif wr:
-            h[:] = [a for a in h if not (lo <= a[1] and a[2] <= hi and ops[a[3]][0] == ops[me][0])]
-        h.append((wr, lo, hi, me))
+            h[:] = [a for a in h if not (covers(acc, a[1]) and ops[a[2]][0] == ops[me][0])]
+        h.append((wr, acc, me))
 
-    def v(name, lo=0, hi=None, st=1, r=128):
+    def v(name, lo=0, hi=None, st=1, r=128, p=0):
         if name in COLS:
-            name, lo = COLS[name]
-            hi = lo + 1
+            name, base, wide = COLS[name]
+            lo, hi = base + lo, base + (wide if hi is None else hi)
         hi = SCRATCH[name][1][1] if hi is None else hi
-        ap = T[name][0:r, lo:hi:st] if st > 1 else T[name][0:r, lo:hi]
-        return (ap, name, lo, hi, (hi - lo + st - 1) // st)
+        ap = T[name][p:r, lo:hi:st] if st > 1 else T[name][p:r, lo:hi]
+        return (ap, name, lo, hi, (hi - lo + st - 1) // st, (p, r), (st, lo % st))
 
-    def v4(base, t, a, b, which=None):
-        name, w = "%s%d" % (base, t), 2 << t
-        ap = T[name][:, a // w:b // w, :, :] if which is None else T[name][:, a // w:b // w, which, :]
-        return (ap, name, a, b, b - a if which is None else (b - a) // 2)
+    def col(name):
+        return v(name, 0, 1)
+
+    def vx(ap, name, lo, hi, n):
+        return (ap, name, lo, hi, n, (0, 128), (1, 0))
+
+    def v4(name, t, a, b, which=None, r=128, p=0):
+        w = 2 << t
+        if which is None:
+            return (T[name][p:r, a // w:b // w, :, :], name, a, b, b - a, (p, r), (1, 0))
+        return (T[name][:, a // w:b // w, which, :], name, a, b, (b - a) // 2, (0, 128), ("pair", which))
 
     def vcost(o, *ins):
         two = all(x[1] not in BANKS and SCRATCH[x[1]][2] in (bf, f16, u16) for x in (o,) + ins[:1])
@@ -122,10 +158,13 @@ def rank_program(g, core, T, topo):
         op("v", lambda: g.vector.tensor_copy(o[0], a[0]), [o], [a], vcost(o, a))
 
     def fill(o, c):
-        op("v", lambda: g.vector.memset(o[0], c), [o], [])
+        op("v", lambda: g.vector.memset(o[0], c), [o], [], vcost(o))
 
     def red(o, a):
         op("v", lambda: g.vector.tensor_reduce(o[0], a[0], AxisListType.X, Op.add), [o], [a])
+
+    def scan(o, d0, d1, first, f0, f1):
+        op("v", lambda: g.vector.tensor_tensor_scan(o[0], d0[0], d1[0], first, f0, f1), [o], [d0, d1], max(64, o[4]) * CYC)
 
     def mm(o, l, r, start, stop):
         me = op("t", lambda: g.tensor.matmul(o[0], l[0], r[0], start, stop), [o], [l, r], max(64, r[4]) * TCYC)
@@ -134,378 +173,461 @@ def rank_program(g, core, T, topo):
         if stop:
             closed[o[1]] = me
 
+    def mms(o, *terms):
+        for i, (l, r) in enumerate(terms):
+            mm(o, l, r, i == 0, i == len(terms) - 1)
+
+    def const(name, n, r=1):
+        return (v(name, 0, 128, r=r), v("one", 0, n, r=r))
+
     def act(o, a, func, **kw):
-        op("s", lambda: g.scalar.activation(o[0], a[0], func, **kw), [o], [a], max(64, o[4]) * CYC)
+        ins = [a] + [x for x in kw.values() if isinstance(x, tuple)]
+        kw = {k: x[0] if isinstance(x, tuple) else x for k, x in kw.items()}
+        op("s", lambda: g.scalar.activation(o[0], a[0], func, **kw), [o], ins, max(64, o[4]) * CYC)
+
+    def actg(o, win, f, func, **kw):
+        ins = [win, f] + [x for x in kw.values() if isinstance(x, tuple)]
+        kw = {k: x[0] if isinstance(x, tuple) else x for k, x in kw.items()}
+        op("s", lambda: g.scalar.activation(o[0], win[0].indirect(f[0]), func, **kw), [o], ins, 0.065 + o[4] * GATH * CYC)
 
     def asel(o, a, pat, cop, base, cm):
         op("g", lambda: g.affine_select(o[0], a[0], pat, cop, 0.0, base, cm), [o], [a], 0.17 + 2 * o[4] * CYC)
 
     def iota(o, pat, base, cm, small=True):
         if small:
-            op("g", lambda: g.iota(o[0], pat, base, cm, allow_small_or_imprecise_dtypes=True), [o], [])
+            op("g", lambda: g.iota(o[0], pat, base, cm, allow_small_or_imprecise_dtypes=True), [o], [], 0.13 + 2 * o[4] * CYC)
         else:
-            op("g", lambda: g.iota(o[0], pat, base, cm), [o], [])
+            op("g", lambda: g.iota(o[0], pat, base, cm), [o], [], 0.13 + 2 * o[4] * CYC)
 
-    def mat(name, k):
-        return v(name, 128 * k, 128 * k + 128)
+    def dma(q, o, a, outs, ins, sem):
+        e = eng[q]
+        op("y" if q == "y" else q, lambda: e.dma_start(o, a), outs, ins, 2.0, sem, 16)
 
-    lists, closed = {}, {}
-    X = (T.X[:, 0:2048], "X", 0, 2048)
+    def place(name, k):
+        return v(name, 15 - k, 143 - k)
 
-    op("y", lambda: g.sync.dma_start(T.Z0[:], T.vein[:]), [v("Z0")], [], 2.0, "d0", 16)
-    op("y", lambda: g.sync.dma_start(T.win[:], T.w[:]), [v("win")], [], 2.0, "d1", 16)
-    op("y", lambda: g.sync.dma_start(T.fin[:], T.front[:]), [v("fin")], [], 2.0, "d2", 16)
-    op("y", lambda: g.sync.dma_start(T.X[:, 0:2048], T.rock[:]), [X], [], 2.0, "d3", 16)
-    op("y", lambda: g.sync.dma_start(T.lin[:], T.lim[:]), [v("lin")], [], 2.0, "d4", 16)
+    closed, phase = {}, [9]
 
-    fill(v("one"), 1.0)
-    iota(v("pi"), [[0, 1]], 0, 1, False)
-    asel(v("BD1"), v("one", 0, 128), [[-16, 8], [0, 16]], Op.is_ge, 0, 1)
-    asel(v("BD"), v("BD1"), [[16, 8], [0, 16]], Op.is_ge, 15, -1)
-    asel(v("I"), v("one", 0, 128), [[-1, 128]], Op.is_equal, 0, 1)
-    iota(v("RC", r=2), [[0, 8], [37, 16]], 0, 0)
-    for m in range(5):
-        fill(v("RM", 96 * m, 96 * m + 96, r=2), float(32 << m))
-        fill(v("RM", 96 * m, 96 * m + 96, r=1), float(m * (32 << m)))
-    fill(v("RC", r=1), 613.0)
-    ts(v("pk"), v("pi"), 15, Op.bitwise_and)
-    cp(v("kc"), v("pk"))
-    cp(v("F0"), v("fin"))
-    ts(v("w2c"), v("win"), 2.0, Op.mult)
-    ts(v("W2"), v("BD"), v("w2c"), Op.mult)
-    for m in range(5):
-        act(mat("I5", m), v("I"), Act.Copy, scale=float(32 << m))
+    def loads(h):
+        rows = slice(64 * h, 64 * h + 64)
+        for j in range(2):
+            z = v4("Z%d0" % h, 0, 0, 128, None, 64 * j + 64, 64 * j)
+            dma("y", z[0], T.vein[rows, 128 * j:128 * j + 128], [z], [], "dZ%d" % h)
+        for name, src, sem in (("win", T.w, "dW"), ("fin", T.front, "dF"), ("X", T.rock, "dX"), ("lin", T.lim, "dL")):
+            for j in range(2):
+                wide = {"fin": 128, "X": 2048}.get(name, 1)
+                o = v("%s%d" % (name, h), 0, wide, r=64 * j + 64, p=64 * j)
+                dma("y", o[0], src[rows, 128 * j:128 * j + 128] if name == "fin" else src[rows, :], [o], [], "%s%d" % (sem, h))
 
-    def prep(t, ch):
-        kind, a, b = ch
-        n = b - a
-        F, Z = v("F%d" % t, a, b), v("Z%d" % t, a, b)
-        mm(v("pU", 0, n), v("W2"), Z, True, False)
-        mm(v("pU", 0, n), v("one", 0, 128, r=1), v("one", 0, n, r=1), False, True)
-        mm(v("pU", n, 2 * n), v("BD"), Z, True, True)
-        mm(v("pU", 2 * n, 3 * n), v("I"), F, True, True)
+    def first_constants():
+        fill(v("one"), 1.0)
+        iota(v("pi"), [[0, 1]], 0, 1, False)
+        asel(v("BDt"), v("one", 0, 128), [[-16, 8], [0, 16]], Op.is_ge, 0, 1)
+        asel(v("BD"), v("BDt"), [[16, 8], [0, 16]], Op.is_ge, 15, -1)
+        asel(v("I"), v("one", 0, 128), [[-1, 128]], Op.is_equal, 0, 1)
+        iota(v("RC", r=2), [[0, 8], [37, 16]], 0, 0)
+        iota(v("cS", r=1), [[0, 8], [-1, 16]], 16, 0)
         for m in range(5):
-            o = v("pR", m * n, m * n + n)
-            mm(o, v("RC", r=2), v("RM", 96 * m, 96 * m + n, r=2), True, False)
-            mm(o, mat("I5", m), F, False, True)
-        cp(v("usi", 2 * a, 2 * b), v("pU", 0, 2 * n))
-        ts(v("u2", a, b), v("usi", 2 * a, 2 * a + n), 4095, Op.bitwise_and)
-        tt(v("P", a, b), v("pU", 2 * n, 3 * n), v("u2", a, b), Op.mult)
+            fill(v("RM", 128 * m, 128 * m + 128, r=2), float(32 << m))
+            fill(v("RM", 128 * m, 128 * m + 128, r=1), float(m * (32 << m)))
+        fill(v("RC", r=1), 613.0)
+        fill(v("cU", r=2), 1.0)
+        fill(v("cU", r=1), 1280.0 * 4096)
+        ts(v("pk"), v("pi"), 15, Op.bitwise_and)
+        cp(v("kc"), v("pk"))
+        act(v("I4096"), v("I"), Act.Copy, scale=-4096.0)
         for m in range(5):
-            cm = (5 * a + m * n, 5 * a + m * n + n)
-            tt(v("Q", *cm), v("pR", m * n, m * n + n), v("P", a, b), Op.add)
-            ts(v("C", *cm), v("Q", *cm), 5 + m, Op.logical_shift_right, 2047, Op.bitwise_and)
-            if kind == "S":
-                cp(v("off6", 6 * a + m, 6 * b - 5 + m, 6), v("C", *cm))
-        if kind == "V":
-            cp(v("offV", 0, 5 * n), v("C", 5 * a, 5 * b))
-        cp(v("c16", 5 * a, 5 * b), v("C", 5 * a, 5 * b))
-        ts(v("si", a, b), v("usi", 2 * a + n, 2 * b), 15, Op.bitwise_and)
-        ts(v4("OP", t, a, b), v("si", a, b), v("kc"), Op.is_equal)
-        ts(v4("UH", t, a, b), v("u2", a, b), 0.5, Op.mult, -0.5, Op.add)
-        ts(v("zq", a, b), Z, 0.25, Op.mult, 1279.625, Op.add)
-        ts(v("Kn", a, b), F, float(KN), Op.add)
+            act(v("I5_%d" % m), v("I"), Act.Copy, scale=float(32 << m))
 
-    def spread(t, ch):
-        kind, a, b = ch
-        for k in range(16):
-            asel(v("Zx", k, 16 * (b - a) - 15 + k, 16), v("Z%d" % t, a, b), [[0, b - a]], Op.is_gt, 1, 0)
-
-    def gather_s(t, ch):
-        for i in range(ch[1], ch[2]):
-            def one(o, f, z):
-                op("s", lambda: g.scalar.activation(o[0], X[0].indirect(f[0]), Act.Abs, bias=z[0], scale=-1.0), [o], [X, f, z], 0.065 + 80 * GATH * CYC)
-            one(v("A", 80 * i, 80 * i + 80), v("off6", 6 * i, 6 * i + 5), v("Z%d" % t, i, i + 1))
-
-    def gather_v(t, ch):
-        n = ch[2] - ch[1]
-        for m in range(5):
-            def one(o, f, z):
-                op("v", lambda: g.vector.tensor_tensor(o[0], X[0].indirect(f[0]), z[0], Op.subtract), [o], [X, f, z], 0.05 + o[4] * GATH * CYC)
-            one(v("D", 16 * n * m, 16 * n * (m + 1)), v("offV", m * n, m * n + n), v("Zx", 0, 16 * n))
-
-    def abs_v(ch):
-        n, a = ch[2] - ch[1], 80 * ch[1]
-        for m in range(5):
-            act(v("A", a + 16 * n * m, a + 16 * n * (m + 1)), v("D", 16 * n * m, 16 * n * (m + 1)), Act.Abs)
-
-    def view5(name, kind, n, m, off=0):
-        if kind == "S":
-            return v(name, off + m, off + 5 * n - 4 + m, 5)
-        return v(name, off + m * n, off + m * n + n)
-
-    def score(ch):
-        kind, a, b = ch
-        n = b - a
-        step = SUB if kind == "S" else n
-        mm(v("pS", 0, 5 * n), v("KC", r=2), v("MCS" if kind == "S" else "MCV", 0, 5 * n, r=2), True, False)
-        for m in range(5):
-            mm(view5("pS", kind, n, m), v("I"), v("c16", 5 * a + m * n, 5 * a + m * n + n), False, False)
-        for p in range(a, b, step):
-            w, off = step, 5 * (p - a)
-            o, on = v("pS", off, off + 5 * w), v("pN", off, off + 5 * w)
-            for k in range(16):
-                mm(o, mat("ES", k), v("A", 80 * p + k, 80 * (p + w) - 15 + k, 16), False, k == 15 and p + w == b)
-            pieces = 1 if kind == "S" else 5
-            for c in range(pieces):
-                x = (80 * p + c * 80 * w // pieces, 80 * p + (c + 1) * 80 * w // pieces)
-                ts(v("NR", *x), v("A", *x), v("top"), Op.is_le)
-            for k in range(16):
-                mm(on, mat("E", k), v("NR", 80 * p + k, 80 * (p + w) - 15 + k, 16), k == 0, k == 15)
-
-    def choose(t, ch):
-        kind, a, b = ch
-        n = b - a
-        KB = v("KB", a, b)
-        K1, K2 = v("K1", a, b), v("K2", a, b)
-        tt(K1, view5("pS", kind, n, 0), v("Kn", a, b), Op.min)
-        tt(K2, view5("pS", kind, n, 1), v("Kn", a, b), Op.min)
-        tt(K1, view5("pS", kind, n, 2), K1, Op.min)
-        tt(K2, view5("pS", kind, n, 3), K2, Op.min)
-        tt(K1, view5("pS", kind, n, 4), K1, Op.min)
-        tt(KB, K1, K2, Op.min)
-        for m in range(5):
-            tt(view5("EQm", kind, n, m, 5 * a), view5("pS", kind, n, m), KB, Op.is_equal)
-        tt(v("TT", 5 * a, 5 * b), v("EQm", 5 * a, 5 * b), v("pN", 0, 5 * n), Op.mult)
-        cnt = v("pN", 416, 416 + n)
-        for m in range(5):
-            mm(cnt, v("I25"), view5("TT", kind, n, m, 5 * a), m == 0, False)
-        mm(cnt, v("c85", r=1), v("one", 0, n, r=1), False, True)
-        tt(v("KF", a, b), cnt, KB, Op.max)
-        tt(v("KI", a, b), v("KF", a, b), v("Kn", a, b), Op.min)
-        ts(v4("FI", t, a, b), v("KI", a, b), 2047, Op.bitwise_and)
-
-    def meeting(t, gi):
-        a, b = GR[gi]
-        h = (b - a) // 2
-        q0, q1 = a // 2, b // 2
-        per = max(x for x in (1, 2, 4, 8, 16) if x * h <= 512)
-        rounds = [(r, "pA" if (r // per) % 2 == 0 else "pB") for r in range(0, 16, per)]
-        S, J = v("SJ", a, a + h), v("SJ", a + h, b)
-
-        def pr(name):
-            for buf, names in (("ph", ("nv", "nvS", "t1", "t2", "ohS", "ohJ")), ("pb", ("mj", "w0", "wM", "ms"))):
-                if name in names:
-                    return v(buf, 128 * names.index(name) + q0, 128 * names.index(name) + q1)
-            return v(name, q0, q1)
-
-        def big(name, k, c=1):
-            return v(name, 8 * a + k * h, 8 * a + (k + c) * h)
-        G, LM, XP, SN = (v("p1", 112 * i, 112 * i + h) for i in range(4))
-        HF = v("pN", 416, 416 + h)
-        ML, MT, JN = (v("p2", 112 * i, 112 * i + h) for i in range(3))
-        ts(v("Hh", a, a + h), v4("FI", t, a, b, 0), 0.125, Op.mult, 1279.5625, Op.add)
-        ts(v("Hh", a + h, b), v4("FI", t, a, b, 1), 0.125, Op.mult, 1279.5625, Op.add)
-        cp(S, v4("FI", t, a, b, 0))
-        cp(J, v4("FI", t, a, b, 1))
-        for r, bank in rounds:
-            for l in range(per):
-                o = v(bank, l * h, l * h + h)
-                mm(o, mat("B", r + l), v("Hh", a, a + h), True, True)
-            for l in range(per):
-                tt(big("EQ2", r + l), v(bank, l * h, l * h + h), v("Hh", a + h, b), Op.is_equal)
-        for l in range(16):
-            mm(HF, v("LT"), big("EQ2", l), l == 0, l == 15)
-        for l in range(16):
-            mm(ML, mat("Q4", l), big("EQ2", l), l == 0, l == 15)
-        for l in range(16):
-            mm(G, v("W32"), big("EQ2", l), l == 0, l == 15)
-        cp(pr("ohS"), v4("OP", t, a, b, 0))
-        cp(pr("ohJ"), v4("OP", t, a, b, 1))
-        tt(pr("JS"), J, S, Op.mult)
-        jq = v("pU", 320, 320 + h)
-        mm(jq, v("I32"), J, True, False)
-        mm(jq, v("I32"), v4("UH", t, a, b, 1), False, True)
-        tt(pr("JQ"), jq, pr("JS"), Op.add)
-        ts(pr("Jn"), pr("JQ"), 5, Op.logical_shift_right, 2047, Op.bitwise_and)
-        tt(pr("t1"), pr("Jn"), J, Op.subtract)
-        ts(pr("w0"), HF, 0.0, Op.is_gt)
-        tt(pr("wM"), ML, pr("w0"), Op.mult)
-        ts(pr("mj"), G, v("p32"), Op.is_ge)
-        mm(LM, v("BD"), pr("wM"), True, True)
-        ts(pr("ms"), LM, v("p4"), Op.is_ge)
-        mm(XP, v("BM"), pr("ms"), True, False)
-        mm(XP, v("BN"), pr("mj"), False, True)
-        for r, bank in rounds:
-            for k in range(per):
-                mm(v(bank, k * h, k * h + h), mat("B", r + k), J, True, True)
-            for k in range(per):
-                ts(big("MK", r + k), XP, v("KX", r + k, r + k + 1), Op.is_equal)
-            tt(big("PJ", r, per), v(bank, 0, per * h), big("MK", r, per), Op.mult)
-        ts(pr("nv"), XP, v("KX", 15, 16), Op.is_gt)
-        tt(pr("nvS"), pr("nv"), S, Op.mult)
-        mm(SN, v("I"), pr("nvS"), True, False)
-        for k in range(16):
-            mm(SN, v("I"), big("PJ", k), False, k == 15)
-        tt(pr("t2"), pr("t1"), pr("mj"), Op.mult)
-        mm(JN, v("I"), J, True, False)
-        mm(JN, v("I"), pr("t2"), False, True)
-        mm(MT, v("S15"), pr("mj"), True, True)
-        tt(v4("Fm", t, a, b, 1), JN, pr("ohJ"), Op.mult)
-        tt(v4("Fm", t, a, b, 0), SN, pr("ohS"), Op.mult)
-        cp(v4("FO", t, a, b, 1), JN)
-        cp(v4("FO", t, a, b, 0), SN)
-        red(v("metc", gi, gi + 1), MT)
-
-    def send(t, gi, what, src):
-        dst = T.cores[(rank + NEXT) % nrank]
-        rid, pid = topo.addr(dst, core)
-        es = topo.engines(core, dst)[:8]
-        a, b = GR[gi]
-        sem = "r%s%d%d" % (what, t + 1, gi)
-
-        def call():
-            g.remote_dma(out_ap=T["%s%d" % (what, t + 1)][:, a:b], in_ap=src[0], remote_sem=T.sem[sem], local_sem=T.sem["loc"],
-                         pid=pid, routing_id=rid, dma_engine_mask=sum(1 << e for e in es))
-        me = op("g", call, [], [src], 0.4, "loc", len(es))
-        ops.append(["r", None, WIRE, {me: False}, sem, len(topo.engines(T.cores[(rank - NEXT) % nrank], core)[:8])])
-        mark("%s%d" % (what, t + 1), a, b, True, len(ops) - 1)
-
-    def mining(t, gi):
-        a, b = GR[gi]
-        n, c0, c1 = b - a, a // 16, b // 16
-        FO, Z, o, f = v4("FO", t, a, b), v("Z%d" % t, a, b), v("Y", a, b), v("Ol", c0, c1)
-        OL, ER, VN, CN, LL = v("p2", 448, 448 + n // 16), v("pA", 0, n), v("pB", 0, n), v("pA", 256, 256 + n), v("p2", 480, 480 + n // 16)
-        if t < 3:
-            send(t, gi, "F", FO)
-        else:
-            cp(v("yo", a, b), FO)
-            op("y", lambda: g.sync.dma_start(T.yf[:, a:b], T.yo[:, a:b]), [], [v("yo", a, b)], 2.0, "oF%d" % gi, 16)
-        w = 2 << t
-        for q in range(16):
-            col = (T["Fm%d" % t][:, a // w + q // w:b // w:16 // w, q % w // (w // 2), q % (w // 2)], "Fm%d" % t, a, b, n // 16)
-            mm(OL, mat("E", q), col, q == 0, q == 15)
-        mm(ER, v("BD"), v4("Fm", t, a, b), True, True)
-        cp(f, OL)
-        cp(v("Ouf", c0, c1), OL)
-        cp(v("Er", a, b), ER)
-        op("s", lambda: g.scalar.activation(o[0], X[0].indirect(f[0]), Act.Copy), [o], [X, f], 0.065 + n * GATH * CYC)
-        if gi == len(GR) - 1:
-            for x in range(gi):
-                scatter(x)
-        mm(VN, v("Ihalf"), Z, True, False)
-        mm(VN, v("q9"), v("one", 0, n), False, False)
-        mm(VN, v("Ihalf"), o, False, True)
-        ts(v("zt", a, b), VN, 1280.0, Op.add)
-        ts(v("Zo%d" % t, a, b), v("zt", a, b), -1280.0, Op.add)
-        if t < 3:
-            send(t, gi, "Z", v("Zo%d" % t, a, b))
-        else:
-            op("y", lambda: g.sync.dma_start(T.yz[:, a:b], T["Zo3"][:, a:b]), [], [v("Zo3", a, b)], 2.0, "oZ%d" % gi, 16)
-
-        def later(c):
-            lo = max(16 * c, a)
-            w = (T.EQW[:, c, lo - 16 * c:b - 16 * c], "EQW", 256 * c + lo - 16 * c, 256 * c + b - 16 * c, b - lo)
-            return lo, w
-        for c in range(c1):
-            lo, w = later(c)
-            ts(w, v("Er", lo, b), v("Ouf", c, c + 1), Op.is_equal)
-        dg = (T.EQW[:, c0:c1, 0:16], "EQW", 256 * c0, 256 * c1, n)
-        op("v", lambda: g.vector.tensor_tensor(dg[0], dg[0], T.DM[:, c0:c1, :], Op.mult), [dg], [dg, ("", "DM", 0, 256)], 2 * n * CYC)
-        for c in range(c1):
-            lo, w = later(c)
-            mm(v("pA", 256 + lo - a, 256 + n), v("BD"), w, c == 0, c == c1 - 1)
-        act(v("lo", a, b), CN, Act.Sign)
-        mm(LL, v("I"), v("IO", c0, c1), True, False)
-        mm(LL, v("c16k", r=1), v("one", 0, n // 16, r=1), False, False)
-        for q in range(16):
-            mm(LL, mat("ES", q), v("lo", a + q, b - 15 + q, 16), False, q == 15)
-        tt(v("R1", a, b), o, v("zq", a, b), Op.subtract)
-        ts(v("R2", a, b), v("R1", a, b), 1280.0, Op.add, 0.0, Op.max)
-        tt(v("LO", c0, c1), LL, v("Ouf", c0, c1), Op.max)
-        cp(v("Ls", c0, c1), v("LO", c0, c1))
-        lists[gi] = (v("Ls", c0, c1), v("R2", a, b))
-
-    def scatter(gi):
-        XW, ls, r2 = (T.X[:, 0:2560], "X", 0, 2560), lists[gi][0], lists[gi][1]
-        op("v", lambda: g.vector.tensor_copy(XW[0].indirect(ls[0]), r2[0]), [XW], [ls, r2], 0.05 + r2[4] * 3.8 * CYC)
-
-    def limits(t):
-        if t == 0:
-            cp(v("limf"), v("lin"))
-            cp(v("top"), v("limf"))
-        else:
-            red(v("mets"), v("metc", 0, len(GR)))
-            cp(v("meti"), v("mets"))
-            ts(v("mete"), v("meti"), 3, Op.bitwise_and)
-            tt(v("top"), v("limf"), v("mete"), Op.add)
+    def stream_constants(h):
+        cp(v("F%d0" % h), v("fin%d" % h))
+        ts(col("w2c%d" % h), col("win%d" % h), 2.0, Op.mult)
+        ts(v("W2%d" % h), v("BD"), col("w2c%d" % h), Op.mult)
+        act(v("W32%d" % h), v("W2%d" % h), Act.Copy, scale=16.0)
+        fill(v("off6%d" % h, 5, 768, 6), 0)
+        cp(col("limf%d" % h), col("lin%d" % h))
+        fill(v("X%d" % h, 2048, 2560), 0.0)
+        fill(v("L5%d" % h), -1.0)
+        fill(v("L5%d" % h, 0, 320, 5), 4 * BIG)
 
     def key_constants():
-        for k in range(16):
-            asel(mat("E", k), v("BD"), [[0, 8], [1, 16]], Op.is_equal, -k, 0)
-            act(mat("ES", k), mat("E", k), Act.Copy, scale=10240.0)
+        fill(v("E"), 0.0)
+        fill(v("E", 15, 144, 16), 1.0)
+        asel(v("ES"), v("E"), [[-1, 144]], Op.is_ge, 15, 1)
+        asel(v("E"), v("ES"), [[1, 144]], Op.is_ge, 0, -1)
+        for name, x in (("ES", 10240.0), ("ES2", 20480.0), ("ESn", -10240.0), ("E25", -float(1 << 25)), ("E24", -float(1 << 24))):
+            act(v(name), v("E"), Act.Copy, scale=x)
         iota(v("KC", r=2), [[0, 128]], -4096, 6144)
-        iota(v("MCS", r=2), [[0, 96], [1, 5]], 0, 0)
-        iota(v("MCV", 0, 5 * NV, r=2), [[1, 5], [0, NV]], 0, 0)
+        iota(v("MCS", r=2), [[0, 64], [1, 5]], 0, 0)
+        iota(v("MCV", r=2), [[1, 5], [0, NV]], 0, 0)
         fill(v("MCS", r=1), 4096.0)
-        fill(v("MCV", 0, 5 * NV, r=1), 4096.0)
+        fill(v("MCV", r=1), 4096.0)
+        fill(v("RS5"), -float(1 << 25))
+        fill(v("RS5", 0, 320, 5), float(KN))
+        iota(v("b5", r=1), [[5, 128]], 0, 0)
+        iota(v("b1", r=1), [[1, 128]], 0, 0)
+        fill(v("oneh", r=1), 1.0)
+        for m in range(1, 5):
+            act(v("IS%d" % m), v("I"), Act.Copy, scale=float(m))
+            act(v("IV%d" % m), v("I"), Act.Copy, scale=float(m * NV))
+        fill(v("c85", r=1), 8.5 * (1 << 25))
+        fill(v("c24", r=1), float(1 << 24))
+        fill(v("cN", r=1), float(KN))
+
+    def pick(name, row):
+        tt(v("PT", 0, row[4]), row, v("OH", 0, row[4]), Op.mult)
+        red(v(name), v("PT", 0, row[4]))
 
     def last_constants():
-        iota(v("io"), [[1, 16]], 0, 0)
-        op("g", lambda: g.iota(T.DMi[:], [[0, 16], [1, 16]], 0, 0, allow_small_or_imprecise_dtypes=True), [("", "DMi", 0, 256)], [])
-        act(v("I25"), v("I"), Act.Copy, scale=-float(1 << 25))
-        fill(v("c85"), 8.5 * (1 << 25))
-        fill(v("c16k"), -163840.0)
-        ts(v("I32"), v("I"), 32.0, Op.mult)
-        ts(v("Ihalf"), v("I"), 0.5, Op.mult)
-        fill(v("q9"), -(2.0 ** -9))
-        ts(v("OH"), v("io"), v("kc"), Op.is_equal)
+        iota(v("io"), [[1, 32]], 0, 0)
+        ts(v("OH", 0, 16), v("io", 0, 16), v("kc"), Op.is_equal)
         for l in range(16):
-            ts(mat("B", l), v("BD"), v("OH", l, l + 1), Op.mult)
-            act(mat("Q4", l), v("I"), Act.Copy, scale=float(4 ** (15 - l)))
-        for r in range(16):
-            fill(v("PW", r, r + 1), 2.0 ** (5 * (15 - r)))
-            fill(v("PW", 16 + r, 17 + r), 2.0 ** (2 * (16 - r)))
-        for j, name in ((0, "p32"), (16, "p4")):
-            tt(v("PT", j, j + 16), v("PW", j, j + 16), v("OH"), Op.mult)
-            red(v(name), v("PT", j, j + 16))
-        asel(v("LT"), v("BD"), [[1, 128]], Op.is_gt, 0, -1)
-        ts(v("LT"), v("LT"), -32.0, Op.mult)
-        tt(v("LT"), v("LT"), v("I"), Op.add)
-        ts(v("W32"), v("BD"), v("p32"), Op.mult)
-        ts(v("BN"), v("BD"), -1.0, Op.mult)
-        ts(v("BD1"), v("I"), -64.0, Op.mult)
-        tt(v("BM"), v("BD1"), v("BD"), Op.add)
+            act(v("B%d" % l), v("BD"), Act.Copy, scale=v("OH", l, l + 1))
+            act(v("Q4_%d" % l), v("I"), Act.Copy, scale=float(4 ** (15 - l)))
+        for name, first, x in (("p32", 2.0 ** 80, 1 / 32), ("p4", 2.0 ** 34, 0.25)):
+            fill(v("d0", 0, 16), x)
+            fill(v("d1", 0, 16), 0.0)
+            scan(v("PW", 0, 16), v("d0", 0, 16), v("d1", 0, 16), first, Op.mult, Op.add)
+            pick(name, v("PW", 0, 16))
+        ts(v("G32"), v("BD"), v("p32"), Op.mult)
+        asel(v("BDt"), v("BD"), [[-1, 128]], Op.is_equal, 1, 1)
+        act(v("SHB"), v("BDt"), Act.Copy, scale=-2.0 ** 33)
         ts(v("S15"), v("one", 0, 128), v("OH", 15, 16), Op.mult)
-        ts(v("kx"), v("kc"), 65.0, Op.add)
-        ts(v("KX"), v("io"), v("kx"), Op.subtract)
-        op("v", lambda: g.vector.tensor_scalar(T.DM[:], T.DMi[:], v("kc")[0], None, Op.is_gt), [("", "DM", 0, 256)], [("", "DMi", 0, 256), v("kc")], 256 * CYC)
-        ts(v("PT", 16, 32), v("io"), 32.0, Op.mult, 2048.0, Op.add)
-        ts(v("PT", 32, 33), v("kc"), 2.0, Op.mult)
-        ts(v("IO"), v("PT", 16, 32), v("PT", 32, 33), Op.add)
+        tt(v("BN"), v("B15"), v("BD"), Op.subtract)
+        ts(v("kn"), v("kc"), -16.0, Op.add)
+        fill(v("c32", r=1), 32.0)
+        act(v("In"), v("I"), Act.Copy, scale=-1.0)
+        act(v("IB"), v("I"), Act.Copy, scale=BIG)
+        act(v("IBn"), v("I"), Act.Copy, scale=-BIG)
+        asel(v("NOK"), v("BD"), [[-16, 8], [1, 16]], Op.is_gt, -15, 1)
+        act(v("NOKn"), v("NOK"), Act.Copy, scale=-BIG)
+        act(v("NOK"), v("NOK"), Act.Copy, scale=BIG)
+        for x in range(2):
+            cp(vx(T.RW[:, :, 16 * x:16 * x + 16], "RW", 0, 256, 128), v("I"))
+        for d in (1, 2, 3, 4, 8, 12):
+            cp(v("Rot%d" % d), vx(T.RW[:, :, d:d + 16], "RW", 0, 256, 128))
+        for a in range(4):
+            for name, cols, s in (("PA", v("OH", 4 * a, 4 * a + 4), a), ("PB", v("OH", a, 16, 4), 4 + a)):
+                red(v("sel", s, s + 1), cols)
+                ts(v("sel", 8 + s, 9 + s), v("sel", s, s + 1), -BIG, Op.mult, BIG, Op.add)
+                act(v("%s%d" % (name, a)), v("BD"), Act.Copy, scale=v("sel", 8 + s, 9 + s))
+        fill(v("RS4"), -1.0)
+        fill(v("RS4", 0, 256, 4), 4 * BIG)
+        act(v("BDn"), v("BD"), Act.Copy, scale=-2048.0)
+        act(v("I32k"), v("I"), Act.Copy, scale=32768.0)
+        act(v("Ih"), v("I"), Act.Copy, scale=0.5)
+        fill(v("cq", r=1), -0.25)
+        fill(v("cP", r=2), -1280.0 * 32768)
+        ts(v("cP", r=1), v("cS", r=1), -2048.0, Op.mult, 2048.0, Op.add)
+        for name, src in (("BD", "BD"), ("I", "I")):
+            for j in range(2):
+                fill(v("%s%d" % (name, j), r=128 - 64 * j, p=64 - 64 * j), 0.0)
+                for x in range(2):
+                    cp(v("%s%d" % (name, j), 64 * x, 64 * x + 64, r=64 * j + 64, p=64 * j), v(src, 64 * j, 64 * j + 64, r=64 * j + 64, p=64 * j))
+        tt(v("BD2"), v("BD0"), v("BD1"), Op.add)
+        fill(v("d0"), 0.25)
+        fill(v("d0", 0, 256, 32), 0.0)
+        fill(v("d1"), 0.0)
+        fill(v("d1", 0, 256, 32), -0.5)
+        scan(v("THR"), v("d0"), v("d1"), 0.0, Op.mult, Op.add)
+        ts(v("pj"), v("pi"), 6, Op.logical_shift_right)
+        ts(v("rc"), v("pj"), 16.0, Op.mult, v("kc"), Op.add)
+        ts(v("OH"), v("io"), v("rc"), Op.is_equal)
+        pick("p4d", v("THR", 0, 32))
+        ts(v("W4D"), v("BD2"), v("p4d"), Op.mult, -0.5, Op.mult)
+        fill(v("c16k", r=1), -163840.0)
+        ts(v("PT", 0, 16), v("io", 0, 16), 32.0, Op.mult, 2048.0, Op.add)
+        ts(v("PT", 16, 17), v("kc"), 2.0, Op.mult)
+        ts(v("IO"), v("PT", 0, 16), v("PT", 16, 17), Op.add)
 
-    vch = [ch for ch in CH if ch[0] == "V"][0]
-    for t in range(4):
-        if t == 0:
-            for ch in CH:
-                prep(0, ch)
+    def visit(t, h):
+        def s(name, *a, **k):
+            return v("%s%d" % (name, h), *a, **k)
+
+        def bank(i, lo, hi, st=1, **k):
+            return v("b%d%d" % (h, i), lo, hi, st, **k)
+        X, zn, fm = s("X", 0, 2048), "Z%d%d" % (h, t), "Fm%d%d" % (h, t)
+
+        def prep(a, b):
+            n = b - a
+            F, Z = v("F%d%d" % (h, t), a, b), v4(zn, t, a, b)
+            U, S, V = bank(2, 0, n), bank(2, n, 2 * n), bank(2, 2 * n, 3 * n)
+            mms(U, (s("W2"), Z), const("one", n))
+            mms(S, (v("BD"), Z), const("cS", n))
+            ts(s("Hu", a, b), U, 1 / 4096, Op.mult, 1279.5, Op.add)
+            R = [bank(3, m * n, m * n + n) if m < 4 else bank(2, 3 * n, 4 * n) for m in range(5)]
+            for m in range(4):
+                mms(R[m], (v("RC", r=2), v("RM", 128 * m, 128 * m + n, r=2)), (v("I5_%d" % m), F))
+            ts(v4("Hs%d%d" % (h, t), t, a, b), S, 1 / 16, Op.mult, 1280 - 15 / 32, Op.add)
+            mms(V, (s("W2"), Z), const("cU", n, 2), (v("I4096"), s("Hu", a, b)))
+            mms(R[4], (v("RC", r=2), v("RM", 512, 512 + n, r=2)), (v("I5_4"), F))
+            tt(s("P", a, b), V, F, Op.mult)
+            cn = "C%d" % h
+            for m in range(5):
+                q = s("Q", 128 * m + a, 128 * m + b)
+                tt(q, R[m], s("P", a, b), Op.add)
+                ts(vx(T[cn][:, m, a:b], cn, 128 * m + a, 128 * m + b, n), q, 5 + m, Op.logical_shift_right, 2047, Op.bitwise_and)
+            for lo, hi in ((a, min(b, VA)), (max(a, VB), b)):
+                if lo < hi:
+                    for m in range(5):
+                        cp(s("off6", 6 * lo + m, 6 * hi - 5 + m, 6), vx(T[cn][:, m, lo:hi], cn, 128 * m + lo, 128 * m + hi, hi - lo))
+                    cp(s("c6", 6 * lo, 6 * hi), s("off6", 6 * lo, 6 * hi))
+            if a <= VA < b:
+                cp(s("offV"), vx(T[cn][:, :, VA:VB], cn, 0, 640, 5 * NV))
+                cp(s("cV"), s("offV"))
+                for k in range(16):
+                    asel(s("Zx", k, 16 * NV - 15 + k, 16), v4(zn, t, VA, VB), [[0, NV]], Op.is_gt, 1, 0)
+            ts(s("zq", a, b), Z, -0.25, Op.mult, -1279.625, Op.add)
+
+        def gather(ch):
+            kind, a, b, e = ch
+            w = 2 << t
+            if kind == "S":
+                for i in range(a, b):
+                    z = vx(T[zn][:, i // w, i % w // (w // 2), i % (w // 2):i % (w // 2) + 1], zn, i, i + 1, 1)
+                    actg(s("A", 80 * i, 80 * i + 80), X, s("off6", 6 * i, 6 * i + 5), Act.Abs, bias=z, scale=-1.0)
+                return
+            for m in range(5):
+                def one(o, f, z):
+                    op("v", lambda: g.vector.tensor_tensor(o[0], X[0].indirect(f[0]), z[0], Op.subtract), [o], [X, f, z], 0.05 + o[4] * GATH * CYC)
+                for x in range(0, NV, VP):
+                    y = min(x + VP, NV)
+                    d = (16 * (NV * m + x), 16 * (NV * m + y))
+                    one(s("D", *d), s("offV", m * NV + x, m * NV + y), s("Zx", 16 * x, 16 * y))
+                    ts(s("RL", *d), s("D", *d), 0.0, Op.max)
+
+        def choose(ci):
+            kind, a, b, e = CH[ci]
+            n, kb = b - a, ci % 2
+            keys = bank(kb, 0, 5 * n)
+            key = [bank(kb, m, 5 * n - 4 + m, 5) if kind == "S" else bank(kb, m * n, m * n + n) for m in range(5)]
+            mm(keys, v("KC", r=2), v("MCS" if kind == "S" else "MCV", 0, 5 * n, r=2), True, False)
+            if kind == "S":
+                for m in range(5):
+                    mm(key[m], v("I"), s("c6", 6 * a + m, 6 * b - 5 + m, 6), False, False)
+                for p in range(a, b, SUB):
+                    w = min(SUB, b - p)
+                    for k in range(16):
+                        mm(bank(kb, 5 * (p - a), 5 * (p - a + w)), place("ES", k), s("A", 80 * p + k, 80 * (p + w) - 15 + k, 16), False, k == 15 and p + w == b)
+                scan(s("KS", 5 * a, 5 * b), v("RS5", 0, 5 * n), keys, 0.0, Op.max, Op.min)
+            else:
+                for name, src in (("ESn", "D"), ("ES2", "RL")):
+                    for k in range(16):
+                        mm(keys, place(name, k), s(src, k, 80 * n - 15 + k, 16), False, False)
+                mm(keys, v("I"), s("cV"), False, True)
+                for m in range(5):
+                    o = s("KS", 5 * a + m, 5 * b - 4 + m, 5)
+                    if m == 0:
+                        ts(o, key[0], float(KN), Op.min)
+                    else:
+                        tt(o, key[m], s("KS", 5 * a + m - 1, 5 * b - 5 + m, 5), Op.min)
+            KB = s("KS", 5 * a + 4, 5 * b, 5)
+            eq = [s("EQm", 128 * (m - 1) + a, 128 * (m - 1) + b) for m in range(1, 5)]
+            for m in range(1, 5):
+                tt(eq[m - 1], key[m], KB, Op.is_equal)
+            at = bank(2, a, b)
+            mms(at, (v("oneh", r=1), v("b5" if kind == "S" else "b1", 0, n, r=1)), *[(v("I%s%d" % (kind, m)), eq[m - 1]) for m in range(1, 5)])
+            ts(s("pos", a, b), at, 16.0, Op.mult, v("kc"), Op.add)
+            sign = kind == "S" and e == "s"
+            win, top = s("A", 80 * a, 80 * b), col("top%d" % h)
+
+            def second(f, near, x, y):
+                if kind == "V":
+                    actg(s("NA", 16 * (x - a), 16 * (y - a)), s("D"), f, Act.Abs)
+                    ts(near, s("NA", 16 * (x - a), 16 * (y - a)), top, Op.is_le)
+                elif sign:
+                    actg(near, win, f, Act.Sign, bias=col("toph%d" % h), scale=-1.0)
+                else:
+                    op("v", lambda: g.vector.tensor_scalar(near[0], win[0].indirect(f[0]), top[0], None, Op.is_le), [near], [win, f, top], 0.05 + near[4] * GATH * CYC)
+            step = NP if e == "v" and kind == "S" else n
+            for x in range(a, b, step):
+                y = min(x + step, b)
+                second(s("pos", x, y), s("NR", 16 * x, 16 * y), x, y)
+            mms(bank(3, a, b), const("c24" if sign else "c85", n), *[(place("E24" if sign else "E25", k), s("NR", 16 * a + k, 16 * b - 15 + k, 16)) for k in range(16)])
+
+        def meeting(gi):
+            a, b = GR[gi]
+            n = b - a
+            c = n // 2
+            q0, q1 = a // 2, b // 2
+            ki, fo = "KI%d%d" % (h, t), "FO%d%d" % (h, t)
+            own = bank(3, 128 + a, 128 + b)
+            mms(own, const("cN", n), (v("I"), v("F%d%d" % (h, t), a, b)))
+            tt(s("KF", a, b), bank(3, a, b), s("KS", 5 * a + 4, 5 * b, 5), Op.max)
+            tt(v4(ki, t, a, b), own, s("KF", a, b), Op.min)
+            for x in range(2):
+                ts(s("SJi", a + x * c, a + x * c + c), v4(ki, t, a, b, x), 2047, Op.bitwise_and)
+            ts(s("Hh", a, b), s("SJi", a, b), 0.125, Op.mult, 1279.5625, Op.add)
+            cp(s("SJ", a, b), s("SJi", a, b))
+            S, J, HS, HJ = s("SJ", a, a + c), s("SJ", a + c, b), s("Hh", a, a + c), s("Hh", a + c, b)
+
+            def pr(name):
+                return s(name, q0, q1)
+
+            def big(l, x=1):
+                return s("EQ2", 8 * a + l * c, 8 * a + (l + x) * c)
+            for r in range(2):
+                for l in range(8):
+                    o = bank(r, l * c, l * c + c)
+                    if c < 64:
+                        mms(o, (v("B%d" % (8 * r + l)), HS), (v("In"), HJ))
+                    else:
+                        mms(o, (v("B%d" % (8 * r + l)), HS))
+                if c < 64:
+                    ts(big(8 * r, 8), bank(r, 0, 8 * c), 0.0, Op.is_equal)
+                else:
+                    for l in range(8):
+                        tt(big(8 * r + l), bank(r, l * c, l * c + c), HJ, Op.is_equal)
+            G, LM, XP, MT = (bank(2, 128 + 64 * i, 128 + 64 * i + c) for i in range(4))
+            ML, S32, UJ = (bank(3, 256 + 64 * i, 256 + 64 * i + c) for i in range(3))
+            mms(S32, const("c32", c), (v("I"), S))
+            mms(UJ, (s("W32"), v4(zn, t, a, b, 1)))
+            tt(pr("JS"), S32, J, Op.mult)
+            tt(pr("JQ"), UJ, pr("JS"), Op.add)
+            ts(pr("Jn"), pr("JQ"), 5, Op.logical_shift_right, 2047, Op.bitwise_and)
+            mms(G, *[(v("G32"), big(l)) for l in range(16)])
+            for l in range(16):
+                mm(ML, v("Q4_%d" % l), big(l), l == 0, False)
+            ts(pr("mj"), G, v("p32"), Op.is_ge)
+            mm(ML, v("SHB"), pr("mj"), False, True)
+            act(pr("wM"), ML, Act.Relu)
+            mms(LM, (v("BD"), pr("wM")))
+            mms(MT, (v("S15"), pr("mj")))
+            ts(pr("ms"), LM, v("p4"), Op.is_ge)
+            if t < 3:
+                x = 4 * t + 2 * h + gi
+                red(v("metc", x, x + 1), MT)
+            mms(XP, (v("BN"), pr("mj")), (v("BD"), pr("ms")))
+            JL, JH = bank(0, 320, 320 + c), bank(0, 384, 384 + c)
+            mms(JL, (v("I"), J), (v("IBn"), pr("mj")))
+            mms(JH, (v("I"), J), (v("IB"), pr("mj")))
+            ts(pr("oha"), XP, v("kc"), Op.is_equal)
+            ts(pr("ohb"), XP, v("kn"), Op.is_equal)
+            tt(pr("t1"), JL, pr("Jn"), Op.max)
+            tt(v4(fo, t, a, b, 1), JH, pr("t1"), Op.min)
+            for x in range(4):
+                mms(bank(1, x, 4 * c - 3 + x, 4), (v("PA%d" % x), pr("oha")), (v("PA%d" % x), pr("ohb")), (v("Rot%d" % (4 * x) if x else "I"), J))
+            SL, PEN = bank(3, 256, 256 + c), [bank(3, 384 + 64 * x, 384 + 64 * x + c) for x in range(2)]
+            mms(SL, (v("I"), S), (v("IBn"), pr("ms")), (v("NOK"), pr("oha")))
+            for x in range(2):
+                mms(PEN[x], const("cP", c, 2), (v("I32k"), v4("Hs%d%d" % (h, t), t, a, b, x)), (v("BDn"), v4(zn, t, a, b, x)))
+            scan(s("T1", 4 * q0, 4 * q1), v("RS4", 0, 4 * c), bank(1, 0, 4 * c), 0.0, Op.max, Op.min)
+            cp(s("L5", 5 * q0 + 4, 5 * q1, 5), SL)
+            mms(bank(0, 4, 5 * c, 5), (v("I"), S), (v("IB"), pr("ms")), (v("NOKn"), pr("oha")))
+            for x in range(4):
+                mms(bank(0, x, 5 * c - 4 + x, 5), (v("PB%d" % x), pr("oha")), (v("PB%d" % x), pr("ohb")), (v("Rot%d" % x if x else "I"), s("T1", 4 * q0 + 3, 4 * q1, 4)))
+            scan(s("T2", 5 * q0, 5 * q1), s("L5", 5 * q0, 5 * q1), bank(0, 0, 5 * c), 0.0, Op.max, Op.min)
+            SN = s("T2", 5 * q0 + 4, 5 * q1, 5)
+            tt(v4(fm, t, a, b, 1), PEN[1], v4(fo, t, a, b, 1), Op.min)
+            tt(v4(fm, t, a, b, 0), PEN[0], SN, Op.min)
+            cp(v4(fo, t, a, b, 0), SN)
+
+        def send(gi, what, src):
+            dst = T.cores[(rank + NEXT) % nrank]
+            rid, pid = topo.addr(dst, core)
+            es = topo.engines(core, dst)[:8]
+            a, b = GR[gi]
+            sem, name = "r%s%d%d%d" % (what, h, t + 1, gi), "%s%d%d" % (what, h, t + 1)
+            land = v(name, a, b) if what == "F" else v4(name, t + 1, a, b)
+
+            def call():
+                g.remote_dma(out_ap=land[0], in_ap=src[0], remote_sem=T.sem[sem], local_sem=T.sem["loc"],
+                             pid=pid, routing_id=rid, dma_engine_mask=sum(1 << e for e in es))
+            me = op("g", call, [], [src], 0.4, "loc", len(es))
+            ops.append(["r", None, WIRE, {me: False}, sem, len(topo.engines(T.cores[(rank - NEXT) % nrank], core)[:8]), phase[0]])
+            mark(land, True, len(ops) - 1)
+
+        def store(out, name, lo, gi, sem):
+            a, b = GR[gi]
+            for j in range(2):
+                src = s(name, lo + a, lo + b, r=64 * j + 64, p=64 * j)
+                dma("y", out[64 * h:64 * h + 64, 128 * j + a:128 * j + b], src[0], [], [src], "%s%d%d" % (sem, h, gi))
+
+        def veins(gi):
+            a, b = GR[gi]
+            n, c0, c1 = b - a, a // 16, b // 16
+            FO, Y, f, zo = v4("FO%d%d" % (h, t), t, a, b), s("Y", a, b), s("Ol", c0, c1), s("Zo", 128 * t + a, 128 * t + b)
+            OL, VN = bank(2, 384 + c0, 384 + c1), bank(1, 256, 256 + n)
+            w = 2 << t
+            mms(OL, *[(place("E", q), vx(T[fm][:, a // w + q // w:b // w:16 // w, q % w // (w // 2), q % (w // 2)], fm, a, b, n // 16)) for q in range(16)])
+            ts(f, OL, REST, Op.add)
+            actg(Y, X, f, Act.Copy)
+            mms(VN, const("cq", n), (v("Ih"), v4(zn, t, a, b)), (v("Ih"), Y))
+            ts(zo, VN, MAGIC, Op.add, -MAGIC, Op.add)
+            if t < 3:
+                send(gi, "F", FO)
+                send(gi, "Z", zo)
+            else:
+                cp(s("yo", a, b), FO)
+                store(T.yf, "yo", 0, gi, "oF")
+                store(T.yz, "Zo", 384, gi, "oZ")
+
+        def mining():
+            ew = "EQW%d" % h
+            ER, RR, CN, OA, LL = bank(0, 0, 256), bank(1, 0, 256), bank(0, 256, 512), bank(2, 400, 416), bank(2, 416, 432)
+            for j in range(2):
+                mms(bank(0, 128 * j, 128 * j + 128), (v("BD%d" % j), v4(fm, t, 0, 128)))
+            ts(s("Er"), ER, REST, Op.add)
+            mms(OA, *[(place("E", q), s("Er", q, 241 + q, 16)) for q in range(16)])
+            for j in range(2):
+                ts(s("OI", 0, 8, r=64 * j + 64, p=64 * j), bank(2, 400 + j, 415 + j, 2, r=64 * j + 64, p=64 * j), 1 / 16, Op.mult)
+            ts(s("Ouf"), OA, 1 / 16, Op.mult)
+            mm(CN, v("I"), v("THR"), True, False)
+            for c in range(8):
+                ts(vx(T[ew][:, c, 0:256 - 32 * c], ew, 256 * c, 256 * c + 256 - 32 * c, 256 - 32 * c), s("Er", 32 * c, 256), s("OI", c, c + 1), Op.is_equal)
+                if c < 7:
+                    mm(bank(0, 288 + 32 * c, 512), v("BD2"), vx(T[ew][:, c, 32:256 - 32 * c], ew, 256 * c + 32, 256 * c + 256, 224 - 32 * c), False, False)
+                mm(bank(0, 256 + 32 * c, 288 + 32 * c), v("W4D"), vx(T[ew][:, c, 0:32], ew, 256 * c, 256 * c + 32, 32), False, c == 7)
+            act(s("lo"), CN, Act.Sign)
+            mms(LL, (v("I"), v("IO")), const("c16k", 16), *[(place("ES", q), s("lo", q, 241 + q, 16)) for q in range(16)])
+            for j in range(2):
+                mms(bank(1, 128 * j, 128 * j + 128), (v("I%d" % j), s("zq")), (v("I%d" % j), s("Y")))
+            ts(s("R2"), RR, 1280.0, Op.add, 0.0, Op.max)
+            tt(s("LO"), LL, s("Ouf"), Op.max)
+            cp(s("Ls"), s("LO"))
+            XW, ls, r2 = s("X"), s("Ls"), s("R2")
+            op("v", lambda: g.vector.tensor_copy(XW[0].indirect(ls[0]), r2[0]), [XW], [ls, r2], 0.05 + 256 * 3.8 * CYC)
+
+        phase[0] = 2 * t + h - (1.5 if t else 0)
+        for a, b in GR:
+            prep(a, b)
+        if t == 0 and h == 0:
+            phase[0] = 9
             key_constants()
             last_constants()
+        phase[0] = 2 * t + h
+        if t and not h:
+            red(v("mets"), v("metc", 4 * t - 4, 4 * t))
+            cp(v("meti"), v("mets"))
+            ts(v("mete"), v("meti"), 3, Op.bitwise_and)
+        if t:
+            tt(col("top%d" % h), col("limf%d" % h), v("mete"), Op.add)
         else:
-            for ch in CH:
-                if ch[1] >= GR[-1][0]:
-                    prep(t, ch)
-        spread(t, vch)
+            cp(col("top%d" % h), col("limf%d" % h))
+        if any(ch[0] == "S" and ch[3] == "s" for ch in CH):
+            ts(col("toph%d" % h), col("top%d" % h), 0.5, Op.add)
         for ch in CH:
-            if ch[0] == "S":
-                gather_s(t, ch)
-        gather_v(t, vch)
-        limits(t)
-        abs_v(vch)
+            gather(ch)
         for gi, (a, b) in enumerate(GR):
-            for ch in CH:
+            for ci, ch in enumerate(CH):
                 if a <= ch[1] < b:
-                    score(ch)
-                    choose(t, ch)
-            meeting(t, gi)
-            mining(t, gi)
-            if gi == len(GR) - 1:
-                scatter(gi)
-            elif t < 3:
-                for ch in CH:
-                    if a <= ch[1] < b:
-                        prep(t + 1, ch)
-    op("y", lambda: g.sync.dma_start(T.yx[:], T.X[:, 0:2048]), [], [X], 2.0, "d3", 16)
+                    choose(ci)
+            meeting(gi)
+            veins(gi)
+        mining()
+        if t == 3:
+            src = s("X", 0, 2048, r=64)
+            dma("y", T.yx[64 * h:64 * h + 64, :], src[0], [], [src], "oX%d0" % h)
+
+    loads(0)
+    loads(1)
+    first_constants()
+    fill(v("metc"), 0.0)
+    for h in range(2):
+        stream_constants(h)
+    for t in range(4):
+        for h in range(2):
+            visit(t, h)
 
     succ = [[] for _ in ops]
     left = [0] * len(ops)
@@ -519,37 +641,46 @@ def rank_program(g, core, T, topo):
         for j in succ[i]:
             best = max(best, way[j] + (WAKE if ops[j][3][i] else 0.0))
         way[i] = best + ops[i][2]
-    free, ready = {}, {}
-    early = [0.0] * len(ops)
-    for i, o in enumerate(ops):
-        free[o[0]] = 0.0
-        ready.setdefault(o[0], [])
-        if not left[i]:
-            ready[o[0]].append(i)
-    order = []
-    while len(order) < len(ops):
-        pick = None
-        for q, r in ready.items():
-            if r:
-                start = max(free[q], min(early[i] for i in r))
-                if pick is None or start < pick[0]:
-                    pick = (start, q)
-        start, q = pick
-        i = max((i for i in ready[q] if early[i] <= start + 1e-9), key=lambda i: way[i])
-        ready[q].remove(i)
+        for j in succ[i]:
+            ops[i][6] = min(ops[i][6], ops[j][6])
+    free = {o[0]: [] for o in ops}
+    rank_of = {i: x for x, i in enumerate(sorted(range(len(ops)), key=lambda i: (ops[i][6], -way[i], i)))}
+    early, ready, placed = [0.0] * len(ops), [(rank_of[i], i) for i in range(len(ops)) if not left[i]], []
+    while ready:
+        first = min(ready)
+        ready.remove(first)
+        i = first[1]
+        q, start = ops[i][0], early[i]
+        hold = {"r": 0.0, "y": 0.1}.get(q, ops[i][2])
+        taken = free[q]
+        x = len(taken)
+        while x and taken[x - 1][0] > start:
+            x -= 1
+        if x and taken[x - 1][1] > start:
+            start = taken[x - 1][1]
+        while x < len(taken) and start + hold > taken[x][0] + SLACK:
+            start = taken[x][1]
+            x += 1
+        if x and taken[x - 1][1] >= start:
+            taken[x - 1][1] = start + hold
+        else:
+            taken.insert(x, [start, start + hold])
+            x += 1
+        if x < len(taken) and taken[x - 1][1] >= taken[x][0]:
+            taken[x - 1][1] = max(taken[x - 1][1], taken[x][1])
+            del taken[x]
+        placed.append((start, len(placed), i))
         end = start + ops[i][2]
-        if q != "r":
-            free[q] = end if q != "y" else start + 0.1
-        order.append(i)
         for j in succ[i]:
             left[j] -= 1
-            early[j] = max(early[j], end + WAKE if ops[j][3][i] else (end if ops[j][0] == "r" else start))
+            early[j] = max(early[j], end + WAKE if ops[j][3][i] else (end if ops[j][0] == "r" else start + hold))
             if not left[j]:
-                ready[ops[j][0]].append(j)
+                ready.append((rank_of[j], j))
+    order = [i for start, x, i in sorted(placed)]
 
     count, know, value, clocks = {}, {q: {} for q in free}, {}, {}
     for i in order:
-        q, fn, cost, deps, sem, inc = ops[i]
+        q, fn, cost, deps, sem, inc = ops[i][:6]
         k = know[q]
         best = {}
         for j, wait in deps.items():
@@ -558,9 +689,9 @@ def rank_program(g, core, T, topo):
         for j in sorted(best.values(), key=lambda j: -len(clocks[j])):
             if k.get(ops[j][4], 0) < value[j]:
                 eng[q].wait_ge(T.sem[ops[j][4]], value[j])
-                for s, x in clocks[j].items():
-                    if k.get(s, 0) < x:
-                        k[s] = x
+                for x, y in clocks[j].items():
+                    if k.get(x, 0) < y:
+                        k[x] = y
         count[sem] = value[i] = count.get(sem, 0) + inc
         clocks[i] = {sem: value[i]}
         if q != "r":
@@ -569,6 +700,6 @@ def rank_program(g, core, T, topo):
                 r.then_inc(T.sem[sem], inc)
             clocks[i] = dict(k)
             clocks[i][sem] = value[i]
-    for s in SEMAPHORES:
-        if count.get(s):
-            g.wait_ge(T.sem[s], count[s])
+    for x in SEMAPHORES:
+        if count.get(x):
+            g.wait_ge(T.sem[x], count[x])

@@ -1,12 +1,15 @@
 from concourse.mybir import dt, AluOpType as Op, AxisListType, ActivationFunctionType as Act
 
 NEXT = 1
-CH = [("S", 0, 64, "v"), ("S", 64, 96, "v"), ("V", 96, 128, "s")]
+USUAL = [("S", 0, 32, "v", 0), ("S", 32, 64, "v", 3), ("V", 96, 128, "s", 1), ("S", 64, 96, "v", 2)]
+FIRST = [("S", 0, 32, "v", 0), ("V", 96, 128, "s", 1), ("V", 64, 96, "s", 2), ("S", 32, 64, "v", 3)]
+PLAN = {}
 GR = [(0, 128)]
+PREP = [(0, 64), (64, 128)]
 VP, NP = 16, 16
 SUB = 16
-VA, VB = [(a, b) for k, a, b, e in CH if k == "V"][0]
-NV = VB - VA
+VA, NV = 64, 64
+WIDE = sorted({ch[2] - ch[1] for chs in [USUAL] + list(PLAN.values()) for ch in chs if ch[0] == "V"})
 KN = 13 << 20
 BIG = 4096.0
 MAGIC = 1.5 * (1 << 23)
@@ -15,7 +18,7 @@ REST = 2048.0 * 105
 f32, bf, f16, i32, u16 = "float32", "bfloat16", "float16", "int32", "uint16"
 SCRATCH = {}
 PER = {
-    "X": ([128, 2560], bf), "A": ([128, 80 * 128], bf), "D": ([128, 80 * NV], bf), "RL": ([128, 80 * NV], bf), "Zx": ([128, 16 * NV], bf),
+    "X": ([128, 2560], bf), "A": ([128, 80 * 128], bf), "RL": ([128, 80 * NV], bf), "Zx": ([128, 16 * NV], bf),
     "off6": ([128, 768], u16), "offV": ([128, 5 * NV], u16), "c6": ([128, 768], f16), "cV": ([128, 5 * NV], f16),
     "P": ([128, 128], f32), "Q": ([128, 640], i32), "C": ([128, 5, 128], i32), "KS": ([128, 640], f32), "EQm": ([128, 512], bf),
     "NR": ([128, 2048], bf), "NA": ([128, 16 * NV], bf), "EQ2": ([128, 1024], bf), "EQW": ([128, 8, 256], bf),
@@ -43,18 +46,19 @@ for _h in range(2):
         for _n, _d in (("Z", bf), ("KI", i32), ("FO", f16), ("Hs", f16), ("Fm", f16)):
             SCRATCH["%s%d%d" % (_n, _h, _t)] = ("sbuf", [128, 64 >> _t, 2, 1 << _t], _d)
     SCRATCH["Zo%d" % _h] = ("sbuf", [128, 4 * 128], bf)
-MATS = ["BD", "I", "In", "BDt", "Ih", "I4096", "I32k", "BDn", "G32", "SHB", "BN", "S15", "NOK", "NOKn", "IB", "IBn", "BD0", "BD1", "I0", "I1", "BD2", "W4D"] + \
-    ["I5_%d" % m for m in range(5)] + ["IS%d" % m for m in range(1, 5)] + ["IV%d" % m for m in range(1, 5)] + \
-    ["B%d" % l for l in range(16)] + ["Q4_%d" % l for l in range(16)] + ["Rot%d" % d for d in (1, 2, 3, 4, 8, 12)] + \
+MATS = ["BD", "I", "BDt", "G32", "SH", "BN", "S15", "NOK", "BD0", "BD1", "I0", "I1", "BD2", "W4D"] + \
+    ["B%d" % l for l in range(16)] + ["Rot%d" % d for d in (1, 2, 3, 4, 8, 12)] + \
     ["PA%d" % a for a in range(4)] + ["PB%d" % a for a in range(4)]
+SCRATCH["pool"] = ("sbuf", [128, 144 * 40], bf)
+EARLY = 30
 SCRATCH["mats"] = ("sbuf", [128, 128 * len(MATS)], bf)
 for _i, _n in enumerate(MATS):
     COLS[_n] = ("mats", 128 * _i, 128)
 CONST = {
-    "cb": (bf, [("one", 256), ("E", 144), ("ES", 144), ("ES2", 144), ("ESn", 144), ("E25", 144), ("E24", 144), ("RS5", 320), ("RS4", 256), ("THR", 256),
-                ("d0", 256), ("d1", 256), ("KC", 128), ("MCS", 320), ("MCV", 5 * NV), ("cU", 128), ("cS", 128), ("cP", 128), ("cN", 128), ("c85", 128),
-                ("c24", 128), ("c32", 128), ("cq", 128), ("c16k", 128)]),
-    "ch": (f16, [("RC", 128), ("RM", 640), ("b5", 128), ("b1", 128), ("IO", 16), ("oneh", 128)]),
+    "cb": (bf, [("one", 256), ("E", 144), ("Et", 144), ("RS5", 320), ("RS4", 256), ("THR", 256),
+                ("d0", 256), ("d1", 256), ("KC", 128), ("MCS", 320), ("cU", 128), ("cS", 128), ("cP", 128), ("cN", 128), ("c85", 128),
+                ("c24", 128), ("c32", 128), ("cq", 128), ("c16k", 128)] + [("MCV%d" % n, 5 * n) for n in WIDE]),
+    "ch": (f16, [("RC", 128), ("RM", 640), ("b1", 64), ("IO", 16), ("oneh", 128), ("c160", 128)]),
     "cf": (f32, [("io", 32), ("OH", 32), ("PW", 32), ("PT", 32), ("kc", 1), ("kn", 1), ("rc", 1), ("p32", 1), ("p4", 1), ("p4d", 1), ("mets", 1), ("metc", 16), ("sel", 16)]),
     "ci": (i32, [("pi", 1), ("pk", 1), ("pj", 1), ("meti", 1), ("mete", 1)]),
 }
@@ -72,7 +76,8 @@ SEMAPHORES = ["sg", "sv", "ss", "st", "loc"] + ["d%s%d" % (c, h) for c in "ZWFXL
     ["o%s%d%d" % (c, h, i) for c in "FZX" for h in range(2) for i in range(len(GR))] + \
     ["r%s%d%d%d" % (c, h, t, i) for c in "FZ" for h in range(2) for t in (1, 2, 3) for i in range(len(GR))]
 
-CYC, TCYC, GATH, WAKE, WIRE, SLACK = 0.9e-3, 0.45e-3, 1.56, 0.25, 3.0, 0.0
+CYC, TCYC, GATH, WAKE, WIRE = 0.85e-3, 0.43e-3, 1.56, 0.21, 3.0
+ROUNDS, AHEAD = 3, 12.0
 
 
 def rank_program(g, core, T, topo):
@@ -95,26 +100,39 @@ def rank_program(g, core, T, topo):
         me, deps = len(ops), {}
         for accs, wr in ((ins, False), (outs, True)):
             for acc in accs:
-                for w, old, i in hist.get(acc[1], ()):
-                    own = ops[i][0] == q
-                    if acc[1] in BANKS:
-                        if not own or (meets(acc, old) and (w or wr)):
-                            deps[i] = deps.get(i, False) or not own
-                    elif (w or wr) and meets(acc, old):
+                writes, reads = hist.get(acc[1], ((), ()))
+                if acc[1] in BANKS:
+                    turn = reads and ops[reads[-1][1]][0] != q
+                    for old, i, w in (reads if turn else writes):
                         deps[i] = True
-        ops.append([q, fn, cost, deps, sem or semof[q], inc, phase[0]])
+                    for old, i, w in (() if turn else reads):
+                        if (w or wr) and meets(acc, old):
+                            deps.setdefault(i, False)
+                else:
+                    for olds in (writes, reads if wr else ()):
+                        for old, i in olds:
+                            if meets(acc, old):
+                                deps[i] = True
+        ops.append([q, fn, cost, deps, sem or semof[q], inc])
         for accs, wr in ((ins, False), (outs, True)):
             for acc in accs:
                 mark(acc, wr, me)
         return me
 
     def mark(acc, wr, me):
-        h = hist.setdefault(acc[1], [])
-        if wr and acc[1] not in BANKS:
-            h[:] = [a for a in h if not covers(acc, a[1])]
-        elif wr:
-            h[:] = [a for a in h if not (covers(acc, a[1]) and ops[a[2]][0] == ops[me][0])]
-        h.append((wr, acc, me))
+        both = hist.setdefault(acc[1], ([], []))
+        if acc[1] in BANKS:
+            if both[1] and ops[both[1][-1][1]][0] != ops[me][0]:
+                both[0][:] = both[1]
+                del both[1][:]
+            if wr:
+                both[1][:] = [a for a in both[1] if not covers(acc, a[0])]
+            both[1].append((acc, me, wr))
+            return
+        if wr:
+            for h in both:
+                h[:] = [a for a in h if not covers(acc, a[0])]
+        both[0 if wr else 1].append((acc, me))
 
     def v(name, lo=0, hi=None, st=1, r=128, p=0):
         if name in COLS:
@@ -203,10 +221,23 @@ def rank_program(g, core, T, topo):
         e = eng[q]
         op("y" if q == "y" else q, lambda: e.dma_start(o, a), outs, ins, 2.0, sem, 16)
 
-    def place(name, k):
-        return v(name, 15 - k, 143 - k)
+    def times(x, name="I", lo=0):
+        if x == 1:
+            return v(name, lo, lo + 128)
+        if (name, x) not in pool:
+            pool[name, x] = c = 144 * len(pool)
+            o = v("pool", c, c + COLS[name][2])
+            if len(pool) <= EARLY:
+                act(o, v(name), Act.Copy, scale=float(x))
+            else:
+                ts(o, v(name), float(x), Op.mult)
+        c = pool[name, x] + lo
+        return v("pool", c, c + 128)
 
-    closed, phase = {}, [9]
+    def place(x, k):
+        return times(x, "E", 15 - k)
+
+    closed, last, pool, due = {}, [], {}, {}
 
     def loads(h):
         rows = slice(64 * h, 64 * h + 64)
@@ -235,15 +266,12 @@ def rank_program(g, core, T, topo):
         fill(v("cU", r=1), 1280.0 * 4096)
         ts(v("pk"), v("pi"), 15, Op.bitwise_and)
         cp(v("kc"), v("pk"))
-        act(v("I4096"), v("I"), Act.Copy, scale=-4096.0)
-        for m in range(5):
-            act(v("I5_%d" % m), v("I"), Act.Copy, scale=float(32 << m))
 
     def stream_constants(h):
         cp(v("F%d0" % h), v("fin%d" % h))
         ts(col("w2c%d" % h), col("win%d" % h), 2.0, Op.mult)
         ts(v("W2%d" % h), v("BD"), col("w2c%d" % h), Op.mult)
-        act(v("W32%d" % h), v("W2%d" % h), Act.Copy, scale=16.0)
+        ts(v("W32%d" % h), v("W2%d" % h), 16.0, Op.mult)
         fill(v("off6%d" % h, 5, 768, 6), 0)
         cp(col("limf%d" % h), col("lin%d" % h))
         fill(v("X%d" % h, 2048, 2560), 0.0)
@@ -253,23 +281,19 @@ def rank_program(g, core, T, topo):
     def key_constants():
         fill(v("E"), 0.0)
         fill(v("E", 15, 144, 16), 1.0)
-        asel(v("ES"), v("E"), [[-1, 144]], Op.is_ge, 15, 1)
-        asel(v("E"), v("ES"), [[1, 144]], Op.is_ge, 0, -1)
-        for name, x in (("ES", 10240.0), ("ES2", 20480.0), ("ESn", -10240.0), ("E25", -float(1 << 25)), ("E24", -float(1 << 24))):
-            act(v(name), v("E"), Act.Copy, scale=x)
+        asel(v("Et"), v("E"), [[-1, 144]], Op.is_ge, 15, 1)
+        asel(v("E"), v("Et"), [[1, 144]], Op.is_ge, 0, -1)
         iota(v("KC", r=2), [[0, 128]], -4096, 6144)
         iota(v("MCS", r=2), [[0, 64], [1, 5]], 0, 0)
-        iota(v("MCV", r=2), [[1, 5], [0, NV]], 0, 0)
         fill(v("MCS", r=1), 4096.0)
-        fill(v("MCV", r=1), 4096.0)
+        for n in WIDE:
+            iota(v("MCV%d" % n, r=2), [[1, 5], [0, n]], 0, 0)
+            fill(v("MCV%d" % n, r=1), 4096.0)
         fill(v("RS5"), -float(1 << 25))
         fill(v("RS5", 0, 320, 5), float(KN))
-        iota(v("b5", r=1), [[5, 128]], 0, 0)
-        iota(v("b1", r=1), [[1, 128]], 0, 0)
+        iota(v("b1", r=1), [[1, 64]], 0, 0)
         fill(v("oneh", r=1), 1.0)
-        for m in range(1, 5):
-            act(v("IS%d" % m), v("I"), Act.Copy, scale=float(m))
-            act(v("IV%d" % m), v("I"), Act.Copy, scale=float(m * NV))
+        fill(v("c160", r=1), 160.0)
         fill(v("c85", r=1), 8.5 * (1 << 25))
         fill(v("c24", r=1), float(1 << 24))
         fill(v("cN", r=1), float(KN))
@@ -282,26 +306,19 @@ def rank_program(g, core, T, topo):
         iota(v("io"), [[1, 32]], 0, 0)
         ts(v("OH", 0, 16), v("io", 0, 16), v("kc"), Op.is_equal)
         for l in range(16):
-            act(v("B%d" % l), v("BD"), Act.Copy, scale=v("OH", l, l + 1))
-            act(v("Q4_%d" % l), v("I"), Act.Copy, scale=float(4 ** (15 - l)))
+            asel(v("B%d" % l), v("one", 0, 128), [[-16, 8], [0, 16]], Op.is_equal, -l, 1)
         for name, first, x in (("p32", 2.0 ** 80, 1 / 32), ("p4", 2.0 ** 34, 0.25)):
             fill(v("d0", 0, 16), x)
             fill(v("d1", 0, 16), 0.0)
             scan(v("PW", 0, 16), v("d0", 0, 16), v("d1", 0, 16), first, Op.mult, Op.add)
             pick(name, v("PW", 0, 16))
         ts(v("G32"), v("BD"), v("p32"), Op.mult)
-        asel(v("BDt"), v("BD"), [[-1, 128]], Op.is_equal, 1, 1)
-        act(v("SHB"), v("BDt"), Act.Copy, scale=-2.0 ** 33)
+        asel(v("SH"), v("BD"), [[-1, 128]], Op.is_equal, 1, 1)
         ts(v("S15"), v("one", 0, 128), v("OH", 15, 16), Op.mult)
         tt(v("BN"), v("B15"), v("BD"), Op.subtract)
         ts(v("kn"), v("kc"), -16.0, Op.add)
         fill(v("c32", r=1), 32.0)
-        act(v("In"), v("I"), Act.Copy, scale=-1.0)
-        act(v("IB"), v("I"), Act.Copy, scale=BIG)
-        act(v("IBn"), v("I"), Act.Copy, scale=-BIG)
         asel(v("NOK"), v("BD"), [[-16, 8], [1, 16]], Op.is_gt, -15, 1)
-        act(v("NOKn"), v("NOK"), Act.Copy, scale=-BIG)
-        act(v("NOK"), v("NOK"), Act.Copy, scale=BIG)
         for x in range(2):
             cp(vx(T.RW[:, :, 16 * x:16 * x + 16], "RW", 0, 256, 128), v("I"))
         for d in (1, 2, 3, 4, 8, 12):
@@ -310,12 +327,9 @@ def rank_program(g, core, T, topo):
             for name, cols, s in (("PA", v("OH", 4 * a, 4 * a + 4), a), ("PB", v("OH", a, 16, 4), 4 + a)):
                 red(v("sel", s, s + 1), cols)
                 ts(v("sel", 8 + s, 9 + s), v("sel", s, s + 1), -BIG, Op.mult, BIG, Op.add)
-                act(v("%s%d" % (name, a)), v("BD"), Act.Copy, scale=v("sel", 8 + s, 9 + s))
+                ts(v("%s%d" % (name, a)), v("BD"), v("sel", 8 + s, 9 + s), Op.mult)
         fill(v("RS4"), -1.0)
         fill(v("RS4", 0, 256, 4), 4 * BIG)
-        act(v("BDn"), v("BD"), Act.Copy, scale=-2048.0)
-        act(v("I32k"), v("I"), Act.Copy, scale=32768.0)
-        act(v("Ih"), v("I"), Act.Copy, scale=0.5)
         fill(v("cq", r=1), -0.25)
         fill(v("cP", r=2), -1280.0 * 32768)
         ts(v("cP", r=1), v("cS", r=1), -2048.0, Op.mult, 2048.0, Op.add)
@@ -340,13 +354,14 @@ def rank_program(g, core, T, topo):
         ts(v("PT", 16, 17), v("kc"), 2.0, Op.mult)
         ts(v("IO"), v("PT", 0, 16), v("PT", 16, 17), Op.add)
 
-    def visit(t, h):
+    def visit(t, h, lists=None):
         def s(name, *a, **k):
             return v("%s%d" % (name, h), *a, **k)
 
         def bank(i, lo, hi, st=1, **k):
             return v("b%d%d" % (h, i), lo, hi, st, **k)
         X, zn, fm = s("X", 0, 2048), "Z%d%d" % (h, t), "Fm%d%d" % (h, t)
+        CH = PLAN.get((t, h), USUAL)
 
         def prep(a, b):
             n = b - a
@@ -357,64 +372,72 @@ def rank_program(g, core, T, topo):
             ts(s("Hu", a, b), U, 1 / 4096, Op.mult, 1279.5, Op.add)
             R = [bank(3, m * n, m * n + n) if m < 4 else bank(2, 3 * n, 4 * n) for m in range(5)]
             for m in range(4):
-                mms(R[m], (v("RC", r=2), v("RM", 128 * m, 128 * m + n, r=2)), (v("I5_%d" % m), F))
+                mms(R[m], (v("RC", r=2), v("RM", 128 * m, 128 * m + n, r=2)), (times(32 << m), F))
             ts(v4("Hs%d%d" % (h, t), t, a, b), S, 1 / 16, Op.mult, 1280 - 15 / 32, Op.add)
-            mms(V, (s("W2"), Z), const("cU", n, 2), (v("I4096"), s("Hu", a, b)))
-            mms(R[4], (v("RC", r=2), v("RM", 512, 512 + n, r=2)), (v("I5_4"), F))
+            mms(V, (s("W2"), Z), const("cU", n, 2), (times(-4096), s("Hu", a, b)))
+            mms(R[4], (v("RC", r=2), v("RM", 512, 512 + n, r=2)), (times(512), F))
             tt(s("P", a, b), V, F, Op.mult)
             cn = "C%d" % h
             for m in range(5):
                 q = s("Q", 128 * m + a, 128 * m + b)
                 tt(q, R[m], s("P", a, b), Op.add)
                 ts(vx(T[cn][:, m, a:b], cn, 128 * m + a, 128 * m + b, n), q, 5 + m, Op.logical_shift_right, 2047, Op.bitwise_and)
-            for lo, hi in ((a, min(b, VA)), (max(a, VB), b)):
-                if lo < hi:
+            for kind in "SV":
+                mine = sorted(ch[1:3] for ch in CH if ch[0] == kind and a <= ch[1] < b)
+                if not mine:
+                    continue
+                lo, hi = mine[0][0], mine[-1][1]
+                if kind == "S":
                     for m in range(5):
                         cp(s("off6", 6 * lo + m, 6 * hi - 5 + m, 6), vx(T[cn][:, m, lo:hi], cn, 128 * m + lo, 128 * m + hi, hi - lo))
                     cp(s("c6", 6 * lo, 6 * hi), s("off6", 6 * lo, 6 * hi))
-            if a <= VA < b:
-                cp(s("offV"), vx(T[cn][:, :, VA:VB], cn, 0, 640, 5 * NV))
-                cp(s("cV"), s("offV"))
+                    continue
+                for x, y in mine:
+                    cp(s("offV", 5 * (x - VA), 5 * (y - VA)), vx(T[cn][:, :, x:y], cn, x, 512 + y, 5 * (y - x)))
+                cp(s("cV", 5 * (lo - VA), 5 * (hi - VA)), s("offV", 5 * (lo - VA), 5 * (hi - VA)))
                 for k in range(16):
-                    asel(s("Zx", k, 16 * NV - 15 + k, 16), v4(zn, t, VA, VB), [[0, NV]], Op.is_gt, 1, 0)
-            ts(s("zq", a, b), Z, -0.25, Op.mult, -1279.625, Op.add)
+                    asel(s("Zx", 16 * (lo - VA) + k, 16 * (hi - VA) - 15 + k, 16), v4(zn, t, lo, hi), [[0, hi - lo]], Op.is_gt, 1, 0)
 
         def gather(ch):
-            kind, a, b, e = ch
+            kind, a, b = ch[:3]
             w = 2 << t
             if kind == "S":
                 for i in range(a, b):
                     z = vx(T[zn][:, i // w, i % w // (w // 2), i % (w // 2):i % (w // 2) + 1], zn, i, i + 1, 1)
                     actg(s("A", 80 * i, 80 * i + 80), X, s("off6", 6 * i, 6 * i + 5), Act.Abs, bias=z, scale=-1.0)
+                    if last:
+                        ops[-1][3].setdefault(last[0], False)
+                    last[:] = [len(ops) - 1]
                 return
             for m in range(5):
                 def one(o, f, z):
                     op("v", lambda: g.vector.tensor_tensor(o[0], X[0].indirect(f[0]), z[0], Op.subtract), [o], [X, f, z], 0.05 + o[4] * GATH * CYC)
-                for x in range(0, NV, VP):
-                    y = min(x + VP, NV)
-                    d = (16 * (NV * m + x), 16 * (NV * m + y))
-                    one(s("D", *d), s("offV", m * NV + x, m * NV + y), s("Zx", 16 * x, 16 * y))
-                    ts(s("RL", *d), s("D", *d), 0.0, Op.max)
+                n, c = b - a, a - VA
+                for x in range(0, n, VP):
+                    y = min(x + VP, n)
+                    d = s("A", 80 * a + 16 * (n * m + x), 80 * a + 16 * (n * m + y))
+                    one(d, s("offV", 5 * c + m * n + x, 5 * c + m * n + y), s("Zx", 16 * (c + x), 16 * (c + y)))
+                    ts(s("RL", 80 * c + 16 * (n * m + x), 80 * c + 16 * (n * m + y)), d, 0.0, Op.max)
 
         def choose(ci):
-            kind, a, b, e = CH[ci]
-            n, kb = b - a, ci % 2
+            kind, a, b, e, kb = CH[ci]
+            n = b - a
             keys = bank(kb, 0, 5 * n)
             key = [bank(kb, m, 5 * n - 4 + m, 5) if kind == "S" else bank(kb, m * n, m * n + n) for m in range(5)]
-            mm(keys, v("KC", r=2), v("MCS" if kind == "S" else "MCV", 0, 5 * n, r=2), True, False)
+            mm(keys, v("KC", r=2), v("MCS" if kind == "S" else "MCV%d" % n, 0, 5 * n, r=2), True, False)
             if kind == "S":
                 for m in range(5):
                     mm(key[m], v("I"), s("c6", 6 * a + m, 6 * b - 5 + m, 6), False, False)
                 for p in range(a, b, SUB):
                     w = min(SUB, b - p)
                     for k in range(16):
-                        mm(bank(kb, 5 * (p - a), 5 * (p - a + w)), place("ES", k), s("A", 80 * p + k, 80 * (p + w) - 15 + k, 16), False, k == 15 and p + w == b)
+                        mm(bank(kb, 5 * (p - a), 5 * (p - a + w)), place(10240, k), s("A", 80 * p + k, 80 * (p + w) - 15 + k, 16), False, k == 15 and p + w == b)
                 scan(s("KS", 5 * a, 5 * b), v("RS5", 0, 5 * n), keys, 0.0, Op.max, Op.min)
             else:
-                for name, src in (("ESn", "D"), ("ES2", "RL")):
+                for x, src, c in ((-10240, "A", a), (20480, "RL", a - VA)):
                     for k in range(16):
-                        mm(keys, place(name, k), s(src, k, 80 * n - 15 + k, 16), False, False)
-                mm(keys, v("I"), s("cV"), False, True)
+                        mm(keys, place(x, k), s(src, 80 * c + k, 80 * (c + n) - 15 + k, 16), False, False)
+                mm(keys, v("I"), s("cV", 5 * (a - VA), 5 * (b - VA)), False, True)
                 for m in range(5):
                     o = s("KS", 5 * a + m, 5 * b - 4 + m, 5)
                     if m == 0:
@@ -425,16 +448,16 @@ def rank_program(g, core, T, topo):
             eq = [s("EQm", 128 * (m - 1) + a, 128 * (m - 1) + b) for m in range(1, 5)]
             for m in range(1, 5):
                 tt(eq[m - 1], key[m], KB, Op.is_equal)
-            at = bank(2, a, b)
-            mms(at, (v("oneh", r=1), v("b5" if kind == "S" else "b1", 0, n, r=1)), *[(v("I%s%d" % (kind, m)), eq[m - 1]) for m in range(1, 5)])
-            ts(s("pos", a, b), at, 16.0, Op.mult, v("kc"), Op.add)
+            at, far = bank(kb, 320, 320 + n), bank(CH[0][4], 384 + a, 384 + b)
+            mms(at, (v("c160" if kind == "S" else "oneh", r=1), v("b1", 0, n, r=1)), *[(times(m * (32 if kind == "S" else n)), eq[m - 1]) for m in range(1, 5)])
+            ts(s("pos", a, b), at, 0.5 if kind == "S" else 16.0, Op.mult, v("kc"), Op.add)
             sign = kind == "S" and e == "s"
             win, top = s("A", 80 * a, 80 * b), col("top%d" % h)
 
             def second(f, near, x, y):
                 if kind == "V":
-                    actg(s("NA", 16 * (x - a), 16 * (y - a)), s("D"), f, Act.Abs)
-                    ts(near, s("NA", 16 * (x - a), 16 * (y - a)), top, Op.is_le)
+                    actg(s("NA", 16 * (x - VA), 16 * (y - VA)), win, f, Act.Abs)
+                    ts(near, s("NA", 16 * (x - VA), 16 * (y - VA)), top, Op.is_le)
                 elif sign:
                     actg(near, win, f, Act.Sign, bias=col("toph%d" % h), scale=-1.0)
                 else:
@@ -443,7 +466,9 @@ def rank_program(g, core, T, topo):
             for x in range(a, b, step):
                 y = min(x + step, b)
                 second(s("pos", x, y), s("NR", 16 * x, 16 * y), x, y)
-            mms(bank(3, a, b), const("c24" if sign else "c85", n), *[(place("E24" if sign else "E25", k), s("NR", 16 * a + k, 16 * b - 15 + k, 16)) for k in range(16)])
+            if ci == 0:
+                mms(bank(kb, 192, 320), const("cN", 128), (v("I"), v("F%d%d" % (h, t))))
+            mms(far, const("c24" if sign else "c85", n), *[(place(-(1 << (24 if sign else 25)), k), s("NR", 16 * a + k, 16 * b - 15 + k, 16)) for k in range(16)])
 
         def meeting(gi):
             a, b = GR[gi]
@@ -451,10 +476,8 @@ def rank_program(g, core, T, topo):
             c = n // 2
             q0, q1 = a // 2, b // 2
             ki, fo = "KI%d%d" % (h, t), "FO%d%d" % (h, t)
-            own = bank(3, 128 + a, 128 + b)
-            mms(own, const("cN", n), (v("I"), v("F%d%d" % (h, t), a, b)))
-            tt(s("KF", a, b), bank(3, a, b), s("KS", 5 * a + 4, 5 * b, 5), Op.max)
-            tt(v4(ki, t, a, b), own, s("KF", a, b), Op.min)
+            tt(s("KF", a, b), bank(CH[0][4], 384 + a, 384 + b), s("KS", 5 * a + 4, 5 * b, 5), Op.max)
+            tt(v4(ki, t, a, b), bank(CH[0][4], 192 + a, 192 + b), s("KF", a, b), Op.min)
             for x in range(2):
                 ts(s("SJi", a + x * c, a + x * c + c), v4(ki, t, a, b, x), 2047, Op.bitwise_and)
             ts(s("Hh", a, b), s("SJi", a, b), 0.125, Op.mult, 1279.5625, Op.add)
@@ -468,18 +491,11 @@ def rank_program(g, core, T, topo):
                 return s("EQ2", 8 * a + l * c, 8 * a + (l + x) * c)
             for r in range(2):
                 for l in range(8):
-                    o = bank(r, l * c, l * c + c)
-                    if c < 64:
-                        mms(o, (v("B%d" % (8 * r + l)), HS), (v("In"), HJ))
-                    else:
-                        mms(o, (v("B%d" % (8 * r + l)), HS))
-                if c < 64:
-                    ts(big(8 * r, 8), bank(r, 0, 8 * c), 0.0, Op.is_equal)
-                else:
-                    for l in range(8):
-                        tt(big(8 * r + l), bank(r, l * c, l * c + c), HJ, Op.is_equal)
-            G, LM, XP, MT = (bank(2, 128 + 64 * i, 128 + 64 * i + c) for i in range(4))
-            ML, S32, UJ = (bank(3, 256 + 64 * i, 256 + 64 * i + c) for i in range(3))
+                    mms(bank(2 + r, l * c, l * c + c), (v("B%d" % (8 * r + l)), HS))
+                for l in range(8):
+                    tt(big(8 * r + l), bank(2 + r, l * c, l * c + c), HJ, Op.is_equal)
+            S32, UJ, G, LM, XP = (bank(0, c * i, c * i + c) for i in range(5))
+            ML, SL, MT = bank(1, 0, c), bank(1, c, 2 * c), bank(2, 4 * c, 5 * c)
             mms(S32, const("c32", c), (v("I"), S))
             mms(UJ, (s("W32"), v4(zn, t, a, b, 1)))
             tt(pr("JS"), S32, J, Op.mult)
@@ -487,9 +503,9 @@ def rank_program(g, core, T, topo):
             ts(pr("Jn"), pr("JQ"), 5, Op.logical_shift_right, 2047, Op.bitwise_and)
             mms(G, *[(v("G32"), big(l)) for l in range(16)])
             for l in range(16):
-                mm(ML, v("Q4_%d" % l), big(l), l == 0, False)
+                mm(ML, times(4 ** (15 - l)), big(l), l == 0, False)
             ts(pr("mj"), G, v("p32"), Op.is_ge)
-            mm(ML, v("SHB"), pr("mj"), False, True)
+            mm(ML, times(-2 ** 33, "SH"), pr("mj"), False, True)
             act(pr("wM"), ML, Act.Relu)
             mms(LM, (v("BD"), pr("wM")))
             mms(MT, (v("S15"), pr("mj")))
@@ -498,25 +514,25 @@ def rank_program(g, core, T, topo):
                 x = 4 * t + 2 * h + gi
                 red(v("metc", x, x + 1), MT)
             mms(XP, (v("BN"), pr("mj")), (v("BD"), pr("ms")))
-            JL, JH = bank(0, 320, 320 + c), bank(0, 384, 384 + c)
-            mms(JL, (v("I"), J), (v("IBn"), pr("mj")))
-            mms(JH, (v("I"), J), (v("IB"), pr("mj")))
+            JL, JH = (bank(3, c * i, c * i + c) for i in (5, 6))
+            mms(JL, (v("I"), J), (times(-BIG), pr("mj")))
+            mms(JH, (v("I"), J), (times(BIG), pr("mj")))
             ts(pr("oha"), XP, v("kc"), Op.is_equal)
             ts(pr("ohb"), XP, v("kn"), Op.is_equal)
             tt(pr("t1"), JL, pr("Jn"), Op.max)
             tt(v4(fo, t, a, b, 1), JH, pr("t1"), Op.min)
             for x in range(4):
-                mms(bank(1, x, 4 * c - 3 + x, 4), (v("PA%d" % x), pr("oha")), (v("PA%d" % x), pr("ohb")), (v("Rot%d" % (4 * x) if x else "I"), J))
-            SL, PEN = bank(3, 256, 256 + c), [bank(3, 384 + 64 * x, 384 + 64 * x + c) for x in range(2)]
-            mms(SL, (v("I"), S), (v("IBn"), pr("ms")), (v("NOK"), pr("oha")))
-            for x in range(2):
-                mms(PEN[x], const("cP", c, 2), (v("I32k"), v4("Hs%d%d" % (h, t), t, a, b, x)), (v("BDn"), v4(zn, t, a, b, x)))
-            scan(s("T1", 4 * q0, 4 * q1), v("RS4", 0, 4 * c), bank(1, 0, 4 * c), 0.0, Op.max, Op.min)
+                mms(bank(2, x, 4 * c - 3 + x, 4), (v("PA%d" % x), pr("oha")), (v("PA%d" % x), pr("ohb")), (v("Rot%d" % (4 * x) if x else "I"), J))
+            PEN = [bank(0, c * i, c * i + c) for i in (6, 7)]
+            mms(SL, (v("I"), S), (times(-BIG), pr("ms")), (times(BIG, "NOK"), pr("oha")))
             cp(s("L5", 5 * q0 + 4, 5 * q1, 5), SL)
-            mms(bank(0, 4, 5 * c, 5), (v("I"), S), (v("IB"), pr("ms")), (v("NOKn"), pr("oha")))
+            scan(s("T1", 4 * q0, 4 * q1), v("RS4", 0, 4 * c), bank(2, 0, 4 * c), 0.0, Op.max, Op.min)
+            mms(bank(3, 4, 5 * c, 5), (v("I"), S), (times(BIG), pr("ms")), (times(-BIG, "NOK"), pr("oha")))
             for x in range(4):
-                mms(bank(0, x, 5 * c - 4 + x, 5), (v("PB%d" % x), pr("oha")), (v("PB%d" % x), pr("ohb")), (v("Rot%d" % x if x else "I"), s("T1", 4 * q0 + 3, 4 * q1, 4)))
-            scan(s("T2", 5 * q0, 5 * q1), s("L5", 5 * q0, 5 * q1), bank(0, 0, 5 * c), 0.0, Op.max, Op.min)
+                mms(bank(3, x, 5 * c - 4 + x, 5), (v("PB%d" % x), pr("oha")), (v("PB%d" % x), pr("ohb")), (v("Rot%d" % x if x else "I"), s("T1", 4 * q0 + 3, 4 * q1, 4)))
+            for x in range(2):
+                mms(PEN[x], const("cP", c, 2), (times(32768), v4("Hs%d%d" % (h, t), t, a, b, x)), (times(-2048, "BD"), v4(zn, t, a, b, x)))
+            scan(s("T2", 5 * q0, 5 * q1), s("L5", 5 * q0, 5 * q1), bank(3, 0, 5 * c), 0.0, Op.max, Op.min)
             SN = s("T2", 5 * q0 + 4, 5 * q1, 5)
             tt(v4(fm, t, a, b, 1), PEN[1], v4(fo, t, a, b, 1), Op.min)
             tt(v4(fm, t, a, b, 0), PEN[0], SN, Op.min)
@@ -534,7 +550,7 @@ def rank_program(g, core, T, topo):
                 g.remote_dma(out_ap=land[0], in_ap=src[0], remote_sem=T.sem[sem], local_sem=T.sem["loc"],
                              pid=pid, routing_id=rid, dma_engine_mask=sum(1 << e for e in es))
             me = op("g", call, [], [src], 0.4, "loc", len(es))
-            ops.append(["r", None, WIRE, {me: False}, sem, len(topo.engines(T.cores[(rank - NEXT) % nrank], core)[:8]), phase[0]])
+            ops.append(["r", None, WIRE, {me: False}, sem, len(topo.engines(T.cores[(rank - NEXT) % nrank], core)[:8])])
             mark(land, True, len(ops) - 1)
 
         def store(out, name, lo, gi, sem):
@@ -547,12 +563,12 @@ def rank_program(g, core, T, topo):
             a, b = GR[gi]
             n, c0, c1 = b - a, a // 16, b // 16
             FO, Y, f, zo = v4("FO%d%d" % (h, t), t, a, b), s("Y", a, b), s("Ol", c0, c1), s("Zo", 128 * t + a, 128 * t + b)
-            OL, VN = bank(2, 384 + c0, 384 + c1), bank(1, 256, 256 + n)
+            OL, VN = bank(1, 288, 288 + c1 - c0), bank(2, 0, n)
             w = 2 << t
-            mms(OL, *[(place("E", q), vx(T[fm][:, a // w + q // w:b // w:16 // w, q % w // (w // 2), q % (w // 2)], fm, a, b, n // 16)) for q in range(16)])
+            mms(OL, *[(place(1, q), vx(T[fm][:, a // w + q // w:b // w:16 // w, q % w // (w // 2), q % (w // 2)], fm, a, b, n // 16)) for q in range(16)])
             ts(f, OL, REST, Op.add)
             actg(Y, X, f, Act.Copy)
-            mms(VN, const("cq", n), (v("Ih"), v4(zn, t, a, b)), (v("Ih"), Y))
+            mms(VN, const("cq", n), (times(0.5), v4(zn, t, a, b)), (times(0.5), Y))
             ts(zo, VN, MAGIC, Op.add, -MAGIC, Op.add)
             if t < 3:
                 send(gi, "F", FO)
@@ -564,13 +580,14 @@ def rank_program(g, core, T, topo):
 
         def mining():
             ew = "EQW%d" % h
-            ER, RR, CN, OA, LL = bank(0, 0, 256), bank(1, 0, 256), bank(0, 256, 512), bank(2, 400, 416), bank(2, 416, 432)
+            ER, RR, CN, OA, LL = bank(0, 0, 256), bank(1, 0, 256), bank(0, 256, 512), bank(1, 256, 272), bank(1, 272, 288)
+            ts(s("zq"), v4(zn, t, 0, 128), -0.25, Op.mult, -1279.625, Op.add)
             for j in range(2):
                 mms(bank(0, 128 * j, 128 * j + 128), (v("BD%d" % j), v4(fm, t, 0, 128)))
             ts(s("Er"), ER, REST, Op.add)
-            mms(OA, *[(place("E", q), s("Er", q, 241 + q, 16)) for q in range(16)])
+            mms(OA, *[(place(1, q), s("Er", q, 241 + q, 16)) for q in range(16)])
             for j in range(2):
-                ts(s("OI", 0, 8, r=64 * j + 64, p=64 * j), bank(2, 400 + j, 415 + j, 2, r=64 * j + 64, p=64 * j), 1 / 16, Op.mult)
+                ts(s("OI", 0, 8, r=64 * j + 64, p=64 * j), bank(1, 256 + j, 271 + j, 2, r=64 * j + 64, p=64 * j), 1 / 16, Op.mult)
             ts(s("Ouf"), OA, 1 / 16, Op.mult)
             mm(CN, v("I"), v("THR"), True, False)
             for c in range(8):
@@ -578,24 +595,25 @@ def rank_program(g, core, T, topo):
                 if c < 7:
                     mm(bank(0, 288 + 32 * c, 512), v("BD2"), vx(T[ew][:, c, 32:256 - 32 * c], ew, 256 * c + 32, 256 * c + 256, 224 - 32 * c), False, False)
                 mm(bank(0, 256 + 32 * c, 288 + 32 * c), v("W4D"), vx(T[ew][:, c, 0:32], ew, 256 * c, 256 * c + 32, 32), False, c == 7)
-            act(s("lo"), CN, Act.Sign)
-            mms(LL, (v("I"), v("IO")), const("c16k", 16), *[(place("ES", q), s("lo", q, 241 + q, 16)) for q in range(16)])
             for j in range(2):
                 mms(bank(1, 128 * j, 128 * j + 128), (v("I%d" % j), s("zq")), (v("I%d" % j), s("Y")))
             ts(s("R2"), RR, 1280.0, Op.add, 0.0, Op.max)
+            act(s("lo"), CN, Act.Sign)
+            mms(LL, (v("I"), v("IO")), const("c16k", 16), *[(place(10240, q), s("lo", q, 241 + q, 16)) for q in range(16)])
             tt(s("LO"), LL, s("Ouf"), Op.max)
             cp(s("Ls"), s("LO"))
             XW, ls, r2 = s("X"), s("Ls"), s("R2")
             op("v", lambda: g.vector.tensor_copy(XW[0].indirect(ls[0]), r2[0]), [XW], [ls, r2], 0.05 + 256 * 3.8 * CYC)
 
-        phase[0] = 2 * t + h - (1.5 if t else 0)
-        for a, b in GR:
-            prep(a, b)
+        if lists is not None:
+            prep(*PREP[lists])
+            return
+        if t == 0:
+            for x in range(len(PREP)):
+                visit(t, h, x)
         if t == 0 and h == 0:
-            phase[0] = 9
             key_constants()
             last_constants()
-        phase[0] = 2 * t + h
         if t and not h:
             red(v("mets"), v("metc", 4 * t - 4, 4 * t))
             cp(v("meti"), v("mets"))
@@ -614,10 +632,16 @@ def rank_program(g, core, T, topo):
                     choose(ci)
             meeting(gi)
             veins(gi)
+        if t < 3:
+            visit(t + 1, h, 0)
         mining()
-        if t == 3:
+        if t < 3:
+            for x in range(1, len(PREP)):
+                visit(t + 1, h, x)
+        else:
             src = s("X", 0, 2048, r=64)
             dma("y", T.yx[64 * h:64 * h + 64, :], src[0], [], [src], "oX%d0" % h)
+            due[len(ops) - 1] = 0.0 if h else AHEAD
 
     loads(0)
     loads(1)
@@ -629,56 +653,63 @@ def rank_program(g, core, T, topo):
         for h in range(2):
             visit(t, h)
 
-    succ = [[] for _ in ops]
-    left = [0] * len(ops)
-    for i, o in enumerate(ops):
-        for j in o[3]:
-            succ[j].append(i)
-            left[i] += 1
+    hold = [{"r": 0.0, "y": 0.1}.get(o[0], o[2]) for o in ops]
+    after, before = [[] for _ in ops], [[] for _ in ops]
+    for j, o in enumerate(ops):
+        for i, wait in o[3].items():
+            lag = ops[i][2] + WAKE if wait else (ops[i][2] if o[0] == "r" else hold[i])
+            after[i].append((j, lag))
+            before[j].append((i, lag + hold[j] - hold[i]))
+
+    def fit(key, follow, lead, early):
+        left = [len(x) for x in lead]
+        free = {o[0]: [] for o in ops}
+        ready, at, turn = [(key[i], i) for i in range(len(ops)) if not left[i]], [0.0] * len(ops), []
+        while ready:
+            first = min(ready)
+            ready.remove(first)
+            i = first[1]
+            start, taken = early[i], free[ops[i][0]]
+            x = len(taken)
+            while x and taken[x - 1][0] > start:
+                x -= 1
+            if x and taken[x - 1][1] > start:
+                start = taken[x - 1][1]
+            while x < len(taken) and start + hold[i] > taken[x][0] + 1e-9:
+                start = taken[x][1]
+                x += 1
+            if x and taken[x - 1][1] >= start:
+                taken[x - 1][1] = start + hold[i]
+            else:
+                taken.insert(x, [start, start + hold[i]])
+                x += 1
+            if x < len(taken) and taken[x - 1][1] >= taken[x][0]:
+                taken[x - 1][1] = max(taken[x - 1][1], taken[x][1])
+                del taken[x]
+            at[i] = start
+            turn.append(i)
+            for j, lag in follow[i]:
+                left[j] -= 1
+                early[j] = max(early[j], start + lag)
+                if not left[j]:
+                    ready.append((key[j], j))
+        return at, turn
     way = [0.0] * len(ops)
     for i in range(len(ops) - 1, -1, -1):
-        best = 0.0
-        for j in succ[i]:
-            best = max(best, way[j] + (WAKE if ops[j][3][i] else 0.0))
-        way[i] = best + ops[i][2]
-        for j in succ[i]:
-            ops[i][6] = min(ops[i][6], ops[j][6])
-    free = {o[0]: [] for o in ops}
-    rank_of = {i: x for x, i in enumerate(sorted(range(len(ops)), key=lambda i: (ops[i][6], -way[i], i)))}
-    early, ready, placed = [0.0] * len(ops), [(rank_of[i], i) for i in range(len(ops)) if not left[i]], []
-    while ready:
-        first = min(ready)
-        ready.remove(first)
-        i = first[1]
-        q, start = ops[i][0], early[i]
-        hold = {"r": 0.0, "y": 0.1}.get(q, ops[i][2])
-        taken = free[q]
-        x = len(taken)
-        while x and taken[x - 1][0] > start:
-            x -= 1
-        if x and taken[x - 1][1] > start:
-            start = taken[x - 1][1]
-        while x < len(taken) and start + hold > taken[x][0] + SLACK:
-            start = taken[x][1]
-            x += 1
-        if x and taken[x - 1][1] >= start:
-            taken[x - 1][1] = start + hold
-        else:
-            taken.insert(x, [start, start + hold])
-            x += 1
-        if x < len(taken) and taken[x - 1][1] >= taken[x][0]:
-            taken[x - 1][1] = max(taken[x - 1][1], taken[x][1])
-            del taken[x]
-        placed.append((start, len(placed), i))
-        end = start + ops[i][2]
-        for j in succ[i]:
-            left[j] -= 1
-            early[j] = max(early[j], end + WAKE if ops[j][3][i] else (end if ops[j][0] == "r" else start + hold))
-            if not left[j]:
-                ready.append((rank_of[j], j))
-    order = [i for start, x, i in sorted(placed)]
+        way[i] = max([ops[i][2] + due.get(i, 0.0)] + [lag + way[j] for j, lag in after[i]])
+    at, turn = fit([-x for x in way], after, before, [0.0] * len(ops))
+    best = None
+    for x in range(ROUNDS + 1):
+        end = max(at[i] + ops[i][2] for i in range(len(ops)))
+        if best is None or end < best[0]:
+            best = (end, at, turn)
+        if x < ROUNDS:
+            back, turn = fit([-at[i] - hold[i] for i in range(len(ops))], before, after, [o[2] - hold[i] + due.get(i, 0.0) for i, o in enumerate(ops)])
+            at, turn = fit([-back[i] - hold[i] for i in range(len(ops))], after, before, [0.0] * len(ops))
+    end, at, turn = best
+    order = sorted(turn, key=lambda i: at[i])
 
-    count, know, value, clocks = {}, {q: {} for q in free}, {}, {}
+    count, know, value, clocks = {}, {o[0]: {} for o in ops}, {}, {}
     for i in order:
         q, fn, cost, deps, sem, inc = ops[i][:6]
         k = know[q]

@@ -1,15 +1,13 @@
 from concourse.mybir import dt, AluOpType as Op, AxisListType, ActivationFunctionType as Act
 
 NEXT = 1
-USUAL = [("S", 0, 32, "v", 0), ("S", 32, 64, "v", 3), ("V", 96, 128, "s", 1), ("S", 64, 96, "v", 2)]
-FIRST = [("S", 0, 32, "v", 0), ("V", 96, 128, "s", 1), ("V", 64, 96, "s", 2), ("S", 32, 64, "v", 3)]
-PLAN = {}
-GR = [(0, 128)]
-PREP = [(0, 64), (64, 128)]
-VP, NP = 16, 16
+SPLIT, SPLITS = 96, {(0, 0): 80}
+WIDE = sorted({128 - x for x in [SPLIT] + list(SPLITS.values())})
+PIECES = [(0, 3), (3, 5)]
+PREP = [(64, 128), (0, 64)]
+VP, RP, NP = 8, 32, 16
 SUB = 16
-VA, NV = 64, 64
-WIDE = sorted({ch[2] - ch[1] for chs in [USUAL] + list(PLAN.values()) for ch in chs if ch[0] == "V"})
+VA = 64
 KN = 13 << 20
 BIG = 4096.0
 MAGIC = 1.5 * (1 << 23)
@@ -18,16 +16,16 @@ REST = 2048.0 * 105
 f32, bf, f16, i32, u16 = "float32", "bfloat16", "float16", "int32", "uint16"
 SCRATCH = {}
 PER = {
-    "X": ([128, 2560], bf), "A": ([128, 80 * 128], bf), "RL": ([128, 80 * NV], bf), "Zx": ([128, 16 * NV], bf),
-    "off6": ([128, 768], u16), "offV": ([128, 5 * NV], u16), "c6": ([128, 768], f16), "cV": ([128, 5 * NV], f16),
+    "X": ([128, 2560], bf), "A": ([128, 80 * 128], bf), "RL": ([128, 80 * 64], bf), "Zx": ([128, 1024], bf), "Zy": ([128, 256], bf),
+    "off6": ([128, 768], u16), "offV": ([128, 320], u16), "c16": ([128, 5, 128], f16),
     "P": ([128, 128], f32), "Q": ([128, 640], i32), "C": ([128, 5, 128], i32), "KS": ([128, 640], f32), "EQm": ([128, 512], bf),
-    "NR": ([128, 2048], bf), "NA": ([128, 16 * NV], bf), "EQ2": ([128, 1024], bf), "EQW": ([128, 8, 256], bf),
-    "W2": ([128, 128], bf), "W32": ([128, 128], bf),
+    "NR": ([128, 2048], bf), "NA": ([128, 1024], bf), "EQ2": ([128, 1024], bf), "EQW": ([128, 8, 256], bf),
+    "W2": ([128, 128], bf), "W32": ([128, 128], bf), "Zo": ([128, 128], bf),
 }
 PARTS = {
-    "h16": (f16, [("Hu", 128), ("zq", 128), ("SJ", 128), ("Hh", 128), ("T1", 256), ("T2", 320), ("L5", 320), ("t1", 64), ("Er", 256)]),
-    "b16": (bf, [("mj", 64), ("wM", 64), ("ms", 64), ("oha", 64), ("ohb", 64), ("Y", 128), ("lo", 256), ("R2", 256)]),
-    "w32": (f32, [("KF", 128), ("JS", 64), ("Ouf", 16), ("OI", 16), ("LO", 16), ("yo", 128), ("w2c", 4), ("limf", 4), ("top", 4), ("toph", 4)]),
+    "h16": (f16, [("Hu", 128), ("zq", 128), ("SJ", 128), ("Hh", 128), ("T1", 256), ("T2", 384), ("L6", 384), ("t1", 64), ("Fj", 64), ("Y", 128)]),
+    "b16": (bf, [("mj", 64), ("wM", 64), ("ms", 64), ("oha", 64), ("ohb", 64), ("Z2", 128), ("lo", 256), ("R2", 256)]),
+    "w32": (f32, [("KF", 128), ("JS", 64), ("Ouf", 16), ("OI", 16), ("LO", 16), ("yo", 128), ("w2c", 4), ("limf", 4), ("top", 4)]),
     "n32": (i32, [("fin", 128), ("SJi", 128), ("JQ", 64), ("Jn", 64), ("win", 4), ("lin", 4)]),
     "u16": (u16, [("pos", 128), ("Ol", 16), ("Ls", 16)]),
 }
@@ -42,24 +40,22 @@ for _h in range(2):
             _c += _w
         SCRATCH["%s%d" % (_b, _h)] = ("sbuf", [128, _c], _d)
     for _t in range(4):
-        SCRATCH["F%d%d" % (_h, _t)] = ("sbuf", [128, 128], f16)
-        for _n, _d in (("Z", bf), ("KI", i32), ("FO", f16), ("Hs", f16), ("Fm", f16)):
-            SCRATCH["%s%d%d" % (_n, _h, _t)] = ("sbuf", [128, 64 >> _t, 2, 1 << _t], _d)
-    SCRATCH["Zo%d" % _h] = ("sbuf", [128, 4 * 128], bf)
+        for _n, _d, _w in (("Z", bf, 64), ("KI", i32, 64), ("Hs", f16, 64), ("Er", f16, 128), ("F", f16, 128), ("FO", f16, 128)):
+            SCRATCH["%s%d%d" % (_n, _h, _t)] = ("sbuf", [128, _w >> _t, 2, 1 << _t], _d)
 MATS = ["BD", "I", "BDt", "G32", "SH", "BN", "S15", "NOK", "BD0", "BD1", "I0", "I1", "BD2", "W4D"] + \
     ["B%d" % l for l in range(16)] + ["Rot%d" % d for d in (1, 2, 3, 4, 8, 12)] + \
     ["PA%d" % a for a in range(4)] + ["PB%d" % a for a in range(4)]
-SCRATCH["pool"] = ("sbuf", [128, 144 * 40], bf)
-EARLY = 30
 SCRATCH["mats"] = ("sbuf", [128, 128 * len(MATS)], bf)
 for _i, _n in enumerate(MATS):
     COLS[_n] = ("mats", 128 * _i, 128)
+SCRATCH["pool"] = ("sbuf", [128, 144 * 40], bf)
+EARLY = 30
 CONST = {
-    "cb": (bf, [("one", 256), ("E", 144), ("Et", 144), ("RS5", 320), ("RS4", 256), ("THR", 256),
-                ("d0", 256), ("d1", 256), ("KC", 128), ("MCS", 320), ("cU", 128), ("cS", 128), ("cP", 128), ("cN", 128), ("c85", 128),
-                ("c24", 128), ("c32", 128), ("cq", 128), ("c16k", 128)] + [("MCV%d" % n, 5 * n) for n in WIDE]),
-    "ch": (f16, [("RC", 128), ("RM", 640), ("b1", 64), ("IO", 16), ("oneh", 128), ("c160", 128)]),
-    "cf": (f32, [("io", 32), ("OH", 32), ("PW", 32), ("PT", 32), ("kc", 1), ("kn", 1), ("rc", 1), ("p32", 1), ("p4", 1), ("p4d", 1), ("mets", 1), ("metc", 16), ("sel", 16)]),
+    "cb": (bf, [("one", 256), ("E", 144), ("Et", 144), ("RS5", 320), ("RS4", 256), ("THR", 256), ("d0", 256), ("d1", 256), ("KC", 128), ("MCS", 320),
+                ("cU", 128), ("cS", 128), ("cP", 128), ("cN", 128), ("c85", 128), ("c32", 128), ("c1280", 64), ("c16k", 128)] +
+           [("MCV%d" % n, 5 * n) for n in WIDE]),
+    "ch": (f16, [("RC", 128), ("RM", 640), ("b1", 64), ("IO", 16), ("c160", 128), ("c1", 128)]),
+    "cf": (f32, [("io", 32), ("OH", 32), ("PW", 32), ("PT", 32), ("kc", 1), ("kn", 1), ("rc", 1), ("p32", 1), ("p4", 1), ("p4d", 1), ("mets", 1), ("metc", 8), ("sel", 16)]),
     "ci": (i32, [("pi", 1), ("pk", 1), ("pj", 1), ("meti", 1), ("mete", 1)]),
 }
 for _b, (_d, _ts) in CONST.items():
@@ -73,10 +69,12 @@ BANKS = ["b%d%d" % (h, i) for h in range(2) for i in range(4)]
 for _n in BANKS:
     SCRATCH[_n] = ("psum", [128, 512], f32)
 SEMAPHORES = ["sg", "sv", "ss", "st", "loc"] + ["d%s%d" % (c, h) for c in "ZWFXL" for h in range(2)] + \
-    ["o%s%d%d" % (c, h, i) for c in "FZX" for h in range(2) for i in range(len(GR))] + \
-    ["r%s%d%d%d" % (c, h, t, i) for c in "FZ" for h in range(2) for t in (1, 2, 3) for i in range(len(GR))]
+    ["o%s%d" % (c, h) for c in "FZX" for h in range(2)] + ["r%s%d%d" % (c, h, t) for c in "FZ" for h in range(2) for t in (1, 2, 3)]
 
-CYC, TCYC, GATH, WAKE, WIRE = 0.85e-3, 0.43e-3, 1.56, 0.21, 3.0
+CYC, TCYC, GATH, WAKE, WIRE = 0.85e-3, 0.46e-3, 1.56, 0.21, 2.6
+GATH2 = 1.56
+SLACK = 0.04
+SOON = 0.0
 ROUNDS, AHEAD = 3, 12.0
 
 
@@ -145,14 +143,14 @@ def rank_program(g, core, T, topo):
     def col(name):
         return v(name, 0, 1)
 
-    def vx(ap, name, lo, hi, n):
-        return (ap, name, lo, hi, n, (0, 128), (1, 0))
+    def vx(ap, name, lo, hi, n, part=(1, 0)):
+        return (ap, name, lo, hi, n, (0, 128), part)
 
-    def v4(name, t, a, b, which=None, r=128, p=0):
+    def v4(name, t, a=0, b=128, which=None, r=128, p=0):
         w = 2 << t
         if which is None:
             return (T[name][p:r, a // w:b // w, :, :], name, a, b, b - a, (p, r), (1, 0))
-        return (T[name][:, a // w:b // w, which, :], name, a, b, (b - a) // 2, (0, 128), ("pair", which))
+        return vx(T[name][:, a // w:b // w, which, :], name, a, b, (b - a) // 2, ("pair", which))
 
     def vcost(o, *ins):
         two = all(x[1] not in BANKS and SCRATCH[x[1]][2] in (bf, f16, u16) for x in (o,) + ins[:1])
@@ -199,17 +197,20 @@ def rank_program(g, core, T, topo):
         return (v(name, 0, 128, r=r), v("one", 0, n, r=r))
 
     def act(o, a, func, **kw):
-        ins = [a] + [x for x in kw.values() if isinstance(x, tuple)]
-        kw = {k: x[0] if isinstance(x, tuple) else x for k, x in kw.items()}
-        op("s", lambda: g.scalar.activation(o[0], a[0], func, **kw), [o], ins, max(64, o[4]) * CYC)
+        op("s", lambda: g.scalar.activation(o[0], a[0], func, **kw), [o], [a], max(64, o[4]) * CYC)
 
-    def actg(o, win, f, func, **kw):
-        ins = [win, f] + [x for x in kw.values() if isinstance(x, tuple)]
-        kw = {k: x[0] if isinstance(x, tuple) else x for k, x in kw.items()}
-        op("s", lambda: g.scalar.activation(o[0], win[0].indirect(f[0]), func, **kw), [o], ins, 0.065 + o[4] * GATH * CYC)
+    def actg(o, win, f, func, z=None):
+        cost = 0.065 + o[4] * GATH * CYC
+        if z is None:
+            op("s", lambda: g.scalar.activation(o[0], win[0].indirect(f[0]), func), [o], [win, f], cost)
+        else:
+            op("s", lambda: g.scalar.activation(o[0], win[0].indirect(f[0]), func, bias=z[0], scale=-1.0), [o], [win, f, z], cost)
 
     def asel(o, a, pat, cop, base, cm):
         op("g", lambda: g.affine_select(o[0], a[0], pat, cop, 0.0, base, cm), [o], [a], 0.17 + 2 * o[4] * CYC)
+
+    def gcp(o, a):
+        asel(o, a, [[0, o[4]]], Op.is_gt, 1, 0)
 
     def iota(o, pat, base, cm, small=True):
         if small:
@@ -217,9 +218,8 @@ def rank_program(g, core, T, topo):
         else:
             op("g", lambda: g.iota(o[0], pat, base, cm), [o], [], 0.13 + 2 * o[4] * CYC)
 
-    def dma(q, o, a, outs, ins, sem):
-        e = eng[q]
-        op("y" if q == "y" else q, lambda: e.dma_start(o, a), outs, ins, 2.0, sem, 16)
+    def dma(o, a, outs, ins, sem):
+        op("y", lambda: g.sync.dma_start(o, a), outs, ins, 2.0, sem, 16)
 
     def times(x, name="I", lo=0):
         if x == 1:
@@ -237,26 +237,27 @@ def rank_program(g, core, T, topo):
     def place(x, k):
         return times(x, "E", 15 - k)
 
-    closed, last, pool, due = {}, [], {}, {}
+    closed, last, pool, due, soon = {}, [], {}, {}, {}
 
     def loads(h):
         rows = slice(64 * h, 64 * h + 64)
         for j in range(2):
             z = v4("Z%d0" % h, 0, 0, 128, None, 64 * j + 64, 64 * j)
-            dma("y", z[0], T.vein[rows, 128 * j:128 * j + 128], [z], [], "dZ%d" % h)
+            dma(z[0], T.vein[rows, 128 * j:128 * j + 128], [z], [], "dZ%d" % h)
         for name, src, sem in (("win", T.w, "dW"), ("fin", T.front, "dF"), ("X", T.rock, "dX"), ("lin", T.lim, "dL")):
             for j in range(2):
                 wide = {"fin": 128, "X": 2048}.get(name, 1)
                 o = v("%s%d" % (name, h), 0, wide, r=64 * j + 64, p=64 * j)
-                dma("y", o[0], src[rows, 128 * j:128 * j + 128] if name == "fin" else src[rows, :], [o], [], "%s%d" % (sem, h))
+                dma(o[0], src[rows, 128 * j:128 * j + 128] if name == "fin" else src[rows, :], [o], [], "%s%d" % (sem, h))
 
-    def first_constants():
+    def list_constants():
         fill(v("one"), 1.0)
         iota(v("pi"), [[0, 1]], 0, 1, False)
         asel(v("BDt"), v("one", 0, 128), [[-16, 8], [0, 16]], Op.is_ge, 0, 1)
         asel(v("BD"), v("BDt"), [[16, 8], [0, 16]], Op.is_ge, 15, -1)
         asel(v("I"), v("one", 0, 128), [[-1, 128]], Op.is_equal, 0, 1)
         iota(v("RC", r=2), [[0, 8], [37, 16]], 0, 0)
+        fill(v("cS", r=2), -16 * 1280.0)
         iota(v("cS", r=1), [[0, 8], [-1, 16]], 16, 0)
         for m in range(5):
             fill(v("RM", 128 * m, 128 * m + 128, r=2), float(32 << m))
@@ -268,15 +269,14 @@ def rank_program(g, core, T, topo):
         cp(v("kc"), v("pk"))
 
     def stream_constants(h):
-        cp(v("F%d0" % h), v("fin%d" % h))
+        cp(v4("F%d0" % h, 0), v("fin%d" % h))
         ts(col("w2c%d" % h), col("win%d" % h), 2.0, Op.mult)
         ts(v("W2%d" % h), v("BD"), col("w2c%d" % h), Op.mult)
         ts(v("W32%d" % h), v("W2%d" % h), 16.0, Op.mult)
-        fill(v("off6%d" % h, 5, 768, 6), 0)
         cp(col("limf%d" % h), col("lin%d" % h))
         fill(v("X%d" % h, 2048, 2560), 0.0)
-        fill(v("L5%d" % h), -1.0)
-        fill(v("L5%d" % h, 0, 320, 5), 4 * BIG)
+        fill(v("L6%d" % h), -1.0)
+        fill(v("L6%d" % h, 0, 384, 6), 4 * BIG)
 
     def key_constants():
         fill(v("E"), 0.0)
@@ -289,20 +289,19 @@ def rank_program(g, core, T, topo):
         for n in WIDE:
             iota(v("MCV%d" % n, r=2), [[1, 5], [0, n]], 0, 0)
             fill(v("MCV%d" % n, r=1), 4096.0)
+        fill(v("c1", r=1), 1.0)
         fill(v("RS5"), -float(1 << 25))
         fill(v("RS5", 0, 320, 5), float(KN))
         iota(v("b1", r=1), [[1, 64]], 0, 0)
-        fill(v("oneh", r=1), 1.0)
         fill(v("c160", r=1), 160.0)
         fill(v("c85", r=1), 8.5 * (1 << 25))
-        fill(v("c24", r=1), float(1 << 24))
         fill(v("cN", r=1), float(KN))
 
     def pick(name, row):
         tt(v("PT", 0, row[4]), row, v("OH", 0, row[4]), Op.mult)
         red(v(name), v("PT", 0, row[4]))
 
-    def last_constants():
+    def meeting_constants():
         iota(v("io"), [[1, 32]], 0, 0)
         ts(v("OH", 0, 16), v("io", 0, 16), v("kc"), Op.is_equal)
         for l in range(16):
@@ -330,14 +329,16 @@ def rank_program(g, core, T, topo):
                 ts(v("%s%d" % (name, a)), v("BD"), v("sel", 8 + s, 9 + s), Op.mult)
         fill(v("RS4"), -1.0)
         fill(v("RS4", 0, 256, 4), 4 * BIG)
-        fill(v("cq", r=1), -0.25)
+
+    def mining_constants():
+        fill(v("c1280"), -1280.0)
         fill(v("cP", r=2), -1280.0 * 32768)
         ts(v("cP", r=1), v("cS", r=1), -2048.0, Op.mult, 2048.0, Op.add)
-        for name, src in (("BD", "BD"), ("I", "I")):
+        for name in ("BD", "I"):
             for j in range(2):
                 fill(v("%s%d" % (name, j), r=128 - 64 * j, p=64 - 64 * j), 0.0)
                 for x in range(2):
-                    cp(v("%s%d" % (name, j), 64 * x, 64 * x + 64, r=64 * j + 64, p=64 * j), v(src, 64 * j, 64 * j + 64, r=64 * j + 64, p=64 * j))
+                    cp(v("%s%d" % (name, j), 64 * x, 64 * x + 64, r=64 * j + 64, p=64 * j), v(name, 64 * j, 64 * j + 64, r=64 * j + 64, p=64 * j))
         tt(v("BD2"), v("BD0"), v("BD1"), Op.add)
         fill(v("d0"), 0.25)
         fill(v("d0", 0, 256, 32), 0.0)
@@ -358,240 +359,231 @@ def rank_program(g, core, T, topo):
         def s(name, *a, **k):
             return v("%s%d" % (name, h), *a, **k)
 
+        def s4(name, a=0, b=128, which=None):
+            return v4("%s%d%d" % (name, h, t), t, a, b, which)
+
         def bank(i, lo, hi, st=1, **k):
             return v("b%d%d" % (h, i), lo, hi, st, **k)
-        X, zn, fm = s("X", 0, 2048), "Z%d%d" % (h, t), "Fm%d%d" % (h, t)
-        CH = PLAN.get((t, h), USUAL)
+
+        def five(name, a, b, m=None):
+            name = "%s%d" % (name, h)
+            if m is None:
+                return vx(T[name][:, :, a:b], name, 0, 640, 5 * (b - a), ("half", a // 64))
+            return vx(T[name][:, m, a:b], name, 128 * m + a, 128 * m + b, b - a, ("half", a // 64))
+
+        X, w = s("X", 0, 2048), 2 << t
+        sv = SPLITS.get((t, h), SPLIT)
+        chunks = [(64, sv, 0), (sv, 128, 1), (0, 32, 3), (32, 64, 2)]
 
         def prep(a, b):
             n = b - a
-            F, Z = v("F%d%d" % (h, t), a, b), v4(zn, t, a, b)
+            F, Z = s4("F", a, b), s4("F", 128 + a, 128 + b) if t else s4("Z", a, b)
+            if t and not lists:
+                ts(s4("Z"), s4("F", 128, 256), -1280.0, Op.add)
+            top = [(s("W2"), v("c1280", 0, n))] if t else []
             U, S, V = bank(2, 0, n), bank(2, n, 2 * n), bank(2, 2 * n, 3 * n)
-            mms(U, (s("W2"), Z), const("one", n))
-            mms(S, (v("BD"), Z), const("cS", n))
+            mms(U, const("one", n), *top, (s("W2"), Z))
+            mms(S, const("cS", n, 2 if t else 1), (v("BD"), Z))
             ts(s("Hu", a, b), U, 1 / 4096, Op.mult, 1279.5, Op.add)
             R = [bank(3, m * n, m * n + n) if m < 4 else bank(2, 3 * n, 4 * n) for m in range(5)]
             for m in range(4):
                 mms(R[m], (v("RC", r=2), v("RM", 128 * m, 128 * m + n, r=2)), (times(32 << m), F))
-            ts(v4("Hs%d%d" % (h, t), t, a, b), S, 1 / 16, Op.mult, 1280 - 15 / 32, Op.add)
-            mms(V, (s("W2"), Z), const("cU", n, 2), (times(-4096), s("Hu", a, b)))
+            ts(s4("Hs", a, b), S, 1 / 16, Op.mult, 1280 - 15 / 32, Op.add)
+            mms(V, (s("W2"), Z), *top, const("cU", n, 2), (times(-4096), s("Hu", a, b)))
             mms(R[4], (v("RC", r=2), v("RM", 512, 512 + n, r=2)), (times(512), F))
             tt(s("P", a, b), V, F, Op.mult)
-            cn = "C%d" % h
             for m in range(5):
                 q = s("Q", 128 * m + a, 128 * m + b)
                 tt(q, R[m], s("P", a, b), Op.add)
-                ts(vx(T[cn][:, m, a:b], cn, 128 * m + a, 128 * m + b, n), q, 5 + m, Op.logical_shift_right, 2047, Op.bitwise_and)
-            for kind in "SV":
-                mine = sorted(ch[1:3] for ch in CH if ch[0] == kind and a <= ch[1] < b)
-                if not mine:
-                    continue
-                lo, hi = mine[0][0], mine[-1][1]
-                if kind == "S":
-                    for m in range(5):
-                        cp(s("off6", 6 * lo + m, 6 * hi - 5 + m, 6), vx(T[cn][:, m, lo:hi], cn, 128 * m + lo, 128 * m + hi, hi - lo))
-                    cp(s("c6", 6 * lo, 6 * hi), s("off6", 6 * lo, 6 * hi))
-                    continue
-                for x, y in mine:
-                    cp(s("offV", 5 * (x - VA), 5 * (y - VA)), vx(T[cn][:, :, x:y], cn, x, 512 + y, 5 * (y - x)))
-                cp(s("cV", 5 * (lo - VA), 5 * (hi - VA)), s("offV", 5 * (lo - VA), 5 * (hi - VA)))
-                for k in range(16):
-                    asel(s("Zx", 16 * (lo - VA) + k, 16 * (hi - VA) - 15 + k, 16), v4(zn, t, lo, hi), [[0, hi - lo]], Op.is_gt, 1, 0)
-
-        def gather(ch):
-            kind, a, b = ch[:3]
-            w = 2 << t
-            if kind == "S":
-                for i in range(a, b):
-                    z = vx(T[zn][:, i // w, i % w // (w // 2), i % (w // 2):i % (w // 2) + 1], zn, i, i + 1, 1)
-                    actg(s("A", 80 * i, 80 * i + 80), X, s("off6", 6 * i, 6 * i + 5), Act.Abs, bias=z, scale=-1.0)
-                    if last:
-                        ops[-1][3].setdefault(last[0], False)
-                    last[:] = [len(ops) - 1]
-                return
+                ts(five("C", a, b, m), q, 5 + m, Op.logical_shift_right, 2047, Op.bitwise_and)
+            gcp(five("c16", a, b), five("C", a, b))
+            hi = min(b, sv)
             for m in range(5):
-                def one(o, f, z):
-                    op("v", lambda: g.vector.tensor_tensor(o[0], X[0].indirect(f[0]), z[0], Op.subtract), [o], [X, f, z], 0.05 + o[4] * GATH * CYC)
-                n, c = b - a, a - VA
-                for x in range(0, n, VP):
-                    y = min(x + VP, n)
-                    d = s("A", 80 * a + 16 * (n * m + x), 80 * a + 16 * (n * m + y))
-                    one(d, s("offV", 5 * c + m * n + x, 5 * c + m * n + y), s("Zx", 16 * (c + x), 16 * (c + y)))
-                    ts(s("RL", 80 * c + 16 * (n * m + x), 80 * c + 16 * (n * m + y)), d, 0.0, Op.max)
+                (gcp if lists else cp)(s("off6", 6 * a + m, 6 * hi - 5 + m, 6), five("C", a, hi, m))
+            if hi < b:
+                cp(s("offV", 0, 5 * (b - hi)), five("C", hi, b))
+                lo = hi // 16 * 16
+                for k in range(4):
+                    gcp(s("Zy", 4 * (lo - VA) + k, 4 * (b - VA) - 3 + k, 4), s4("Z", lo, b))
+                for k in range(4):
+                    gcp(s("Zx", 16 * (hi - VA) + k, 16 * (b - VA) - 3 + k, 4), s("Zy", 4 * (hi - VA), 4 * (b - VA)))
 
-        def choose(ci):
-            kind, a, b, e, kb = CH[ci]
-            n = b - a
+        def gather(a, b):
+            zn = "Z%d%d" % (h, t)
+            for i in range(a, min(b, sv)):
+                z = vx(T[zn][:, i // w, i % w // (w // 2), i % (w // 2):i % (w // 2) + 1], zn, i, i + 1, 1)
+                actg(s("A", 80 * i, 80 * i + 80), X, s("off6", 6 * i, 6 * i + 5), Act.Abs, z)
+                if last:
+                    ops[-1][3].setdefault(last[0], False)
+                last[:] = [len(ops) - 1]
+
+            def one(o, f, z):
+                op("v", lambda: g.vector.tensor_tensor(o[0], X[0].indirect(f[0]), z[0], Op.subtract), [o], [X, f, z], 0.05 + o[4] * GATH2 * CYC)
+            n = b - sv
+            for m in range(5 if n > 0 else 0):
+                for x in range(m * n, m * n + n, VP):
+                    one(s("A", 80 * a + 16 * x, 80 * a + 16 * (x + VP)), s("offV", x, x + VP), s("Zx", 16 * (a - VA + x % n), 16 * (a - VA + x % n + VP)))
+                for x in range(m * n, m * n + n, RP):
+                    y = min(x + RP, m * n + n)
+                    ts(s("RL", 16 * x, 16 * y), s("A", 80 * a + 16 * x, 80 * a + 16 * y), 0.0, Op.max)
+
+        def choose(a, b, kb):
+            n, own = b - a, a < sv
             keys = bank(kb, 0, 5 * n)
-            key = [bank(kb, m, 5 * n - 4 + m, 5) if kind == "S" else bank(kb, m * n, m * n + n) for m in range(5)]
-            mm(keys, v("KC", r=2), v("MCS" if kind == "S" else "MCV%d" % n, 0, 5 * n, r=2), True, False)
-            if kind == "S":
+            key = [bank(kb, m, 5 * n - 4 + m, 5) if own else bank(kb, m * n, m * n + n) for m in range(5)]
+            mm(keys, v("KC", r=2), v("MCS" if own else "MCV%d" % n, 0, 5 * n, r=2), True, False)
+            if own:
                 for m in range(5):
-                    mm(key[m], v("I"), s("c6", 6 * a + m, 6 * b - 5 + m, 6), False, False)
+                    mm(key[m], v("I"), five("c16", a, b, m), False, False)
                 for p in range(a, b, SUB):
-                    w = min(SUB, b - p)
+                    q = min(p + SUB, b)
                     for k in range(16):
-                        mm(bank(kb, 5 * (p - a), 5 * (p - a + w)), place(10240, k), s("A", 80 * p + k, 80 * (p + w) - 15 + k, 16), False, k == 15 and p + w == b)
+                        mm(bank(kb, 5 * (p - a), 5 * (q - a)), place(10240, k), s("A", 80 * p + k, 80 * q - 15 + k, 16), False, k == 15 and q == b)
                 scan(s("KS", 5 * a, 5 * b), v("RS5", 0, 5 * n), keys, 0.0, Op.max, Op.min)
             else:
-                for x, src, c in ((-10240, "A", a), (20480, "RL", a - VA)):
-                    for k in range(16):
-                        mm(keys, place(x, k), s(src, 80 * c + k, 80 * (c + n) - 15 + k, 16), False, False)
-                mm(keys, v("I"), s("cV", 5 * (a - VA), 5 * (b - VA)), False, True)
-                for m in range(5):
-                    o = s("KS", 5 * a + m, 5 * b - 4 + m, 5)
-                    if m == 0:
-                        ts(o, key[0], float(KN), Op.min)
-                    else:
-                        tt(o, key[m], s("KS", 5 * a + m - 1, 5 * b - 5 + m, 5), Op.min)
-            KB = s("KS", 5 * a + 4, 5 * b, 5)
+                for m0, m1 in PIECES:
+                    for x, src, c in ((-10240, "A", 80 * a), (20480, "RL", 0)):
+                        for k in range(16):
+                            mm(bank(kb, m0 * n, m1 * n), place(x, k), s(src, c + 16 * n * m0 + k, c + 16 * n * m1 - 15 + k, 16), False, False)
+                mm(keys, v("I"), five("c16", a, b), False, True)
+                least = [s("KS", 5 * a + m, 5 * b - 4 + m, 5) for m in range(5)]
+                ts(least[0], key[0], float(KN), Op.min)
+                for m in range(1, 5):
+                    tt(least[m], key[m], least[m - 1], Op.min)
             eq = [s("EQm", 128 * (m - 1) + a, 128 * (m - 1) + b) for m in range(1, 5)]
             for m in range(1, 5):
-                tt(eq[m - 1], key[m], KB, Op.is_equal)
-            at, far = bank(kb, 320, 320 + n), bank(CH[0][4], 384 + a, 384 + b)
-            mms(at, (v("c160" if kind == "S" else "oneh", r=1), v("b1", 0, n, r=1)), *[(times(m * (32 if kind == "S" else n)), eq[m - 1]) for m in range(1, 5)])
-            ts(s("pos", a, b), at, 0.5 if kind == "S" else 16.0, Op.mult, v("kc"), Op.add)
-            sign = kind == "S" and e == "s"
+                tt(eq[m - 1], key[m], s("KS", 5 * a + 4, 5 * b, 5), Op.is_equal)
+            at = bank(kb, 328, 328 + n)
+            mms(at, (v("c160" if own else "c1", r=1), v("b1", 0, n, r=1)), *[(times(m * (32 if own else n)), eq[m - 1]) for m in range(1, 5)])
+            ts(s("pos", a, b), at, 0.5 if own else 16.0, Op.mult, v("kc"), Op.add)
             win, top = s("A", 80 * a, 80 * b), col("top%d" % h)
 
-            def second(f, near, x, y):
-                if kind == "V":
-                    actg(s("NA", 16 * (x - VA), 16 * (y - VA)), win, f, Act.Abs)
-                    ts(near, s("NA", 16 * (x - VA), 16 * (y - VA)), top, Op.is_le)
-                elif sign:
-                    actg(near, win, f, Act.Sign, bias=col("toph%d" % h), scale=-1.0)
-                else:
-                    op("v", lambda: g.vector.tensor_scalar(near[0], win[0].indirect(f[0]), top[0], None, Op.is_le), [near], [win, f, top], 0.05 + near[4] * GATH * CYC)
-            step = NP if e == "v" and kind == "S" else n
-            for x in range(a, b, step):
-                y = min(x + step, b)
-                second(s("pos", x, y), s("NR", 16 * x, 16 * y), x, y)
-            if ci == 0:
-                mms(bank(kb, 192, 320), const("cN", 128), (v("I"), v("F%d%d" % (h, t))))
-            mms(far, const("c24" if sign else "c85", n), *[(place(-(1 << (24 if sign else 25)), k), s("NR", 16 * a + k, 16 * b - 15 + k, 16)) for k in range(16)])
+            def second(f, near):
+                op("v", lambda: g.vector.tensor_scalar(near[0], win[0].indirect(f[0]), top[0], None, Op.is_le), [near], [win, f, top], 0.05 + near[4] * GATH * CYC)
+            if own:
+                for x in range(a, b, NP):
+                    y = min(x + NP, b)
+                    second(s("pos", x, y), s("NR", 16 * x, 16 * y))
+            else:
+                actg(s("NA", 0, 16 * n), win, s("pos", a, b), Act.Abs)
+                ts(s("NR", 16 * a, 16 * b), s("NA", 0, 16 * n), top, Op.is_le)
+            if kb == 0:
+                mms(bank(0, 200, 328), const("cN", 128), (v("I"), s4("F")))
+            mms(bank(0, 384 + a, 384 + b), const("c85", n), *[(place(-(1 << 25), k), s("NR", 16 * a + k, 16 * b - 15 + k, 16)) for k in range(16)])
 
-        def meeting(gi):
-            a, b = GR[gi]
-            n = b - a
-            c = n // 2
-            q0, q1 = a // 2, b // 2
-            ki, fo = "KI%d%d" % (h, t), "FO%d%d" % (h, t)
-            tt(s("KF", a, b), bank(CH[0][4], 384 + a, 384 + b), s("KS", 5 * a + 4, 5 * b, 5), Op.max)
-            tt(v4(ki, t, a, b), bank(CH[0][4], 192 + a, 192 + b), s("KF", a, b), Op.min)
+        def meeting():
+            c = 64
+            tt(s("KF"), bank(0, 384, 512), s("KS", 4, 640, 5), Op.max)
+            tt(s4("KI"), bank(0, 200, 328), s("KF"), Op.min)
             for x in range(2):
-                ts(s("SJi", a + x * c, a + x * c + c), v4(ki, t, a, b, x), 2047, Op.bitwise_and)
-            ts(s("Hh", a, b), s("SJi", a, b), 0.125, Op.mult, 1279.5625, Op.add)
-            cp(s("SJ", a, b), s("SJi", a, b))
-            S, J, HS, HJ = s("SJ", a, a + c), s("SJ", a + c, b), s("Hh", a, a + c), s("Hh", a + c, b)
-
-            def pr(name):
-                return s(name, q0, q1)
-
-            def big(l, x=1):
-                return s("EQ2", 8 * a + l * c, 8 * a + (l + x) * c)
+                ts(s("SJi", x * c, x * c + c), s4("KI", which=x), 2047, Op.bitwise_and)
+            ts(s("Hh"), s("SJi"), 0.125, Op.mult, 1279.5625, Op.add)
+            gcp(s("SJ"), s("SJi"))
+            S, J, HS, HJ = s("SJ", 0, c), s("SJ", c, 2 * c), s("Hh", 0, c), s("Hh", c, 2 * c)
+            eq = [s("EQ2", l * c, l * c + c) for l in range(16)]
             for r in range(2):
                 for l in range(8):
                     mms(bank(2 + r, l * c, l * c + c), (v("B%d" % (8 * r + l)), HS))
                 for l in range(8):
-                    tt(big(8 * r + l), bank(2 + r, l * c, l * c + c), HJ, Op.is_equal)
-            S32, UJ, G, LM, XP = (bank(0, c * i, c * i + c) for i in range(5))
+                    tt(eq[8 * r + l], bank(2 + r, l * c, l * c + c), HJ, Op.is_equal)
+            G, LM, XP = (bank(0, c * i, c * i + c) for i in range(3))
             ML, SL, MT = bank(1, 0, c), bank(1, c, 2 * c), bank(2, 4 * c, 5 * c)
+            S32, UJ, JL, JH = (bank(3, c * i, c * i + c) for i in (0, 1, 6, 7))
             mms(S32, const("c32", c), (v("I"), S))
-            mms(UJ, (s("W32"), v4(zn, t, a, b, 1)))
-            tt(pr("JS"), S32, J, Op.mult)
-            tt(pr("JQ"), UJ, pr("JS"), Op.add)
-            ts(pr("Jn"), pr("JQ"), 5, Op.logical_shift_right, 2047, Op.bitwise_and)
-            mms(G, *[(v("G32"), big(l)) for l in range(16)])
+            mms(UJ, (s("W32"), s4("Z", which=1)))
+            tt(s("JS"), S32, J, Op.mult)
+            tt(s("JQ"), UJ, s("JS"), Op.add)
+            ts(s("Jn"), s("JQ"), 5, Op.logical_shift_right, 2047, Op.bitwise_and)
+            mms(G, *[(v("G32"), eq[l]) for l in range(16)])
             for l in range(16):
-                mm(ML, times(4 ** (15 - l)), big(l), l == 0, False)
-            ts(pr("mj"), G, v("p32"), Op.is_ge)
-            mm(ML, times(-2 ** 33, "SH"), pr("mj"), False, True)
-            act(pr("wM"), ML, Act.Relu)
-            mms(LM, (v("BD"), pr("wM")))
-            mms(MT, (v("S15"), pr("mj")))
-            ts(pr("ms"), LM, v("p4"), Op.is_ge)
+                mm(ML, times(4 ** (15 - l)), eq[l], l == 0, False)
+            ts(s("mj"), G, v("p32"), Op.is_ge)
+            mm(ML, times(-2 ** 33, "SH"), s("mj"), False, True)
+            act(s("wM"), ML, Act.Relu)
+            mms(LM, (v("BD"), s("wM")))
+            ts(s("ms"), LM, v("p4"), Op.is_ge)
             if t < 3:
-                x = 4 * t + 2 * h + gi
-                red(v("metc", x, x + 1), MT)
-            mms(XP, (v("BN"), pr("mj")), (v("BD"), pr("ms")))
-            JL, JH = (bank(3, c * i, c * i + c) for i in (5, 6))
-            mms(JL, (v("I"), J), (times(-BIG), pr("mj")))
-            mms(JH, (v("I"), J), (times(BIG), pr("mj")))
-            ts(pr("oha"), XP, v("kc"), Op.is_equal)
-            ts(pr("ohb"), XP, v("kn"), Op.is_equal)
-            tt(pr("t1"), JL, pr("Jn"), Op.max)
-            tt(v4(fo, t, a, b, 1), JH, pr("t1"), Op.min)
+                mms(MT, (v("S15"), s("mj")))
+                red(v("metc", 2 * t + h, 2 * t + h + 1), MT)
+            mms(XP, (v("BN"), s("mj")), (v("BD"), s("ms")))
+            mms(JL, (v("I"), J), (times(-BIG), s("mj")))
+            mms(JH, (v("I"), J), (times(BIG), s("mj")))
+            ts(s("oha"), XP, v("kc"), Op.is_equal)
+            ts(s("ohb"), XP, v("kn"), Op.is_equal)
+            tt(s("t1"), JL, s("Jn"), Op.max)
+            tt(s4("FO", which=1), JH, s("t1"), Op.min)
             for x in range(4):
-                mms(bank(2, x, 4 * c - 3 + x, 4), (v("PA%d" % x), pr("oha")), (v("PA%d" % x), pr("ohb")), (v("Rot%d" % (4 * x) if x else "I"), J))
-            PEN = [bank(0, c * i, c * i + c) for i in (6, 7)]
-            mms(SL, (v("I"), S), (times(-BIG), pr("ms")), (times(BIG, "NOK"), pr("oha")))
-            cp(s("L5", 5 * q0 + 4, 5 * q1, 5), SL)
-            scan(s("T1", 4 * q0, 4 * q1), v("RS4", 0, 4 * c), bank(2, 0, 4 * c), 0.0, Op.max, Op.min)
-            mms(bank(3, 4, 5 * c, 5), (v("I"), S), (times(BIG), pr("ms")), (times(-BIG, "NOK"), pr("oha")))
-            for x in range(4):
-                mms(bank(3, x, 5 * c - 4 + x, 5), (v("PB%d" % x), pr("oha")), (v("PB%d" % x), pr("ohb")), (v("Rot%d" % x if x else "I"), s("T1", 4 * q0 + 3, 4 * q1, 4)))
+                mms(bank(2, x, 4 * c - 3 + x, 4), (v("PA%d" % x), s("oha")), (v("PA%d" % x), s("ohb")), (v("Rot%d" % (4 * x) if x else "I"), J))
+            mms(SL, (v("I"), S), (times(-BIG), s("ms")), (times(BIG, "NOK"), s("oha")))
+            cp(s("L6", 4, 6 * c, 6), SL)
+            scan(s("T1"), v("RS4"), bank(2, 0, 4 * c), 0.0, Op.max, Op.min)
+            mms(bank(3, 4, 6 * c - 1, 6), (v("I"), S), (times(BIG), s("ms")), (times(-BIG, "NOK"), s("oha")))
+            PEN = [bank(3, 5, 6 * c, 6), bank(0, 6 * c, 7 * c)]
             for x in range(2):
-                mms(PEN[x], const("cP", c, 2), (times(32768), v4("Hs%d%d" % (h, t), t, a, b, x)), (times(-2048, "BD"), v4(zn, t, a, b, x)))
-            scan(s("T2", 5 * q0, 5 * q1), s("L5", 5 * q0, 5 * q1), bank(3, 0, 5 * c), 0.0, Op.max, Op.min)
-            SN = s("T2", 5 * q0 + 4, 5 * q1, 5)
-            tt(v4(fm, t, a, b, 1), PEN[1], v4(fo, t, a, b, 1), Op.min)
-            tt(v4(fm, t, a, b, 0), PEN[0], SN, Op.min)
-            cp(v4(fo, t, a, b, 0), SN)
+                mms(PEN[x], const("cP", c, 2), (times(32768), s4("Hs", which=x)), (times(-2048, "BD"), s4("Z", which=x)))
+            for x in range(4):
+                mms(bank(3, x, 6 * c - 5 + x, 6), (v("PB%d" % x), s("oha")), (v("PB%d" % x), s("ohb")), (v("Rot%d" % x if x else "I"), s("T1", 3, 4 * c, 4)))
+            tt(s("Fj"), PEN[1], s4("FO", which=1), Op.min)
+            scan(s("T2"), s("L6"), bank(3, 0, 6 * c), 0.0, Op.max, Op.min)
+            gcp(s4("FO", which=0), s("T2", 4, 6 * c, 6))
 
-        def send(gi, what, src):
+        def send(what, a):
             dst = T.cores[(rank + NEXT) % nrank]
             rid, pid = topo.addr(dst, core)
             es = topo.engines(core, dst)[:8]
-            a, b = GR[gi]
-            sem, name = "r%s%d%d%d" % (what, h, t + 1, gi), "%s%d%d" % (what, h, t + 1)
-            land = v(name, a, b) if what == "F" else v4(name, t + 1, a, b)
+            name = "%s%d%d" % (what, h, t + 1)
+            src, land = s4("FO", a, a + 128), v4("F%d%d" % (h, t + 1), t + 1, a, a + 128)
 
             def call():
-                g.remote_dma(out_ap=land[0], in_ap=src[0], remote_sem=T.sem[sem], local_sem=T.sem["loc"],
+                g.remote_dma(out_ap=land[0], in_ap=src[0], remote_sem=T.sem["r" + name], local_sem=T.sem["loc"],
                              pid=pid, routing_id=rid, dma_engine_mask=sum(1 << e for e in es))
             me = op("g", call, [], [src], 0.4, "loc", len(es))
-            ops.append(["r", None, WIRE, {me: False}, sem, len(topo.engines(T.cores[(rank - NEXT) % nrank], core)[:8])])
+            ops.append(["r", None, WIRE, {me: False}, "r" + name, len(topo.engines(T.cores[(rank - NEXT) % nrank], core)[:8])])
             mark(land, True, len(ops) - 1)
 
-        def store(out, name, lo, gi, sem):
-            a, b = GR[gi]
+        def store(out, name, sem):
             for j in range(2):
-                src = s(name, lo + a, lo + b, r=64 * j + 64, p=64 * j)
-                dma("y", out[64 * h:64 * h + 64, 128 * j + a:128 * j + b], src[0], [], [src], "%s%d%d" % (sem, h, gi))
+                src = s(name, r=64 * j + 64, p=64 * j)
+                dma(out[64 * h:64 * h + 64, 128 * j:128 * j + 128], src[0], [], [src], "%s%d" % (sem, h))
 
-        def veins(gi):
-            a, b = GR[gi]
-            n, c0, c1 = b - a, a // 16, b // 16
-            FO, Y, f, zo = v4("FO%d%d" % (h, t), t, a, b), s("Y", a, b), s("Ol", c0, c1), s("Zo", 128 * t + a, 128 * t + b)
-            OL, VN = bank(1, 288, 288 + c1 - c0), bank(2, 0, n)
-            w = 2 << t
-            mms(OL, *[(place(1, q), vx(T[fm][:, a // w + q // w:b // w:16 // w, q % w // (w // 2), q % (w // 2)], fm, a, b, n // 16)) for q in range(16)])
-            ts(f, OL, REST, Op.add)
-            actg(Y, X, f, Act.Copy)
-            mms(VN, const("cq", n), (times(0.5), v4(zn, t, a, b)), (times(0.5), Y))
-            ts(zo, VN, MAGIC, Op.add, -MAGIC, Op.add)
+        def veins():
+            OL = bank(1, 288, 296)
+            terms = []
+            for q in sorted(range(16), key=lambda q: -(q % w // (w // 2))):
+                pair = q // w * (w // 2) + q % (w // 2)
+                terms.append((place(1, q), s("Fj", pair, 64, 8) if q % w // (w // 2) else s("T2", 6 * pair + 5, 384, 48)))
+            mms(OL, *terms)
+            ts(s("Ol", 0, 8), OL, REST, Op.add)
+            y, f, z = s("Y"), s("Ol", 0, 8), s("Z2")
+            gcp(z, s4("Z"))
+            op("v", lambda: g.vector.tensor_tensor(y[0], X[0].indirect(f[0]), z[0], Op.add), [y], [X, f, z], 0.05 + 128 * GATH2 * CYC)
+            ts(s4("FO", 128, 256), y, 0.5, Op.mult, 1279.75, Op.add)
             if t < 3:
-                send(gi, "F", FO)
-                send(gi, "Z", zo)
+                send("F", 0)
+                send("Z", 128)
             else:
-                cp(s("yo", a, b), FO)
-                store(T.yf, "yo", 0, gi, "oF")
-                store(T.yz, "Zo", 384, gi, "oZ")
+                ts(s("Zo"), s4("FO", 128, 256), -1280.0, Op.add)
+                gcp(s("yo"), s4("FO"))
+                store(T.yf, "yo", "oF")
+                store(T.yz, "Zo", "oZ")
 
         def mining():
             ew = "EQW%d" % h
-            ER, RR, CN, OA, LL = bank(0, 0, 256), bank(1, 0, 256), bank(0, 256, 512), bank(1, 256, 272), bank(1, 272, 288)
-            ts(s("zq"), v4(zn, t, 0, 128), -0.25, Op.mult, -1279.625, Op.add)
-            for j in range(2):
-                mms(bank(0, 128 * j, 128 * j + 128), (v("BD%d" % j), v4(fm, t, 0, 128)))
-            ts(s("Er"), ER, REST, Op.add)
-            mms(OA, *[(place(1, q), s("Er", q, 241 + q, 16)) for q in range(16)])
+            RR, CN, OA, LL = bank(1, 0, 256), bank(0, 256, 512), bank(1, 256, 272), bank(1, 272, 288)
+            er = "Er%d%d" % (h, t)
+            ts(s("zq"), s4("Z"), -1.25, Op.mult, -1279.625, Op.add)
+            for x, src in ((1, s("Fj")), (0, s("T2", 5, 384, 6))):
+                for j in range(2):
+                    mms(bank(0, 128 * x + 64 * j, 128 * x + 64 * j + 64), (v("BD%d" % j), src))
+            for x in range(2):
+                ts(s4("Er", 0, 256, x), bank(0, 128 * x, 128 * x + 128), REST, Op.add)
+            mms(OA, *[(place(1, q), vx(T[er][:, q // w::16 // w, q % w // (w // 2), q % (w // 2)], er, 0, 256, 16)) for q in range(16)])
             for j in range(2):
                 ts(s("OI", 0, 8, r=64 * j + 64, p=64 * j), bank(1, 256 + j, 271 + j, 2, r=64 * j + 64, p=64 * j), 1 / 16, Op.mult)
             ts(s("Ouf"), OA, 1 / 16, Op.mult)
             mm(CN, v("I"), v("THR"), True, False)
             for c in range(8):
-                ts(vx(T[ew][:, c, 0:256 - 32 * c], ew, 256 * c, 256 * c + 256 - 32 * c, 256 - 32 * c), s("Er", 32 * c, 256), s("OI", c, c + 1), Op.is_equal)
+                ts(vx(T[ew][:, c, 0:256 - 32 * c], ew, 256 * c, 256 * c + 256 - 32 * c, 256 - 32 * c), s4("Er", 32 * c, 256), s("OI", c, c + 1), Op.is_equal)
                 if c < 7:
                     mm(bank(0, 288 + 32 * c, 512), v("BD2"), vx(T[ew][:, c, 32:256 - 32 * c], ew, 256 * c + 32, 256 * c + 256, 224 - 32 * c), False, False)
                 mm(bank(0, 256 + 32 * c, 288 + 32 * c), v("W4D"), vx(T[ew][:, c, 0:32], ew, 256 * c, 256 * c + 32, 32), False, c == 7)
@@ -603,50 +595,44 @@ def rank_program(g, core, T, topo):
             tt(s("LO"), LL, s("Ouf"), Op.max)
             cp(s("Ls"), s("LO"))
             XW, ls, r2 = s("X"), s("Ls"), s("R2")
-            op("v", lambda: g.vector.tensor_copy(XW[0].indirect(ls[0]), r2[0]), [XW], [ls, r2], 0.05 + 256 * 3.8 * CYC)
+            soon[op("v", lambda: g.vector.tensor_copy(XW[0].indirect(ls[0]), r2[0]), [XW], [ls, r2], 0.05 + 256 * 3.8 * CYC)] = SOON if t < 3 else 0.0
 
         if lists is not None:
             prep(*PREP[lists])
             return
         if t == 0:
-            for x in range(len(PREP)):
-                visit(t, h, x)
-        if t == 0 and h == 0:
-            key_constants()
-            last_constants()
-        if t and not h:
-            red(v("mets"), v("metc", 4 * t - 4, 4 * t))
-            cp(v("meti"), v("mets"))
-            ts(v("mete"), v("meti"), 3, Op.bitwise_and)
-        if t:
-            tt(col("top%d" % h), col("limf%d" % h), v("mete"), Op.add)
-        else:
+            visit(t, h, 0)
+            visit(t, h, 1)
+            if h == 0:
+                key_constants()
+                meeting_constants()
+                mining_constants()
             cp(col("top%d" % h), col("limf%d" % h))
-        if any(ch[0] == "S" and ch[3] == "s" for ch in CH):
-            ts(col("toph%d" % h), col("top%d" % h), 0.5, Op.add)
-        for ch in CH:
-            gather(ch)
-        for gi, (a, b) in enumerate(GR):
-            for ci, ch in enumerate(CH):
-                if a <= ch[1] < b:
-                    choose(ci)
-            meeting(gi)
-            veins(gi)
+        else:
+            if h == 0:
+                red(v("mets"), v("metc", 2 * t - 2, 2 * t))
+                cp(v("meti"), v("mets"))
+                ts(v("mete"), v("meti"), 3, Op.bitwise_and)
+            tt(col("top%d" % h), col("limf%d" % h), v("mete"), Op.add)
+        for a, b, kb in chunks:
+            gather(a, b)
+        for ch in chunks:
+            choose(*ch)
+        meeting()
+        veins()
         if t < 3:
             visit(t + 1, h, 0)
         mining()
         if t < 3:
-            for x in range(1, len(PREP)):
-                visit(t + 1, h, x)
+            visit(t + 1, h, 1)
         else:
             src = s("X", 0, 2048, r=64)
-            dma("y", T.yx[64 * h:64 * h + 64, :], src[0], [], [src], "oX%d0" % h)
+            dma(T.yx[64 * h:64 * h + 64, :], src[0], [], [src], "oX%d" % h)
             due[len(ops) - 1] = 0.0 if h else AHEAD
 
     loads(0)
     loads(1)
-    first_constants()
-    fill(v("metc"), 0.0)
+    list_constants()
     for h in range(2):
         stream_constants(h)
     for t in range(4):
@@ -657,7 +643,7 @@ def rank_program(g, core, T, topo):
     after, before = [[] for _ in ops], [[] for _ in ops]
     for j, o in enumerate(ops):
         for i, wait in o[3].items():
-            lag = ops[i][2] + WAKE if wait else (ops[i][2] if o[0] == "r" else hold[i])
+            lag = ops[i][2] + WAKE + soon.get(i, 0.0) if wait else (ops[i][2] if o[0] == "r" else hold[i])
             after[i].append((j, lag))
             before[j].append((i, lag + hold[j] - hold[i]))
 
@@ -675,7 +661,7 @@ def rank_program(g, core, T, topo):
                 x -= 1
             if x and taken[x - 1][1] > start:
                 start = taken[x - 1][1]
-            while x < len(taken) and start + hold[i] > taken[x][0] + 1e-9:
+            while x < len(taken) and start + hold[i] > taken[x][0] + SLACK:
                 start = taken[x][1]
                 x += 1
             if x and taken[x - 1][1] >= start:
@@ -711,13 +697,13 @@ def rank_program(g, core, T, topo):
 
     count, know, value, clocks = {}, {o[0]: {} for o in ops}, {}, {}
     for i in order:
-        q, fn, cost, deps, sem, inc = ops[i][:6]
+        q, call, cost, deps, sem, inc = ops[i]
         k = know[q]
-        best = {}
+        latest = {}
         for j, wait in deps.items():
-            if wait and (ops[j][4] not in best or value[best[ops[j][4]]] < value[j]):
-                best[ops[j][4]] = j
-        for j in sorted(best.values(), key=lambda j: -len(clocks[j])):
+            if wait and (ops[j][4] not in latest or value[latest[ops[j][4]]] < value[j]):
+                latest[ops[j][4]] = j
+        for j in sorted(latest.values(), key=lambda j: -len(clocks[j])):
             if k.get(ops[j][4], 0) < value[j]:
                 eng[q].wait_ge(T.sem[ops[j][4]], value[j])
                 for x, y in clocks[j].items():
@@ -726,7 +712,7 @@ def rank_program(g, core, T, topo):
         count[sem] = value[i] = count.get(sem, 0) + inc
         clocks[i] = {sem: value[i]}
         if q != "r":
-            r = fn()
+            r = call()
             if r is not None:
                 r.then_inc(T.sem[sem], inc)
             clocks[i] = dict(k)

@@ -1,13 +1,17 @@
 from concourse.mybir import dt, AluOpType as Op, AxisListType, ActivationFunctionType as Act
 
 NEXT = 1
-SPLIT, SPLITS = 96, {(0, 0): 80}
-WIDE = sorted({128 - x for x in [SPLIT] + list(SPLITS.values())})
+SPLIT, SPLITS = 44, {(0, 0): 48, (3, 1): 54}
+WIDE = sorted({SPLIT} | set(SPLITS.values()))
 PIECES = [(0, 3), (3, 5)]
-PREP = [(64, 128), (0, 64)]
-VP, RP, NP = 8, 32, 16
-SUB = 16
-VA = 64
+PREP = [(0, 64), (64, 128)]
+LAST = 24
+VP, RP, NP, NS = (2, 2, 2, 2, 2), 22, 24, 64
+SUB = 13
+BYS = 52
+R2S, OVG, JOIN, FREE = 4, 2, 1, []
+BYSCALAR = []
+BS, MSS, MSG = 0, 0, 0
 KN = 13 << 20
 BIG = 4096.0
 MAGIC = 1.5 * (1 << 23)
@@ -16,17 +20,17 @@ REST = 2048.0 * 105
 f32, bf, f16, i32, u16 = "float32", "bfloat16", "float16", "int32", "uint16"
 SCRATCH = {}
 PER = {
-    "X": ([128, 2560], bf), "A": ([128, 80 * 128], bf), "RL": ([128, 80 * 64], bf), "Zx": ([128, 1024], bf), "Zy": ([128, 256], bf),
-    "off6": ([128, 768], u16), "offV": ([128, 320], u16), "c16": ([128, 5, 128], f16),
-    "P": ([128, 128], f32), "Q": ([128, 640], i32), "C": ([128, 5, 128], i32), "KS": ([128, 640], f32), "EQm": ([128, 512], bf),
+    "X": ([128, 2304], bf), "A": ([128, 80 * 128], bf), "RL": ([128, 80 * 64], bf), "Zx": ([128, 1024], bf), "Zy": ([128, 256], bf),
+    "off6": ([128, 768], u16), "offV": ([128, 320], u16), "c16": ([128, 128, 6], f16),
+    "P": ([128, 128], f32), "Q": ([128, 640], i32), "C": ([128, 768], i32), "KS": ([128, 640], i32), "EQm": ([128, 512], bf),
     "NR": ([128, 2048], bf), "NA": ([128, 1024], bf), "EQ2": ([128, 1024], bf), "EQW": ([128, 8, 256], bf),
-    "W2": ([128, 128], bf), "W32": ([128, 128], bf), "Zo": ([128, 128], bf),
+    "W2": ([128, 128], bf), "W32": ([128, 128], bf), "Zo": ([128, 128], bf), "LW": ([128, 1184], f32),
 }
 PARTS = {
-    "h16": (f16, [("Hu", 128), ("zq", 128), ("SJ", 128), ("Hh", 128), ("T1", 256), ("T2", 384), ("L6", 384), ("t1", 64), ("Fj", 64), ("Y", 128)]),
-    "b16": (bf, [("mj", 64), ("wM", 64), ("ms", 64), ("oha", 64), ("ohb", 64), ("Z2", 128), ("lo", 256), ("R2", 256)]),
-    "w32": (f32, [("KF", 128), ("JS", 64), ("Ouf", 16), ("OI", 16), ("LO", 16), ("yo", 128), ("w2c", 4), ("limf", 4), ("top", 4)]),
-    "n32": (i32, [("fin", 128), ("SJi", 128), ("JQ", 64), ("Jn", 64), ("win", 4), ("lin", 4)]),
+    "h16": (f16, [("Hu", 128), ("zq", 128), ("SJ", 128), ("Hh", 128), ("T1", 256), ("T2", 384), ("t1", 64), ("Fj", 64), ("Y", 128), ("Of", 8)]),
+    "b16": (bf, [("mj", 64), ("ms", 64), ("oha", 64), ("ohb", 64), ("Z2", 128), ("R2", 256)]),
+    "w32": (f32, [("JS", 64), ("LO", 48), ("yo", 128), ("w2c", 4), ("limf", 4), ("top", 4)]),
+    "n32": (i32, [("Cc", 128), ("fin", 128), ("SJi", 128), ("JQ", 64), ("Jn", 64), ("win", 4), ("lin", 4)]),
     "u16": (u16, [("pos", 128), ("Ol", 16), ("Ls", 16)]),
 }
 COLS = {}
@@ -42,20 +46,20 @@ for _h in range(2):
     for _t in range(4):
         for _n, _d, _w in (("Z", bf, 64), ("KI", i32, 64), ("Hs", f16, 64), ("Er", f16, 128), ("F", f16, 128), ("FO", f16, 128)):
             SCRATCH["%s%d%d" % (_n, _h, _t)] = ("sbuf", [128, _w >> _t, 2, 1 << _t], _d)
-MATS = ["BD", "I", "BDt", "G32", "SH", "BN", "S15", "NOK", "BD0", "BD1", "I0", "I1", "BD2", "W4D"] + \
-    ["B%d" % l for l in range(16)] + ["Rot%d" % d for d in (1, 2, 3, 4, 8, 12)] + \
-    ["PA%d" % a for a in range(4)] + ["PB%d" % a for a in range(4)]
+MATS = ["BD", "I", "BDt", "TRI", "BN", "S15", "NOK", "BD2", "BD0", "BD1", "I0", "I1", "I00", "I01", "I10", "I11", "W4D"] + \
+    ["%s%d" % (x, l) for x in ("B", "MS") for l in range(16)] + ["Rot%d" % d for d in (1, 2, 3, 4, 8, 12)] + \
+    ["%s%d" % (x, a) for x in ("PA", "PB", "PN") for a in range(4)] + ["BDN"]
 SCRATCH["mats"] = ("sbuf", [128, 128 * len(MATS)], bf)
 for _i, _n in enumerate(MATS):
     COLS[_n] = ("mats", 128 * _i, 128)
-SCRATCH["pool"] = ("sbuf", [128, 144 * 40], bf)
+SCRATCH["pool"] = ("sbuf", [128, 144 * 30], bf)
 EARLY = 30
 CONST = {
-    "cb": (bf, [("one", 256), ("E", 144), ("Et", 144), ("RS5", 320), ("RS4", 256), ("THR", 256), ("d0", 256), ("d1", 256), ("KC", 128), ("MCS", 320),
-                ("cU", 128), ("cS", 128), ("cP", 128), ("cN", 128), ("c85", 128), ("c32", 128), ("c1280", 64), ("c16k", 128)] +
+    "cb": (bf, [("one", 256), ("E", 144), ("Et", 144), ("RS5", 320), ("RS4", 256), ("RS6", 384), ("cBIG", 128), ("THR", 32), ("THM", 256), ("RS16", 256), ("RSL", 48), ("d0", 32), ("d1", 32), ("KC", 128), ("MCS", 320),
+                ("cU", 128), ("cS", 128), ("cP", 128), ("c2k", 128), ("c34k", 128), ("c32", 128), ("c1280", 128)] +
            [("MCV%d" % n, 5 * n) for n in WIDE]),
-    "ch": (f16, [("RC", 128), ("RM", 640), ("b1", 64), ("IO", 16), ("c160", 128), ("c1", 128)]),
-    "cf": (f32, [("io", 32), ("OH", 32), ("PW", 32), ("PT", 32), ("kc", 1), ("kn", 1), ("rc", 1), ("p32", 1), ("p4", 1), ("p4d", 1), ("mets", 1), ("metc", 8), ("sel", 16)]),
+    "ch": (f16, [("RC", 128), ("RM", 640), ("b1", 64), ("c160", 128), ("c1", 128)]),
+    "cf": (f32, [("io", 32), ("OH", 32), ("PW", 32), ("PT", 32), ("kc", 1), ("ks0", 1), ("ks1", 1), ("kn", 1), ("km", 1), ("rc", 1), ("p512", 1), ("p4d", 1), ("mets", 1), ("metc", 8), ("sel", 8)]),
     "ci": (i32, [("pi", 1), ("pk", 1), ("pj", 1), ("meti", 1), ("mete", 1)]),
 }
 for _b, (_d, _ts) in CONST.items():
@@ -64,18 +68,24 @@ for _b, (_d, _ts) in CONST.items():
         COLS[_n] = (_b, _c, _w)
         _c += _w
     SCRATCH[_b] = ("sbuf", [128, _c], _d)
-SCRATCH["RW"] = ("sbuf", [128, 8, 32], bf)
+SCRATCH["RW"] = SCRATCH["RX"] = ("sbuf", [128, 8, 32], bf)
 BANKS = ["b%d%d" % (h, i) for h in range(2) for i in range(4)]
 for _n in BANKS:
     SCRATCH[_n] = ("psum", [128, 512], f32)
-SEMAPHORES = ["sg", "sv", "ss", "st", "loc"] + ["d%s%d" % (c, h) for c in "ZWFXL" for h in range(2)] + \
+HALVES = [("BD2", "BD", [0, 1], [0, 1])] + [("%s%d" % (n, j), n, [j], [0, 1]) for n in ("BD", "I") for j in range(2)] + \
+    [("I%d%d" % (j, x), "I", [j], [x]) for j in range(2) for x in range(2)]
+SEMAPHORES = ["sg", "sv", "ss", "st", "loc"] + ["d" + x[0] for x in HALVES] + ["d%s%d" % (c, h) for c in "ZWFXL" for h in range(2)] + \
     ["o%s%d" % (c, h) for c in "FZX" for h in range(2)] + ["r%s%d%d" % (c, h, t) for c in "FZ" for h in range(2) for t in (1, 2, 3)]
 
 CYC, TCYC, GATH, WAKE, WIRE = 0.85e-3, 0.46e-3, 1.56, 0.21, 2.6
-GATH2 = 1.56
+CASES = [(GATH, 1, WAKE, WIRE, {}), (1.1, 1, 0.15, 2.0, {"t": 0.9, "g": 0.8}), (2.05, 1, 0.17, 2.2, {"t": 1.1}),
+         (1.3, 1, 0.33, 3.5, {"g": 1.1}), (1.75, 1, 0.14, 1.8, {"g": 0.87})]
+GSLOW = 1.0
 SLACK = 0.04
+ROUNDS, AHEAD = 4, 4.0
 SOON = 0.0
-ROUNDS, AHEAD = 3, 12.0
+TRIES, STRETCH, SHAKE, SEED, WORSE = 200, 12.0, (0.2, 0.7, 2.0), 1, 0.03
+ORDER = []
 
 
 def rank_program(g, core, T, topo):
@@ -184,10 +194,9 @@ def rank_program(g, core, T, topo):
 
     def mm(o, l, r, start, stop):
         me = op("t", lambda: g.tensor.matmul(o[0], l[0], r[0], start, stop), [o], [l, r], max(64, r[4]) * TCYC)
-        if start and o[1] in closed:
-            ops[me][3].setdefault(closed[o[1]], False)
-        if stop:
-            closed[o[1]] = me
+        for i in group.get(o[1], ()) if start or stop else ():
+            ops[me][3].setdefault(i, False)
+        group[o[1]] = [me] if start or stop else group[o[1]] + [me]
 
     def mms(o, *terms):
         for i, (l, r) in enumerate(terms):
@@ -199,15 +208,30 @@ def rank_program(g, core, T, topo):
     def act(o, a, func, **kw):
         op("s", lambda: g.scalar.activation(o[0], a[0], func, **kw), [o], [a], max(64, o[4]) * CYC)
 
+    def line(who, o, a, x, y):
+        if who not in BYSCALAR:
+            return ts(o, a, x, Op.mult, y, Op.add)
+        ins, bias = ([a, y], y[0]) if isinstance(y, tuple) else ([a], y)
+        op("s", lambda: g.scalar.activation(o[0], a[0], Act.Identity, bias=bias, scale=x), [o], ins, max(64, o[4]) * CYC)
+
+    def scaled(o, a, x):
+        op("s", lambda: g.scalar.activation(o[0], a[0], Act.Copy, scale=x[0]), [o], [a, x], max(64, o[4]) * CYC)
+
+    def relu(o, a, y):
+        op("s", lambda: g.scalar.activation(o[0], a[0], Act.Relu, bias=y[0]), [o], [a, y], max(64, o[4]) * CYC)
+
     def actg(o, win, f, func, z=None):
-        cost = 0.065 + o[4] * GATH * CYC
+        cost, picks[len(ops)] = 0.065 + o[4] * GATH * CYC, o[4]
         if z is None:
             op("s", lambda: g.scalar.activation(o[0], win[0].indirect(f[0]), func), [o], [win, f], cost)
         else:
             op("s", lambda: g.scalar.activation(o[0], win[0].indirect(f[0]), func, bias=z[0], scale=-1.0), [o], [win, f, z], cost)
 
+    def vgather(call, o, ins):
+        picks[op("v", call, [o], ins, 0.05 + o[4] * GATH * CYC)] = o[4]
+
     def asel(o, a, pat, cop, base, cm):
-        op("g", lambda: g.affine_select(o[0], a[0], pat, cop, 0.0, base, cm), [o], [a], 0.17 + 2 * o[4] * CYC)
+        op("g", lambda: g.affine_select(o[0], a[0], pat, cop, 0.0, base, cm), [o], [a], GSLOW * (0.17 + 2 * o[4] * CYC))
 
     def gcp(o, a):
         asel(o, a, [[0, o[4]]], Op.is_gt, 1, 0)
@@ -237,7 +261,18 @@ def rank_program(g, core, T, topo):
     def place(x, k):
         return times(x, "E", 15 - k)
 
-    closed, last, pool, due, soon = {}, [], {}, {}, {}
+    def turn(d):
+        return v("Rot%d" % d if d else "I")
+
+    def half(j):
+        return {"p": 64 * j, "r": 64 * j + 64}
+
+    def inturn():
+        if last:
+            ops[-1][3].setdefault(last[0], False)
+        last[:] = [len(ops) - 1]
+
+    group, last, pool, due, picks = {}, [], {}, {}, {}
 
     def loads(h):
         rows = slice(64 * h, 64 * h + 64)
@@ -257,7 +292,6 @@ def rank_program(g, core, T, topo):
         asel(v("BD"), v("BDt"), [[16, 8], [0, 16]], Op.is_ge, 15, -1)
         asel(v("I"), v("one", 0, 128), [[-1, 128]], Op.is_equal, 0, 1)
         iota(v("RC", r=2), [[0, 8], [37, 16]], 0, 0)
-        fill(v("cS", r=2), -16 * 1280.0)
         iota(v("cS", r=1), [[0, 8], [-1, 16]], 16, 0)
         for m in range(5):
             fill(v("RM", 128 * m, 128 * m + 128, r=2), float(32 << m))
@@ -267,16 +301,17 @@ def rank_program(g, core, T, topo):
         fill(v("cU", r=1), 1280.0 * 4096)
         ts(v("pk"), v("pi"), 15, Op.bitwise_and)
         cp(v("kc"), v("pk"))
+        for x in range(2):
+            ts(v("ks%d" % x), v("pk"), -1 / 16, Op.mult, 1281 - 15 / 32 - 1280 * x, Op.add)
 
     def stream_constants(h):
         cp(v4("F%d0" % h, 0), v("fin%d" % h))
         ts(col("w2c%d" % h), col("win%d" % h), 2.0, Op.mult)
         ts(v("W2%d" % h), v("BD"), col("w2c%d" % h), Op.mult)
         ts(v("W32%d" % h), v("W2%d" % h), 16.0, Op.mult)
-        cp(col("limf%d" % h), col("lin%d" % h))
-        fill(v("X%d" % h, 2048, 2560), 0.0)
-        fill(v("L6%d" % h), -1.0)
-        fill(v("L6%d" % h, 0, 384, 6), 4 * BIG)
+        ts(col("limf%d" % h), col("lin%d" % h), 0.5, Op.add)
+        fill(v("X%d" % h, 2048, 2304), 0.0)
+        fill(v("C%d" % h, 5, 768, 6), 0)
 
     def key_constants():
         fill(v("E"), 0.0)
@@ -294,8 +329,8 @@ def rank_program(g, core, T, topo):
         fill(v("RS5", 0, 320, 5), float(KN))
         iota(v("b1", r=1), [[1, 64]], 0, 0)
         fill(v("c160", r=1), 160.0)
-        fill(v("c85", r=1), 8.5 * (1 << 25))
-        fill(v("cN", r=1), float(KN))
+        fill(v("c2k", r=1), 2048.0)
+        fill(v("c34k", r=1), 2048.0 * 17)
 
     def pick(name, row):
         tt(v("PT", 0, row[4]), row, v("OH", 0, row[4]), Op.mult)
@@ -305,55 +340,84 @@ def rank_program(g, core, T, topo):
         iota(v("io"), [[1, 32]], 0, 0)
         ts(v("OH", 0, 16), v("io", 0, 16), v("kc"), Op.is_equal)
         for l in range(16):
-            asel(v("B%d" % l), v("one", 0, 128), [[-16, 8], [0, 16]], Op.is_equal, -l, 1)
-        for name, first, x in (("p32", 2.0 ** 80, 1 / 32), ("p4", 2.0 ** 34, 0.25)):
-            fill(v("d0", 0, 16), x)
-            fill(v("d1", 0, 16), 0.0)
-            scan(v("PW", 0, 16), v("d0", 0, 16), v("d1", 0, 16), first, Op.mult, Op.add)
-            pick(name, v("PW", 0, 16))
-        ts(v("G32"), v("BD"), v("p32"), Op.mult)
-        asel(v("SH"), v("BD"), [[-1, 128]], Op.is_equal, 1, 1)
+            if l < BS:
+                scaled(v("B%d" % l), v("BD"), v("OH", l, l + 1))
+            else:
+                asel(v("B%d" % l), v("one", 0, 128), [[-16, 8], [0, 16]], Op.is_equal, -l, 1)
+        fill(v("d0", 0, 16), 1 / 512)
+        fill(v("d1", 0, 16), 0.0)
+        scan(v("PW", 0, 16), v("d0", 0, 16), v("d1", 0, 16), 2.0 ** 73, Op.mult, Op.add)
+        pick("p512", v("PW", 0, 16))
+        for x, f in enumerate((-1.0, 16.0)):
+            ts(vx(T.RX[:, :, 16 * x:16 * x + 16], "RX", 0, 256, 128), v("BD"), v("p512"), Op.mult, f, Op.mult)
+        for l in range(16):
+            o, a = v("MS%d" % l), vx(T.RX[:, :, 15 - l:31 - l], "RX", 0, 256, 128)
+            if l < MSS:
+                act(o, a, Act.Copy)
+            elif l < MSG:
+                gcp(o, a)
+            else:
+                cp(o, a)
+        asel(v("TRI"), v("BD"), [[1, 128]], Op.is_ge, 0, -1)
         ts(v("S15"), v("one", 0, 128), v("OH", 15, 16), Op.mult)
-        tt(v("BN"), v("B15"), v("BD"), Op.subtract)
+        ts(v("PT", 0, 1), v("OH", 15, 16), -1.0, Op.add)
+        ts(v("BN"), v("BD"), v("PT", 0, 1), Op.mult)
         ts(v("kn"), v("kc"), -16.0, Op.add)
+        ts(v("km"), v("kc"), -32.0, Op.add)
         fill(v("c32", r=1), 32.0)
         asel(v("NOK"), v("BD"), [[-16, 8], [1, 16]], Op.is_gt, -15, 1)
         for x in range(2):
             cp(vx(T.RW[:, :, 16 * x:16 * x + 16], "RW", 0, 256, 128), v("I"))
         for d in (1, 2, 3, 4, 8, 12):
-            cp(v("Rot%d" % d), vx(T.RW[:, :, d:d + 16], "RW", 0, 256, 128))
+            cp(turn(d), vx(T.RW[:, :, d:d + 16], "RW", 0, 256, 128))
+        tt(v("BDN"), times(BIG, "BD"), times(BIG, "NOK"), Op.add)
+        for x, f in enumerate((Op.logical_shift_right, Op.bitwise_and)):
+            ts(v("pj"), v("pk"), 2 + x, f)
+            cp(v("rc"), v("pj"))
+            ts(v("sel", 4 * x, 4 * x + 4), v("io", 0, 4), v("rc"), Op.is_equal, -BIG, Op.mult)
         for a in range(4):
-            for name, cols, s in (("PA", v("OH", 4 * a, 4 * a + 4), a), ("PB", v("OH", a, 16, 4), 4 + a)):
-                red(v("sel", s, s + 1), cols)
-                ts(v("sel", 8 + s, 9 + s), v("sel", s, s + 1), -BIG, Op.mult, BIG, Op.add)
-                ts(v("%s%d" % (name, a)), v("BD"), v("sel", 8 + s, 9 + s), Op.mult)
-        fill(v("RS4"), -1.0)
-        fill(v("RS4", 0, 256, 4), 4 * BIG)
+            for name, src, s in (("PA", times(BIG, "BD"), a), ("PB", times(BIG, "BD"), 4 + a), ("PN", v("BDN"), 4 + a)):
+                if name in BYSCALAR:
+                    relu(v("%s%d" % (name, a)), src, v("sel", s, s + 1))
+                    due[len(ops) - 1] = SOON
+                else:
+                    ts(v("%s%d" % (name, a)), src, v("sel", s, s + 1), Op.add, 0.0, Op.max)
+        fill(v("cBIG", r=1), BIG)
+        for name, n in (("RS4", 4), ("RS6", 6)):
+            fill(v(name), -1.0)
+            fill(v(name, 0, 64 * n, n), 4 * BIG)
 
     def mining_constants():
         fill(v("c1280"), -1280.0)
         fill(v("cP", r=2), -1280.0 * 32768)
         ts(v("cP", r=1), v("cS", r=1), -2048.0, Op.mult, 2048.0, Op.add)
-        for name in ("BD", "I"):
-            for j in range(2):
-                fill(v("%s%d" % (name, j), r=128 - 64 * j, p=64 - 64 * j), 0.0)
-                for x in range(2):
-                    cp(v("%s%d" % (name, j), 64 * x, 64 * x + 64, r=64 * j + 64, p=64 * j), v(name, 64 * j, 64 * j + 64, r=64 * j + 64, p=64 * j))
-        tt(v("BD2"), v("BD0"), v("BD1"), Op.add)
+        fill(v("mats", COLS["BD0"][1], COLS["I11"][1] + 128), 0.0)
+        for name, src, froms, tos in HALVES:
+            for j in froms:
+                for x in tos:
+                    o, a = v(name, 64 * x, 64 * x + 64, **half(j)), v(src, 64 * j, 64 * j + 64, **half(j))
+                    dma(o[0], a[0], [o], [a], "d" + name)
         fill(v("d0"), 0.25)
-        fill(v("d0", 0, 256, 32), 0.0)
         fill(v("d1"), 0.0)
-        fill(v("d1", 0, 256, 32), -0.5)
-        scan(v("THR"), v("d0"), v("d1"), 0.0, Op.mult, Op.add)
+        scan(v("THR"), v("d0"), v("d1"), 2.0, Op.mult, Op.add)
         ts(v("pj"), v("pi"), 6, Op.logical_shift_right)
         ts(v("rc"), v("pj"), 16.0, Op.mult, v("kc"), Op.add)
         ts(v("OH"), v("io"), v("rc"), Op.is_equal)
         pick("p4d", v("THR", 0, 32))
         ts(v("W4D"), v("BD2"), v("p4d"), Op.mult, -0.5, Op.mult)
-        fill(v("c16k", r=1), -163840.0)
-        ts(v("PT", 0, 16), v("io", 0, 16), 32.0, Op.mult, 2048.0, Op.add)
-        ts(v("PT", 16, 17), v("kc"), 2.0, Op.mult)
-        ts(v("IO"), v("PT", 0, 16), v("PT", 16, 17), Op.add)
+        for x in range(2):
+            ts(v("d1", 16 * x, 16 * x + 16), v("io", 0, 16), v("kc"), Op.not_equal, 1024.0, Op.mult)
+        tt(v("THM", 0, 32), v("THR"), v("d1"), Op.max)
+        for x in (32, 64, 128):
+            gcp(v("THM", x, 2 * x), v("THM", 0, x))
+        fill(v("RS16"), 1.0)
+        fill(v("RS16", 0, 256, 16), 0.0)
+        fill(v("RSL"), -1.0)
+        fill(v("RSL", 0, 48, 3), 0.0)
+        fill(v("RSL", 1, 48, 3), -2.0 ** 80)
+        ts(v("PT", 0, 16), v("io", 0, 16), 16.0, Op.mult, 2048.0, Op.add)
+        for h in range(2):
+            ts(v("LW%d" % h, 61, 800, 48), v("PT", 0, 16), v("kc"), Op.add)
 
     def visit(t, h, lists=None):
         def s(name, *a, **k):
@@ -365,91 +429,94 @@ def rank_program(g, core, T, topo):
         def bank(i, lo, hi, st=1, **k):
             return v("b%d%d" % (h, i), lo, hi, st, **k)
 
-        def five(name, a, b, m=None):
-            name = "%s%d" % (name, h)
-            if m is None:
-                return vx(T[name][:, :, a:b], name, 0, 640, 5 * (b - a), ("half", a // 64))
-            return vx(T[name][:, m, a:b], name, 128 * m + a, 128 * m + b, b - a, ("half", a // 64))
+        def nodes(a, b, m0, m1):
+            return vx(T["c16%d" % h][:, a:b, m0:m1], "c16%d" % h, 6 * a, 6 * b, (m1 - m0) * (b - a))
 
         X, w = s("X", 0, 2048), 2 << t
         sv = SPLITS.get((t, h), SPLIT)
-        chunks = [(64, sv, 0), (sv, 128, 1), (0, 32, 3), (32, 64, 2)]
+        cut = min(128 - LAST, sv + 64)
+        chunks = [(0, sv, 1), (sv, cut, 3), (cut, 128, 2)]
 
         def prep(a, b):
             n = b - a
-            F, Z = s4("F", a, b), s4("F", 128 + a, 128 + b) if t else s4("Z", a, b)
-            if t and not lists:
-                ts(s4("Z"), s4("F", 128, 256), -1280.0, Op.add)
-            top = [(s("W2"), v("c1280", 0, n))] if t else []
+            raw = t and not lists
+            F, Z = s4("F", a, b), s4("F", 128 + a, 128 + b) if raw else s4("Z", a, b)
+            if raw:
+                line("Z", s4("Z"), s4("F", 128, 256), 1.0, -1280.0)
+            top = [(s("W2"), v("c1280", 0, n))] if raw else []
             U, S, V = bank(2, 0, n), bank(2, n, 2 * n), bank(2, 2 * n, 3 * n)
-            mms(U, const("one", n), *top, (s("W2"), Z))
-            mms(S, const("cS", n, 2 if t else 1), (v("BD"), Z))
-            ts(s("Hu", a, b), U, 1 / 4096, Op.mult, 1279.5, Op.add)
+            mms(U, *top, (s("W2"), Z))
+            mms(S, (v("BD"), Z))
+            line("Hu%d" % lists, s("Hu", a, b), U, 1 / 4096, 1279.5 + 1 / 4096)
             R = [bank(3, m * n, m * n + n) if m < 4 else bank(2, 3 * n, 4 * n) for m in range(5)]
             for m in range(4):
                 mms(R[m], (v("RC", r=2), v("RM", 128 * m, 128 * m + n, r=2)), (times(32 << m), F))
-            ts(s4("Hs", a, b), S, 1 / 16, Op.mult, 1280 - 15 / 32, Op.add)
+            line("Hs", s4("Hs", a, b), S, 1 / 16, v("ks1" if raw else "ks0"))
             mms(V, (s("W2"), Z), *top, const("cU", n, 2), (times(-4096), s("Hu", a, b)))
             mms(R[4], (v("RC", r=2), v("RM", 512, 512 + n, r=2)), (times(512), F))
             tt(s("P", a, b), V, F, Op.mult)
             for m in range(5):
                 q = s("Q", 128 * m + a, 128 * m + b)
                 tt(q, R[m], s("P", a, b), Op.add)
-                ts(five("C", a, b, m), q, 5 + m, Op.logical_shift_right, 2047, Op.bitwise_and)
-            gcp(five("c16", a, b), five("C", a, b))
-            hi = min(b, sv)
-            for m in range(5):
-                (gcp if lists else cp)(s("off6", 6 * a + m, 6 * hi - 5 + m, 6), five("C", a, hi, m))
-            if hi < b:
-                cp(s("offV", 0, 5 * (b - hi)), five("C", hi, b))
-                lo = hi // 16 * 16
+                ts(s("C", 6 * a + m, 6 * b - 5 + m, 6), q, 5 + m, Op.logical_shift_right, 2047, Op.bitwise_and)
+            lo = max(a, sv)
+            (gcp if lists else cp)(s("off6", 6 * lo, 6 * b), s("C", 6 * lo, 6 * b))
+            gcp(nodes(a, b, 0, 6), s("C", 6 * a, 6 * b))
+            if a < lo:
+                for m in range(5):
+                    (gcp if m >= OVG else cp)(s("offV", m * sv, m * sv + sv), s("C", m, 6 * sv - 5 + m, 6))
+                hi = -(-sv // 16) * 16
                 for k in range(4):
-                    gcp(s("Zy", 4 * (lo - VA) + k, 4 * (b - VA) - 3 + k, 4), s4("Z", lo, b))
+                    gcp(s("Zy", k, 4 * hi - 3 + k, 4), s4("Z", 0, hi))
                 for k in range(4):
-                    gcp(s("Zx", 16 * (hi - VA) + k, 16 * (b - VA) - 3 + k, 4), s("Zy", 4 * (hi - VA), 4 * (b - VA)))
+                    gcp(s("Zx", k, 16 * sv - 3 + k, 4), s("Zy", 0, 4 * sv))
 
         def gather(a, b):
             zn = "Z%d%d" % (h, t)
-            for i in range(a, min(b, sv)):
+            for i in range(max(a, sv), b):
                 z = vx(T[zn][:, i // w, i % w // (w // 2), i % (w // 2):i % (w // 2) + 1], zn, i, i + 1, 1)
                 actg(s("A", 80 * i, 80 * i + 80), X, s("off6", 6 * i, 6 * i + 5), Act.Abs, z)
-                if last:
-                    ops[-1][3].setdefault(last[0], False)
-                last[:] = [len(ops) - 1]
+                inturn()
 
             def one(o, f, z):
-                op("v", lambda: g.vector.tensor_tensor(o[0], X[0].indirect(f[0]), z[0], Op.subtract), [o], [X, f, z], 0.05 + o[4] * GATH2 * CYC)
-            n = b - sv
-            for m in range(5 if n > 0 else 0):
-                for x in range(m * n, m * n + n, VP):
-                    one(s("A", 80 * a + 16 * x, 80 * a + 16 * (x + VP)), s("offV", x, x + VP), s("Zx", 16 * (a - VA + x % n), 16 * (a - VA + x % n + VP)))
+                vgather(lambda: g.vector.tensor_tensor(o[0], X[0].indirect(f[0]), z[0], Op.subtract), o, [X, f, z])
+            n = sv
+            for m in range(0 if a else 5):
+                for x in range(VP[m]):
+                    x, y = x * n // VP[m] // 2 * 2, (x + 1) * n // VP[m] // 2 * 2
+                    one(s("A", 16 * (m * n + x), 16 * (m * n + y)), s("offV", m * n + x, m * n + y), s("Zx", 16 * x, 16 * y))
                 for x in range(m * n, m * n + n, RP):
                     y = min(x + RP, m * n + n)
-                    ts(s("RL", 16 * x, 16 * y), s("A", 80 * a + 16 * x, 80 * a + 16 * y), 0.0, Op.max)
+                    ts(s("RL", 16 * x, 16 * y), s("A", 16 * x, 16 * y), 0.0, Op.max)
 
         def choose(a, b, kb):
-            n, own = b - a, a < sv
+            n, own = b - a, a >= sv
             keys = bank(kb, 0, 5 * n)
             key = [bank(kb, m, 5 * n - 4 + m, 5) if own else bank(kb, m * n, m * n + n) for m in range(5)]
-            mm(keys, v("KC", r=2), v("MCS" if own else "MCV%d" % n, 0, 5 * n, r=2), True, False)
             if own:
-                for m in range(5):
-                    mm(key[m], v("I"), five("c16", a, b, m), False, False)
-                for p in range(a, b, SUB):
-                    q = min(p + SUB, b)
+                mm(keys, v("KC", r=2), v("MCS", 0, 5 * n, r=2), True, False)
+                parts = max(1, n // SUB)
+                for x in range(parts):
+                    p, q = a + x * n // parts, a + (x + 1) * n // parts
+                    if q == b:
+                        mm(keys, v("I"), nodes(a, b, 0, 5), False, False)
                     for k in range(16):
                         mm(bank(kb, 5 * (p - a), 5 * (q - a)), place(10240, k), s("A", 80 * p + k, 80 * q - 15 + k, 16), False, k == 15 and q == b)
                 scan(s("KS", 5 * a, 5 * b), v("RS5", 0, 5 * n), keys, 0.0, Op.max, Op.min)
             else:
-                for m0, m1 in PIECES:
-                    for x, src, c in ((-10240, "A", 80 * a), (20480, "RL", 0)):
-                        for k in range(16):
-                            mm(bank(kb, m0 * n, m1 * n), place(x, k), s(src, c + 16 * n * m0 + k, c + 16 * n * m1 - 15 + k, 16), False, False)
-                mm(keys, v("I"), five("c16", a, b), False, True)
                 least = [s("KS", 5 * a + m, 5 * b - 4 + m, 5) for m in range(5)]
-                ts(least[0], key[0], float(KN), Op.min)
-                for m in range(1, 5):
-                    tt(least[m], key[m], least[m - 1], Op.min)
+                for m0, m1 in PIECES:
+                    mm(bank(kb, m0 * n, m1 * n), v("KC", r=2), v("MCV%d" % n, m0 * n, m1 * n, r=2), True, False)
+                    for x, src in ((-10240, "A"), (20480, "RL")):
+                        for k in range(16):
+                            mm(bank(kb, m0 * n, m1 * n), place(x, k), s(src, 16 * n * m0 + k, 16 * n * m1 - 15 + k, 16), False, False)
+                    for m in range(m0, m1):
+                        mm(key[m], v("I"), nodes(a, b, m, m + 1), False, m == m1 - 1)
+                    for m in range(m0, m1):
+                        if m:
+                            tt(least[m], key[m], least[m - 1], Op.min)
+                        else:
+                            ts(least[0], key[0], float(KN), Op.min)
             eq = [s("EQm", 128 * (m - 1) + a, 128 * (m - 1) + b) for m in range(1, 5)]
             for m in range(1, 5):
                 tt(eq[m - 1], key[m], s("KS", 5 * a + 4, 5 * b, 5), Op.is_equal)
@@ -459,22 +526,36 @@ def rank_program(g, core, T, topo):
             win, top = s("A", 80 * a, 80 * b), col("top%d" % h)
 
             def second(f, near):
-                op("v", lambda: g.vector.tensor_scalar(near[0], win[0].indirect(f[0]), top[0], None, Op.is_le), [near], [win, f, top], 0.05 + near[4] * GATH * CYC)
+                vgather(lambda: g.vector.tensor_scalar(near[0], win[0].indirect(f[0]), top[0], 2.0, Op.is_le, Op.mult), near, [win, f, top])
+            mid = min(b, a + BYS) if a == sv else a
             if own:
-                for x in range(a, b, NP):
+                for x in range(a, mid, NS):
+                    y = min(x + NS, mid)
+                    actg(s("NR", 16 * x, 16 * y), win, s("pos", x, y), Act.Sign, top)
+                    if (t, h) not in FREE:
+                        inturn()
+                for x in range(mid, b, NP):
                     y = min(x + NP, b)
                     second(s("pos", x, y), s("NR", 16 * x, 16 * y))
             else:
                 actg(s("NA", 0, 16 * n), win, s("pos", a, b), Act.Abs)
-                ts(s("NR", 16 * a, 16 * b), s("NA", 0, 16 * n), top, Op.is_le)
-            if kb == 0:
-                mms(bank(0, 200, 328), const("cN", 128), (v("I"), s4("F")))
-            mms(bank(0, 384 + a, 384 + b), const("c85", n), *[(place(-(1 << 25), k), s("NR", 16 * a + k, 16 * b - 15 + k, 16)) for k in range(16)])
+                if (t, h) not in FREE:
+                    inturn()
+                ts(s("NR", 16 * a, 16 * b), s("NA", 0, 16 * n), top, Op.is_le, 2.0, Op.mult)
+                mm(bank(0, 384, 512), v("I"), s4("F"), True, False)
+            for x, y, name in ((a, mid, "c2k"), (mid, b, "c34k")):
+                if x < y:
+                    mm(bank(0, 384 + x, 384 + y), *const(name, y - x), False, False)
+            join = JOIN and (t, h) not in FREE
+            if own or not join:
+                x = 0 if join and a == sv else a
+                for k in range(16):
+                    mm(bank(0, 384 + x, 384 + b), place(-2048, k), s("NR", 16 * x + k, 16 * b - 15 + k, 16), False, b == 128 and k == 15)
 
         def meeting():
             c = 64
-            tt(s("KF"), bank(0, 384, 512), s("KS", 4, 640, 5), Op.max)
-            tt(s4("KI"), bank(0, 200, 328), s("KF"), Op.min)
+            ts(s("Cc"), s("KS", 4, 640, 5), 2047, Op.bitwise_and)
+            tt(s4("KI"), bank(0, 384, 512), s("Cc"), Op.max)
             for x in range(2):
                 ts(s("SJi", x * c, x * c + c), s4("KI", which=x), 2047, Op.bitwise_and)
             ts(s("Hh"), s("SJi"), 0.125, Op.mult, 1279.5625, Op.add)
@@ -486,45 +567,40 @@ def rank_program(g, core, T, topo):
                     mms(bank(2 + r, l * c, l * c + c), (v("B%d" % (8 * r + l)), HS))
                 for l in range(8):
                     tt(eq[8 * r + l], bank(2 + r, l * c, l * c + c), HJ, Op.is_equal)
-            G, LM, XP = (bank(0, c * i, c * i + c) for i in range(3))
-            ML, SL, MT = bank(1, 0, c), bank(1, c, 2 * c), bank(2, 4 * c, 5 * c)
-            S32, UJ, JL, JH = (bank(3, c * i, c * i + c) for i in (0, 1, 6, 7))
+            G, XP = (bank(0, c * i, c * i + c) for i in range(2))
+            ML, JL, JH = (bank(1, c * i, c * i + c) for i in range(3))
+            MT, S32, UJ = (bank(2, c * i, c * i + c) for i in (4, 5, 6))
             mms(S32, const("c32", c), (v("I"), S))
             mms(UJ, (s("W32"), s4("Z", which=1)))
             tt(s("JS"), S32, J, Op.mult)
             tt(s("JQ"), UJ, s("JS"), Op.add)
             ts(s("Jn"), s("JQ"), 5, Op.logical_shift_right, 2047, Op.bitwise_and)
-            mms(G, *[(v("G32"), eq[l]) for l in range(16)])
-            for l in range(16):
-                mm(ML, times(4 ** (15 - l)), eq[l], l == 0, False)
-            ts(s("mj"), G, v("p32"), Op.is_ge)
-            mm(ML, times(-2 ** 33, "SH"), s("mj"), False, True)
-            act(s("wM"), ML, Act.Relu)
-            mms(LM, (v("BD"), s("wM")))
-            ts(s("ms"), LM, v("p4"), Op.is_ge)
-            if t < 3:
-                mms(MT, (v("S15"), s("mj")))
-                red(v("metc", 2 * t + h, 2 * t + h + 1), MT)
-            mms(XP, (v("BN"), s("mj")), (v("BD"), s("ms")))
+            mms(G, *[(v("TRI"), eq[l]) for l in range(16)])
+            mms(ML, *[(v("MS%d" % l), eq[l]) for l in range(16)])
+            ts(s("mj"), G, 0.0, Op.is_gt)
+            ts(s("ms"), ML, 0.0, Op.is_le)
+            mms(XP, (v("BN"), s("mj")), (times(-1, "BD"), s("ms")))
             mms(JL, (v("I"), J), (times(-BIG), s("mj")))
             mms(JH, (v("I"), J), (times(BIG), s("mj")))
-            ts(s("oha"), XP, v("kc"), Op.is_equal)
-            ts(s("ohb"), XP, v("kn"), Op.is_equal)
+            ts(s("oha"), XP, v("kn"), Op.is_equal)
+            ts(s("ohb"), XP, v("km"), Op.is_equal)
             tt(s("t1"), JL, s("Jn"), Op.max)
             tt(s4("FO", which=1), JH, s("t1"), Op.min)
             for x in range(4):
-                mms(bank(2, x, 4 * c - 3 + x, 4), (v("PA%d" % x), s("oha")), (v("PA%d" % x), s("ohb")), (v("Rot%d" % (4 * x) if x else "I"), J))
-            mms(SL, (v("I"), S), (times(-BIG), s("ms")), (times(BIG, "NOK"), s("oha")))
-            cp(s("L6", 4, 6 * c, 6), SL)
+                mms(bank(2, x, 4 * c - 3 + x, 4), (v("PA%d" % x), s("oha")), (v("PA%d" % x), s("ohb")), (turn(4 * x), J))
             scan(s("T1"), v("RS4"), bank(2, 0, 4 * c), 0.0, Op.max, Op.min)
-            mms(bank(3, 4, 6 * c - 1, 6), (v("I"), S), (times(BIG), s("ms")), (times(-BIG, "NOK"), s("oha")))
+            if t < 3:
+                mms(MT, (v("S15"), s("mj")))
+                red(v("metc", 2 * t + h, 2 * t + h + 1), MT)
+            mms(bank(3, 4, 6 * c - 1, 6), const("cBIG", c), (v("I"), S), (times(-BIG), s("ms")), (times(-BIG, "NOK"), s("oha")))
             PEN = [bank(3, 5, 6 * c, 6), bank(0, 6 * c, 7 * c)]
             for x in range(2):
                 mms(PEN[x], const("cP", c, 2), (times(32768), s4("Hs", which=x)), (times(-2048, "BD"), s4("Z", which=x)))
             for x in range(4):
-                mms(bank(3, x, 6 * c - 5 + x, 6), (v("PB%d" % x), s("oha")), (v("PB%d" % x), s("ohb")), (v("Rot%d" % x if x else "I"), s("T1", 3, 4 * c, 4)))
+                mms(bank(3, x, 6 * c - 5 + x, 6), (times(BIG), s("ms")), (v("PN%d" % x), s("oha")), (v("PB%d" % x), s("ohb")),
+                    (turn(x), s("T1", 3, 4 * c, 4)))
             tt(s("Fj"), PEN[1], s4("FO", which=1), Op.min)
-            scan(s("T2"), s("L6"), bank(3, 0, 6 * c), 0.0, Op.max, Op.min)
+            scan(s("T2"), v("RS6"), bank(3, 0, 6 * c), 0.0, Op.max, Op.min)
             gcp(s4("FO", which=0), s("T2", 4, 6 * c, 6))
 
         def send(what, a):
@@ -554,9 +630,10 @@ def rank_program(g, core, T, topo):
                 terms.append((place(1, q), s("Fj", pair, 64, 8) if q % w // (w // 2) else s("T2", 6 * pair + 5, 384, 48)))
             mms(OL, *terms)
             ts(s("Ol", 0, 8), OL, REST, Op.add)
+            line("Of", s("Of"), OL, 1.0, REST)
             y, f, z = s("Y"), s("Ol", 0, 8), s("Z2")
             gcp(z, s4("Z"))
-            op("v", lambda: g.vector.tensor_tensor(y[0], X[0].indirect(f[0]), z[0], Op.add), [y], [X, f, z], 0.05 + 128 * GATH2 * CYC)
+            vgather(lambda: g.vector.tensor_tensor(y[0], X[0].indirect(f[0]), z[0], Op.add), y, [X, f, z])
             ts(s4("FO", 128, 256), y, 0.5, Op.mult, 1279.75, Op.add)
             if t < 3:
                 send("F", 0)
@@ -569,33 +646,34 @@ def rank_program(g, core, T, topo):
 
         def mining():
             ew = "EQW%d" % h
-            RR, CN, OA, LL = bank(1, 0, 256), bank(0, 256, 512), bank(1, 256, 272), bank(1, 272, 288)
-            er = "Er%d%d" % (h, t)
-            ts(s("zq"), s4("Z"), -1.25, Op.mult, -1279.625, Op.add)
-            for x, src in ((1, s("Fj")), (0, s("T2", 5, 384, 6))):
+            RR, CN, OA = bank(1, 0, 256), bank(0, 256, 512), bank(1, 256, 280)
+            line("zq", s("zq"), s4("Z"), -1.25, -1279.625)
+            for x, src in ((1, ("Fj",)), (0, ("T2", 5, 384, 6))):
                 for j in range(2):
-                    mms(bank(0, 128 * x + 64 * j, 128 * x + 64 * j + 64), (v("BD%d" % j), src))
+                    mms(bank(0, 128 * x + 64 * j, 128 * x + 64 * j + 64), (v("BD%d" % j), s(*src)))
             for x in range(2):
-                ts(s4("Er", 0, 256, x), bank(0, 128 * x, 128 * x + 128), REST, Op.add)
-            mms(OA, *[(place(1, q), vx(T[er][:, q // w::16 // w, q % w // (w // 2), q % (w // 2)], er, 0, 256, 16)) for q in range(16)])
+                line("Er", s4("Er", 0, 256, x), bank(0, 128 * x, 128 * x + 128), -1.0, -REST)
             for j in range(2):
-                ts(s("OI", 0, 8, r=64 * j + 64, p=64 * j), bank(1, 256 + j, 271 + j, 2, r=64 * j + 64, p=64 * j), 1 / 16, Op.mult)
-            ts(s("Ouf"), OA, 1 / 16, Op.mult)
-            mm(CN, v("I"), v("THR"), True, False)
+                mms(bank(1, 256 + 8 * j, 264 + 8 * j), (v("I%d" % j), s("Of")))
+                mms(bank(1, 272 + 4 * j, 276 + 4 * j), *[(v("I%d%d" % (j, x)), s("Of", x, 7 + x, 2)) for x in range(2)])
+            ts(s("LW", 77, 1184, 48), OA, -1.0, Op.mult)
+            mm(CN, v("I"), v("THM"), True, False)
             for c in range(8):
-                ts(vx(T[ew][:, c, 0:256 - 32 * c], ew, 256 * c, 256 * c + 256 - 32 * c, 256 - 32 * c), s4("Er", 32 * c, 256), s("OI", c, c + 1), Op.is_equal)
+                ts(vx(T[ew][:, c, 0:256 - 32 * c], ew, 256 * c, 256 * c + 256 - 32 * c, 256 - 32 * c), s4("Er", 32 * c, 256), s("LW", 845 + 48 * c, 846 + 48 * c), Op.is_equal)
                 if c < 7:
-                    mm(bank(0, 288 + 32 * c, 512), v("BD2"), vx(T[ew][:, c, 32:256 - 32 * c], ew, 256 * c + 32, 256 * c + 256, 224 - 32 * c), False, False)
+                    mm(bank(0, 288 + 32 * c, 512), times(-1, "BD2"), vx(T[ew][:, c, 32:256 - 32 * c], ew, 256 * c + 32, 256 * c + 256, 224 - 32 * c), False, False)
                 mm(bank(0, 256 + 32 * c, 288 + 32 * c), v("W4D"), vx(T[ew][:, c, 0:32], ew, 256 * c, 256 * c + 32, 32), False, c == 7)
             for j in range(2):
                 mms(bank(1, 128 * j, 128 * j + 128), (v("I%d" % j), s("zq")), (v("I%d" % j), s("Y")))
-            ts(s("R2"), RR, 1280.0, Op.add, 0.0, Op.max)
-            act(s("lo"), CN, Act.Sign)
-            mms(LL, (v("I"), v("IO")), const("c16k", 16), *[(place(10240, q), s("lo", q, 241 + q, 16)) for q in range(16)])
-            tt(s("LO"), LL, s("Ouf"), Op.max)
-            cp(s("Ls"), s("LO"))
+            if t >= R2S:
+                act(s("R2"), RR, Act.Relu, bias=1280.0)
+            else:
+                ts(s("R2"), RR, 1280.0, Op.add, 0.0, Op.max)
+            scan(s("LW", 0, 768, 3), v("RS16"), CN, 0.0, Op.mult, Op.min)
+            scan(s("LO"), v("RSL"), s("LW", 45, 800, 16), 0.0, Op.mult, Op.min)
+            ts(s("Ls"), s("LO", 2, 48, 3), -1.0, Op.mult)
             XW, ls, r2 = s("X"), s("Ls"), s("R2")
-            soon[op("v", lambda: g.vector.tensor_copy(XW[0].indirect(ls[0]), r2[0]), [XW], [ls, r2], 0.05 + 256 * 3.8 * CYC)] = SOON if t < 3 else 0.0
+            op("v", lambda: g.vector.tensor_copy(XW[0].indirect(ls[0]), r2[0]), [XW], [ls, r2], 0.05 + 256 * 3.8 * CYC)
 
         if lists is not None:
             prep(*PREP[lists])
@@ -604,7 +682,9 @@ def rank_program(g, core, T, topo):
             visit(t, h, 0)
             visit(t, h, 1)
             if h == 0:
+                x = len(ops)
                 key_constants()
+                due.update((i, SOON) for i in range(x, len(ops)))
                 meeting_constants()
                 mining_constants()
             cp(col("top%d" % h), col("limf%d" % h))
@@ -639,22 +719,21 @@ def rank_program(g, core, T, topo):
         for h in range(2):
             visit(t, h)
 
+    every = list(range(len(ops)))
     hold = [{"r": 0.0, "y": 0.1}.get(o[0], o[2]) for o in ops]
     after, before = [[] for _ in ops], [[] for _ in ops]
     for j, o in enumerate(ops):
         for i, wait in o[3].items():
-            lag = ops[i][2] + WAKE + soon.get(i, 0.0) if wait else (ops[i][2] if o[0] == "r" else hold[i])
+            lag = ops[i][2] + WAKE if wait else (ops[i][2] if o[0] == "r" else hold[i])
             after[i].append((j, lag))
             before[j].append((i, lag + hold[j] - hold[i]))
 
     def fit(key, follow, lead, early):
         left = [len(x) for x in lead]
         free = {o[0]: [] for o in ops}
-        ready, at, turn = [(key[i], i) for i in range(len(ops)) if not left[i]], [0.0] * len(ops), []
+        ready, at, turn = sorted(((key[i], i) for i in every if not left[i]), reverse=True), [0.0] * len(ops), []
         while ready:
-            first = min(ready)
-            ready.remove(first)
-            i = first[1]
+            i = ready.pop()[1]
             start, taken = early[i], free[ops[i][0]]
             x = len(taken)
             while x and taken[x - 1][0] > start:
@@ -676,24 +755,63 @@ def rank_program(g, core, T, topo):
             turn.append(i)
             for j, lag in follow[i]:
                 left[j] -= 1
-                early[j] = max(early[j], start + lag)
+                if early[j] < start + lag:
+                    early[j] = start + lag
                 if not left[j]:
-                    ready.append((key[j], j))
+                    new, a, b = (key[j], j), 0, len(ready)
+                    while a < b:
+                        if ready[(a + b) // 2] > new:
+                            a = (a + b) // 2 + 1
+                        else:
+                            b = (a + b) // 2
+                    ready.insert(a, new)
         return at, turn
-    way = [0.0] * len(ops)
-    for i in range(len(ops) - 1, -1, -1):
-        way[i] = max([ops[i][2] + due.get(i, 0.0)] + [lag + way[j] for j, lag in after[i]])
-    at, turn = fit([-x for x in way], after, before, [0.0] * len(ops))
-    best = None
-    for x in range(ROUNDS + 1):
-        end = max(at[i] + ops[i][2] for i in range(len(ops)))
-        if best is None or end < best[0]:
-            best = (end, at, turn)
-        if x < ROUNDS:
-            back, turn = fit([-at[i] - hold[i] for i in range(len(ops))], before, after, [o[2] - hold[i] + due.get(i, 0.0) for i, o in enumerate(ops)])
-            at, turn = fit([-back[i] - hold[i] for i in range(len(ops))], after, before, [0.0] * len(ops))
-    end, at, turn = best
-    order = sorted(turn, key=lambda i: at[i])
+
+    def again(at):
+        back, turn = fit([-at[i] - hold[i] for i in every], before, after, [o[2] - hold[i] + due.get(i, 0.0) for i, o in enumerate(ops)])
+        at, turn = fit([-back[i] - hold[i] for i in every], after, before, [0.0] * len(ops))
+        return at, sorted(turn, key=lambda i: at[i])
+
+    def length(order):
+        total = 0.0
+        for (gath, fixed, wake, wire, slow), cost in zip(CASES, costs):
+            now, done = {o[0]: 0.0 for o in ops}, [0.0] * len(ops)
+            for i in order:
+                q = ops[i][0]
+                start = now[q]
+                for j in waits[i]:
+                    if done[j] > start:
+                        start = done[j]
+                done[i] = start + cost[i] + wake
+                now[q] = start + cost[i] if q in semof else (start + 0.1 if q == "y" else 0.0)
+            total += max(done)
+        return total / len(CASES)
+
+    if not ORDER:
+        waits = [[j for j, wait in o[3].items() if wait or o[0] == "r"] for o in ops]
+        costs = [[wire - wake if o[0] == "r" else fixed * o[2] + picks[i] * (gath - fixed * GATH) * CYC if i in picks else o[2] * slow.get(o[0], 1)
+                  for i, o in enumerate(ops)] for gath, fixed, wake, wire, slow in CASES]
+        way = [0.0] * len(ops)
+        for i in every[::-1]:
+            way[i] = max([ops[i][2] + due.get(i, 0.0)] + [lag + way[j] for j, lag in after[i]])
+        at, turn = fit([-x for x in way], after, before, [0.0] * len(ops))
+        best, seed = None, SEED
+        for x in range(ROUNDS + TRIES):
+            if x >= ROUNDS:
+                at, seed = list(now[1]), (seed * 1103515245 + 12345) % (1 << 31)
+                lo, size = seed % 1000 / 1000 * (max(at) + STRETCH) - STRETCH, SHAKE[x % len(SHAKE)]
+                for i in every:
+                    if lo < at[i] < lo + STRETCH:
+                        seed = (seed * 1103515245 + 12345) % (1 << 31)
+                        at[i] += size * ((seed >> 8) % 2001 / 1000 - 1)
+            at, order = again(at)
+            end = length(order)
+            if best is None or end < now[0] + WORSE * (1 - x / (ROUNDS + TRIES)):
+                now = (end, at, order)
+            if best is None or end < best[0]:
+                best = now
+        ORDER.append(best)
+    end, at, order = ORDER[0]
 
     count, know, value, clocks = {}, {o[0]: {} for o in ops}, {}, {}
     for i in order:

from concourse.mybir import dt, AluOpType as Op, AxisListType, ActivationFunctionType as Act

NEXT = 1
SPLIT, SPLITS = 44, {(0, 0): 48, (3, 1): 54}
WIDE = sorted({SPLIT} | set(SPLITS.values()))
PIECES = [(0, 3), (3, 5)]
PREP = [(0, 64), (64, 128)]
LAST = 24
VP, RP, NP, NS = (2, 2, 2, 2, 2), 22, 24, 64
SUB = 13
BYS = 52
R2S, OVG, JOIN, FREE = 4, 2, 1, []
BYSCALAR = []
BS, MSS, MSG = 0, 0, 0
KN = 13 << 20
BIG = 4096.0
MAGIC = 1.5 * (1 << 23)
REST = 2048.0 * 105

f32, bf, f16, i32, u16 = "float32", "bfloat16", "float16", "int32", "uint16"
SCRATCH = {}
PER = {
    "X": ([128, 2304], bf), "A": ([128, 80 * 128], bf), "RL": ([128, 80 * 64], bf), "Zx": ([128, 1024], bf), "Zy": ([128, 256], bf),
    "off6": ([128, 768], u16), "offV": ([128, 320], u16), "c16": ([128, 128, 6], f16),
    "P": ([128, 128], f32), "Q": ([128, 640], i32), "C": ([128, 768], i32), "KS": ([128, 640], i32), "EQm": ([128, 512], bf),
    "NR": ([128, 2048], bf), "NA": ([128, 1024], bf), "EQ2": ([128, 1024], bf), "EQW": ([128, 8, 256], bf),
    "W2": ([128, 128], bf), "W32": ([128, 128], bf), "Zo": ([128, 128], bf), "LW": ([128, 1184], f32),
}
PARTS = {
    "h16": (f16, [("Hu", 128), ("zq", 128), ("SJ", 128), ("Hh", 128), ("T1", 256), ("T2", 384), ("t1", 64), ("Fj", 64), ("Y", 128), ("Of", 8)]),
    "b16": (bf, [("mj", 64), ("ms", 64), ("oha", 64), ("ohb", 64), ("Z2", 128), ("R2", 256)]),
    "w32": (f32, [("JS", 64), ("LO", 48), ("yo", 128), ("w2c", 4), ("limf", 4), ("top", 4)]),
    "n32": (i32, [("Cc", 128), ("fin", 128), ("SJi", 128), ("JQ", 64), ("Jn", 64), ("win", 4), ("lin", 4)]),
    "u16": (u16, [("pos", 128), ("Ol", 16), ("Ls", 16)]),
}
COLS = {}
for _h in range(2):
    for _n, (_s, _d) in PER.items():
        SCRATCH["%s%d" % (_n, _h)] = ("sbuf", _s, _d)
    for _b, (_d, _ts) in PARTS.items():
        _c = 0
        for _n, _w in _ts:
            COLS["%s%d" % (_n, _h)] = ("%s%d" % (_b, _h), _c, _w)
            _c += _w
        SCRATCH["%s%d" % (_b, _h)] = ("sbuf", [128, _c], _d)
    for _t in range(4):
        for _n, _d, _w in (("Z", bf, 64), ("KI", i32, 64), ("Hs", f16, 64), ("Er", f16, 128), ("F", f16, 128), ("FO", f16, 128)):
            SCRATCH["%s%d%d" % (_n, _h, _t)] = ("sbuf", [128, _w >> _t, 2, 1 << _t], _d)
MATS = ["BD", "I", "BDt", "TRI", "BN", "S15", "NOK", "BD2", "BD0", "BD1", "I0", "I1", "I00", "I01", "I10", "I11", "W4D"] + \
    ["%s%d" % (x, l) for x in ("B", "MS") for l in range(16)] + ["Rot%d" % d for d in (1, 2, 3, 4, 8, 12)] + \
    ["%s%d" % (x, a) for x in ("PA", "PB", "PN") for a in range(4)] + ["BDN"]
SCRATCH["mats"] = ("sbuf", [128, 128 * len(MATS)], bf)
for _i, _n in enumerate(MATS):
    COLS[_n] = ("mats", 128 * _i, 128)
SCRATCH["pool"] = ("sbuf", [128, 144 * 30], bf)
EARLY = 30
CONST = {
    "cb": (bf, [("one", 256), ("E", 144), ("Et", 144), ("RS5", 320), ("RS4", 256), ("RS6", 384), ("cBIG", 128), ("THR", 32), ("THM", 256), ("RS16", 256), ("RSL", 48), ("d0", 32), ("d1", 32), ("KC", 128), ("MCS", 320),
                ("cU", 128), ("cS", 128), ("cP", 128), ("c2k", 128), ("c34k", 128), ("c32", 128), ("c1280", 128)] +
           [("MCV%d" % n, 5 * n) for n in WIDE]),
    "ch": (f16, [("RC", 128), ("RM", 640), ("b1", 64), ("c160", 128), ("c1", 128)]),
    "cf": (f32, [("io", 32), ("OH", 32), ("PW", 32), ("PT", 32), ("kc", 1), ("ks0", 1), ("ks1", 1), ("kn", 1), ("km", 1), ("rc", 1), ("p512", 1), ("p4d", 1), ("mets", 1), ("metc", 8), ("sel", 8)]),
    "ci": (i32, [("pi", 1), ("pk", 1), ("pj", 1), ("meti", 1), ("mete", 1)]),
}
for _b, (_d, _ts) in CONST.items():
    _c = 0
    for _n, _w in _ts:
        COLS[_n] = (_b, _c, _w)
        _c += _w
    SCRATCH[_b] = ("sbuf", [128, _c], _d)
SCRATCH["RW"] = SCRATCH["RX"] = ("sbuf", [128, 8, 32], bf)
BANKS = ["b%d%d" % (h, i) for h in range(2) for i in range(4)]
for _n in BANKS:
    SCRATCH[_n] = ("psum", [128, 512], f32)
HALVES = [("BD2", "BD", [0, 1], [0, 1])] + [("%s%d" % (n, j), n, [j], [0, 1]) for n in ("BD", "I") for j in range(2)] + \
    [("I%d%d" % (j, x), "I", [j], [x]) for j in range(2) for x in range(2)]
SEMAPHORES = ["sg", "sv", "ss", "st", "loc"] + ["d" + x[0] for x in HALVES] + ["d%s%d" % (c, h) for c in "ZWFXL" for h in range(2)] + \
    ["o%s%d" % (c, h) for c in "FZX" for h in range(2)] + ["r%s%d%d" % (c, h, t) for c in "FZ" for h in range(2) for t in (1, 2, 3)]

CYC, TCYC, GATH, WAKE, WIRE = 0.85e-3, 0.46e-3, 1.56, 0.21, 2.6
CASES = [(GATH, 1, WAKE, WIRE, {}), (1.1, 1, 0.15, 2.0, {"t": 0.9, "g": 0.8}), (2.05, 1, 0.17, 2.2, {"t": 1.1}),
         (1.3, 1, 0.33, 3.5, {"g": 1.1}), (1.75, 1, 0.14, 1.8, {"g": 0.87})]
GSLOW = 1.0
SLACK = 0.04
ROUNDS, AHEAD = 4, 4.0
SOON = 0.0
TRIES, STRETCH, SHAKE, SEED, WORSE = 200, 12.0, (0.2, 0.7, 2.0), 1, 0.03
ORDER = []


def rank_program(g, core, T, topo):
    rank = T.rank_of(core)
    if rank is None:
        return
    nrank = len(T.cores)
    eng = {"g": g, "v": g.vector, "s": g.scalar, "t": g.tensor, "y": g.sync}
    semof = {"g": "sg", "v": "sv", "s": "ss", "t": "st"}
    ops = []
    hist = {}

    def meets(a, b):
        return a[2] < b[3] and b[2] < a[3] and a[5][0] < b[5][1] and b[5][0] < a[5][1] and not (a[6][0] == b[6][0] and a[6][1] != b[6][1])

    def covers(a, b):
        return a[2] <= b[2] and b[3] <= a[3] and a[5][0] <= b[5][0] and b[5][1] <= a[5][1] and (a[6][0] == 1 or a[6] == b[6])

    def op(q, fn, outs, ins, cost=0.06, sem=None, inc=1):
        me, deps = len(ops), {}
        for accs, wr in ((ins, False), (outs, True)):
            for acc in accs:
                writes, reads = hist.get(acc[1], ((), ()))
                if acc[1] in BANKS:
                    turn = reads and ops[reads[-1][1]][0] != q
                    for old, i, w in (reads if turn else writes):
                        deps[i] = True
                    for old, i, w in (() if turn else reads):
                        if (w or wr) and meets(acc, old):
                            deps.setdefault(i, False)
                else:
                    for olds in (writes, reads if wr else ()):
                        for old, i in olds:
                            if meets(acc, old):
                                deps[i] = True
        ops.append([q, fn, cost, deps, sem or semof[q], inc])
        for accs, wr in ((ins, False), (outs, True)):
            for acc in accs:
                mark(acc, wr, me)
        return me

    def mark(acc, wr, me):
        both = hist.setdefault(acc[1], ([], []))
        if acc[1] in BANKS:
            if both[1] and ops[both[1][-1][1]][0] != ops[me][0]:
                both[0][:] = both[1]
                del both[1][:]
            if wr:
                both[1][:] = [a for a in both[1] if not covers(acc, a[0])]
            both[1].append((acc, me, wr))
            return
        if wr:
            for h in both:
                h[:] = [a for a in h if not covers(acc, a[0])]
        both[0 if wr else 1].append((acc, me))

    def v(name, lo=0, hi=None, st=1, r=128, p=0):
        if name in COLS:
            name, base, wide = COLS[name]
            lo, hi = base + lo, base + (wide if hi is None else hi)
        hi = SCRATCH[name][1][1] if hi is None else hi
        ap = T[name][p:r, lo:hi:st] if st > 1 else T[name][p:r, lo:hi]
        return (ap, name, lo, hi, (hi - lo + st - 1) // st, (p, r), (st, lo % st))

    def col(name):
        return v(name, 0, 1)

    def vx(ap, name, lo, hi, n, part=(1, 0)):
        return (ap, name, lo, hi, n, (0, 128), part)

    def v4(name, t, a=0, b=128, which=None, r=128, p=0):
        w = 2 << t
        if which is None:
            return (T[name][p:r, a // w:b // w, :, :], name, a, b, b - a, (p, r), (1, 0))
        return vx(T[name][:, a // w:b // w, which, :], name, a, b, (b - a) // 2, ("pair", which))

    def vcost(o, *ins):
        two = all(x[1] not in BANKS and SCRATCH[x[1]][2] in (bf, f16, u16) for x in (o,) + ins[:1])
        if len(ins) == 2:
            return max(64, o[4] * (1 if ins[0][1] in BANKS or ins[1][1] in BANKS else 2)) * CYC
        return max(64, o[4] * (0.5 if two else 1)) * CYC

    def tt(o, a, b, f):
        op("v", lambda: g.vector.tensor_tensor(o[0], a[0], b[0], f), [o], [a, b], vcost(o, a, b))

    def ts(o, a, s1, f1, s2=None, f2=None):
        ins = [a] + [s for s in (s1, s2) if isinstance(s, tuple)]
        x1 = s1[0] if isinstance(s1, tuple) else s1
        x2 = s2[0] if isinstance(s2, tuple) else s2
        if f2 is None:
            op("v", lambda: g.vector.tensor_scalar(o[0], a[0], x1, None, f1), [o], ins, vcost(o, a))
        else:
            op("v", lambda: g.vector.tensor_scalar(o[0], a[0], x1, x2, f1, f2), [o], ins, vcost(o, a))

    def cp(o, a):
        op("v", lambda: g.vector.tensor_copy(o[0], a[0]), [o], [a], vcost(o, a))

    def fill(o, c):
        op("v", lambda: g.vector.memset(o[0], c), [o], [], vcost(o))

    def red(o, a):
        op("v", lambda: g.vector.tensor_reduce(o[0], a[0], AxisListType.X, Op.add), [o], [a])

    def scan(o, d0, d1, first, f0, f1):
        op("v", lambda: g.vector.tensor_tensor_scan(o[0], d0[0], d1[0], first, f0, f1), [o], [d0, d1], max(64, o[4]) * CYC)

    def mm(o, l, r, start, stop):
        me = op("t", lambda: g.tensor.matmul(o[0], l[0], r[0], start, stop), [o], [l, r], max(64, r[4]) * TCYC)
        for i in group.get(o[1], ()) if start or stop else ():
            ops[me][3].setdefault(i, False)
        group[o[1]] = [me] if start or stop else group[o[1]] + [me]

    def mms(o, *terms):
        for i, (l, r) in enumerate(terms):
            mm(o, l, r, i == 0, i == len(terms) - 1)

    def const(name, n, r=1):
        return (v(name, 0, 128, r=r), v("one", 0, n, r=r))

    def act(o, a, func, **kw):
        op("s", lambda: g.scalar.activation(o[0], a[0], func, **kw), [o], [a], max(64, o[4]) * CYC)

    def line(who, o, a, x, y):
        if who not in BYSCALAR:
            return ts(o, a, x, Op.mult, y, Op.add)
        ins, bias = ([a, y], y[0]) if isinstance(y, tuple) else ([a], y)
        op("s", lambda: g.scalar.activation(o[0], a[0], Act.Identity, bias=bias, scale=x), [o], ins, max(64, o[4]) * CYC)

    def scaled(o, a, x):
        op("s", lambda: g.scalar.activation(o[0], a[0], Act.Copy, scale=x[0]), [o], [a, x], max(64, o[4]) * CYC)

    def relu(o, a, y):
        op("s", lambda: g.scalar.activation(o[0], a[0], Act.Relu, bias=y[0]), [o], [a, y], max(64, o[4]) * CYC)

    def actg(o, win, f, func, z=None):
        cost, picks[len(ops)] = 0.065 + o[4] * GATH * CYC, o[4]
        if z is None:
            op("s", lambda: g.scalar.activation(o[0], win[0].indirect(f[0]), func), [o], [win, f], cost)
        else:
            op("s", lambda: g.scalar.activation(o[0], win[0].indirect(f[0]), func, bias=z[0], scale=-1.0), [o], [win, f, z], cost)

    def vgather(call, o, ins):
        picks[op("v", call, [o], ins, 0.05 + o[4] * GATH * CYC)] = o[4]

    def asel(o, a, pat, cop, base, cm):
        op("g", lambda: g.affine_select(o[0], a[0], pat, cop, 0.0, base, cm), [o], [a], GSLOW * (0.17 + 2 * o[4] * CYC))

    def gcp(o, a):
        asel(o, a, [[0, o[4]]], Op.is_gt, 1, 0)

    def iota(o, pat, base, cm, small=True):
        if small:
            op("g", lambda: g.iota(o[0], pat, base, cm, allow_small_or_imprecise_dtypes=True), [o], [], 0.13 + 2 * o[4] * CYC)
        else:
            op("g", lambda: g.iota(o[0], pat, base, cm), [o], [], 0.13 + 2 * o[4] * CYC)

    def dma(o, a, outs, ins, sem):
        op("y", lambda: g.sync.dma_start(o, a), outs, ins, 2.0, sem, 16)

    def times(x, name="I", lo=0):
        if x == 1:
            return v(name, lo, lo + 128)
        if (name, x) not in pool:
            pool[name, x] = c = 144 * len(pool)
            o = v("pool", c, c + COLS[name][2])
            if len(pool) <= EARLY:
                act(o, v(name), Act.Copy, scale=float(x))
            else:
                ts(o, v(name), float(x), Op.mult)
        c = pool[name, x] + lo
        return v("pool", c, c + 128)

    def place(x, k):
        return times(x, "E", 15 - k)

    def turn(d):
        return v("Rot%d" % d if d else "I")

    def half(j):
        return {"p": 64 * j, "r": 64 * j + 64}

    def inturn():
        if last:
            ops[-1][3].setdefault(last[0], False)
        last[:] = [len(ops) - 1]

    group, last, pool, due, picks = {}, [], {}, {}, {}

    def loads(h):
        rows = slice(64 * h, 64 * h + 64)
        for j in range(2):
            z = v4("Z%d0" % h, 0, 0, 128, None, 64 * j + 64, 64 * j)
            dma(z[0], T.vein[rows, 128 * j:128 * j + 128], [z], [], "dZ%d" % h)
        for name, src, sem in (("win", T.w, "dW"), ("fin", T.front, "dF"), ("X", T.rock, "dX"), ("lin", T.lim, "dL")):
            for j in range(2):
                wide = {"fin": 128, "X": 2048}.get(name, 1)
                o = v("%s%d" % (name, h), 0, wide, r=64 * j + 64, p=64 * j)
                dma(o[0], src[rows, 128 * j:128 * j + 128] if name == "fin" else src[rows, :], [o], [], "%s%d" % (sem, h))

    def list_constants():
        fill(v("one"), 1.0)
        iota(v("pi"), [[0, 1]], 0, 1, False)
        asel(v("BDt"), v("one", 0, 128), [[-16, 8], [0, 16]], Op.is_ge, 0, 1)
        asel(v("BD"), v("BDt"), [[16, 8], [0, 16]], Op.is_ge, 15, -1)
        asel(v("I"), v("one", 0, 128), [[-1, 128]], Op.is_equal, 0, 1)
        iota(v("RC", r=2), [[0, 8], [37, 16]], 0, 0)
        iota(v("cS", r=1), [[0, 8], [-1, 16]], 16, 0)
        for m in range(5):
            fill(v("RM", 128 * m, 128 * m + 128, r=2), float(32 << m))
            fill(v("RM", 128 * m, 128 * m + 128, r=1), float(m * (32 << m)))
        fill(v("RC", r=1), 613.0)
        fill(v("cU", r=2), 1.0)
        fill(v("cU", r=1), 1280.0 * 4096)
        ts(v("pk"), v("pi"), 15, Op.bitwise_and)
        cp(v("kc"), v("pk"))
        for x in range(2):
            ts(v("ks%d" % x), v("pk"), -1 / 16, Op.mult, 1281 - 15 / 32 - 1280 * x, Op.add)

    def stream_constants(h):
        cp(v4("F%d0" % h, 0), v("fin%d" % h))
        ts(col("w2c%d" % h), col("win%d" % h), 2.0, Op.mult)
        ts(v("W2%d" % h), v("BD"), col("w2c%d" % h), Op.mult)
        ts(v("W32%d" % h), v("W2%d" % h), 16.0, Op.mult)
        ts(col("limf%d" % h), col("lin%d" % h), 0.5, Op.add)
        fill(v("X%d" % h, 2048, 2304), 0.0)
        fill(v("C%d" % h, 5, 768, 6), 0)

    def key_constants():
        fill(v("E"), 0.0)
        fill(v("E", 15, 144, 16), 1.0)
        asel(v("Et"), v("E"), [[-1, 144]], Op.is_ge, 15, 1)
        asel(v("E"), v("Et"), [[1, 144]], Op.is_ge, 0, -1)
        iota(v("KC", r=2), [[0, 128]], -4096, 6144)
        iota(v("MCS", r=2), [[0, 64], [1, 5]], 0, 0)
        fill(v("MCS", r=1), 4096.0)
        for n in WIDE:
            iota(v("MCV%d" % n, r=2), [[1, 5], [0, n]], 0, 0)
            fill(v("MCV%d" % n, r=1), 4096.0)
        fill(v("c1", r=1), 1.0)
        fill(v("RS5"), -float(1 << 25))
        fill(v("RS5", 0, 320, 5), float(KN))
        iota(v("b1", r=1), [[1, 64]], 0, 0)
        fill(v("c160", r=1), 160.0)
        fill(v("c2k", r=1), 2048.0)
        fill(v("c34k", r=1), 2048.0 * 17)

    def pick(name, row):
        tt(v("PT", 0, row[4]), row, v("OH", 0, row[4]), Op.mult)
        red(v(name), v("PT", 0, row[4]))

    def meeting_constants():
        iota(v("io"), [[1, 32]], 0, 0)
        ts(v("OH", 0, 16), v("io", 0, 16), v("kc"), Op.is_equal)
        for l in range(16):
            if l < BS:
                scaled(v("B%d" % l), v("BD"), v("OH", l, l + 1))
            else:
                asel(v("B%d" % l), v("one", 0, 128), [[-16, 8], [0, 16]], Op.is_equal, -l, 1)
        fill(v("d0", 0, 16), 1 / 512)
        fill(v("d1", 0, 16), 0.0)
        scan(v("PW", 0, 16), v("d0", 0, 16), v("d1", 0, 16), 2.0 ** 73, Op.mult, Op.add)
        pick("p512", v("PW", 0, 16))
        for x, f in enumerate((-1.0, 16.0)):
            ts(vx(T.RX[:, :, 16 * x:16 * x + 16], "RX", 0, 256, 128), v("BD"), v("p512"), Op.mult, f, Op.mult)
        for l in range(16):
            o, a = v("MS%d" % l), vx(T.RX[:, :, 15 - l:31 - l], "RX", 0, 256, 128)
            if l < MSS:
                act(o, a, Act.Copy)
            elif l < MSG:
                gcp(o, a)
            else:
                cp(o, a)
        asel(v("TRI"), v("BD"), [[1, 128]], Op.is_ge, 0, -1)
        ts(v("S15"), v("one", 0, 128), v("OH", 15, 16), Op.mult)
        ts(v("PT", 0, 1), v("OH", 15, 16), -1.0, Op.add)
        ts(v("BN"), v("BD"), v("PT", 0, 1), Op.mult)
        ts(v("kn"), v("kc"), -16.0, Op.add)
        ts(v("km"), v("kc"), -32.0, Op.add)
        fill(v("c32", r=1), 32.0)
        asel(v("NOK"), v("BD"), [[-16, 8], [1, 16]], Op.is_gt, -15, 1)
        for x in range(2):
            cp(vx(T.RW[:, :, 16 * x:16 * x + 16], "RW", 0, 256, 128), v("I"))
        for d in (1, 2, 3, 4, 8, 12):
            cp(turn(d), vx(T.RW[:, :, d:d + 16], "RW", 0, 256, 128))
        tt(v("BDN"), times(BIG, "BD"), times(BIG, "NOK"), Op.add)
        for x, f in enumerate((Op.logical_shift_right, Op.bitwise_and)):
            ts(v("pj"), v("pk"), 2 + x, f)
            cp(v("rc"), v("pj"))
            ts(v("sel", 4 * x, 4 * x + 4), v("io", 0, 4), v("rc"), Op.is_equal, -BIG, Op.mult)
        for a in range(4):
            for name, src, s in (("PA", times(BIG, "BD"), a), ("PB", times(BIG, "BD"), 4 + a), ("PN", v("BDN"), 4 + a)):
                if name in BYSCALAR:
                    relu(v("%s%d" % (name, a)), src, v("sel", s, s + 1))
                    due[len(ops) - 1] = SOON
                else:
                    ts(v("%s%d" % (name, a)), src, v("sel", s, s + 1), Op.add, 0.0, Op.max)
        fill(v("cBIG", r=1), BIG)
        for name, n in (("RS4", 4), ("RS6", 6)):
            fill(v(name), -1.0)
            fill(v(name, 0, 64 * n, n), 4 * BIG)

    def mining_constants():
        fill(v("c1280"), -1280.0)
        fill(v("cP", r=2), -1280.0 * 32768)
        ts(v("cP", r=1), v("cS", r=1), -2048.0, Op.mult, 2048.0, Op.add)
        fill(v("mats", COLS["BD0"][1], COLS["I11"][1] + 128), 0.0)
        for name, src, froms, tos in HALVES:
            for j in froms:
                for x in tos:
                    o, a = v(name, 64 * x, 64 * x + 64, **half(j)), v(src, 64 * j, 64 * j + 64, **half(j))
                    dma(o[0], a[0], [o], [a], "d" + name)
        fill(v("d0"), 0.25)
        fill(v("d1"), 0.0)
        scan(v("THR"), v("d0"), v("d1"), 2.0, Op.mult, Op.add)
        ts(v("pj"), v("pi"), 6, Op.logical_shift_right)
        ts(v("rc"), v("pj"), 16.0, Op.mult, v("kc"), Op.add)
        ts(v("OH"), v("io"), v("rc"), Op.is_equal)
        pick("p4d", v("THR", 0, 32))
        ts(v("W4D"), v("BD2"), v("p4d"), Op.mult, -0.5, Op.mult)
        for x in range(2):
            ts(v("d1", 16 * x, 16 * x + 16), v("io", 0, 16), v("kc"), Op.not_equal, 1024.0, Op.mult)
        tt(v("THM", 0, 32), v("THR"), v("d1"), Op.max)
        for x in (32, 64, 128):
            gcp(v("THM", x, 2 * x), v("THM", 0, x))
        fill(v("RS16"), 1.0)
        fill(v("RS16", 0, 256, 16), 0.0)
        fill(v("RSL"), -1.0)
        fill(v("RSL", 0, 48, 3), 0.0)
        fill(v("RSL", 1, 48, 3), -2.0 ** 80)
        ts(v("PT", 0, 16), v("io", 0, 16), 16.0, Op.mult, 2048.0, Op.add)
        for h in range(2):
            ts(v("LW%d" % h, 61, 800, 48), v("PT", 0, 16), v("kc"), Op.add)

    def visit(t, h, lists=None):
        def s(name, *a, **k):
            return v("%s%d" % (name, h), *a, **k)

        def s4(name, a=0, b=128, which=None):
            return v4("%s%d%d" % (name, h, t), t, a, b, which)

        def bank(i, lo, hi, st=1, **k):
            return v("b%d%d" % (h, i), lo, hi, st, **k)

        def nodes(a, b, m0, m1):
            return vx(T["c16%d" % h][:, a:b, m0:m1], "c16%d" % h, 6 * a, 6 * b, (m1 - m0) * (b - a))

        X, w = s("X", 0, 2048), 2 << t
        sv = SPLITS.get((t, h), SPLIT)
        cut = min(128 - LAST, sv + 64)
        chunks = [(0, sv, 1), (sv, cut, 3), (cut, 128, 2)]

        def prep(a, b):
            n = b - a
            raw = t and not lists
            F, Z = s4("F", a, b), s4("F", 128 + a, 128 + b) if raw else s4("Z", a, b)
            if raw:
                line("Z", s4("Z"), s4("F", 128, 256), 1.0, -1280.0)
            top = [(s("W2"), v("c1280", 0, n))] if raw else []
            U, S, V = bank(2, 0, n), bank(2, n, 2 * n), bank(2, 2 * n, 3 * n)
            mms(U, *top, (s("W2"), Z))
            mms(S, (v("BD"), Z))
            line("Hu%d" % lists, s("Hu", a, b), U, 1 / 4096, 1279.5 + 1 / 4096)
            R = [bank(3, m * n, m * n + n) if m < 4 else bank(2, 3 * n, 4 * n) for m in range(5)]
            for m in range(4):
                mms(R[m], (v("RC", r=2), v("RM", 128 * m, 128 * m + n, r=2)), (times(32 << m), F))
            line("Hs", s4("Hs", a, b), S, 1 / 16, v("ks1" if raw else "ks0"))
            mms(V, (s("W2"), Z), *top, const("cU", n, 2), (times(-4096), s("Hu", a, b)))
            mms(R[4], (v("RC", r=2), v("RM", 512, 512 + n, r=2)), (times(512), F))
            tt(s("P", a, b), V, F, Op.mult)
            for m in range(5):
                q = s("Q", 128 * m + a, 128 * m + b)
                tt(q, R[m], s("P", a, b), Op.add)
                ts(s("C", 6 * a + m, 6 * b - 5 + m, 6), q, 5 + m, Op.logical_shift_right, 2047, Op.bitwise_and)
            lo = max(a, sv)
            (gcp if lists else cp)(s("off6", 6 * lo, 6 * b), s("C", 6 * lo, 6 * b))
            gcp(nodes(a, b, 0, 6), s("C", 6 * a, 6 * b))
            if a < lo:
                for m in range(5):
                    (gcp if m >= OVG else cp)(s("offV", m * sv, m * sv + sv), s("C", m, 6 * sv - 5 + m, 6))
                hi = -(-sv // 16) * 16
                for k in range(4):
                    gcp(s("Zy", k, 4 * hi - 3 + k, 4), s4("Z", 0, hi))
                for k in range(4):
                    gcp(s("Zx", k, 16 * sv - 3 + k, 4), s("Zy", 0, 4 * sv))

        def gather(a, b):
            zn = "Z%d%d" % (h, t)
            for i in range(max(a, sv), b):
                z = vx(T[zn][:, i // w, i % w // (w // 2), i % (w // 2):i % (w // 2) + 1], zn, i, i + 1, 1)
                actg(s("A", 80 * i, 80 * i + 80), X, s("off6", 6 * i, 6 * i + 5), Act.Abs, z)
                inturn()

            def one(o, f, z):
                vgather(lambda: g.vector.tensor_tensor(o[0], X[0].indirect(f[0]), z[0], Op.subtract), o, [X, f, z])
            n = sv
            for m in range(0 if a else 5):
                for x in range(VP[m]):
                    x, y = x * n // VP[m] // 2 * 2, (x + 1) * n // VP[m] // 2 * 2
                    one(s("A", 16 * (m * n + x), 16 * (m * n + y)), s("offV", m * n + x, m * n + y), s("Zx", 16 * x, 16 * y))
                for x in range(m * n, m * n + n, RP):
                    y = min(x + RP, m * n + n)
                    ts(s("RL", 16 * x, 16 * y), s("A", 16 * x, 16 * y), 0.0, Op.max)

        def choose(a, b, kb):
            n, own = b - a, a >= sv
            keys = bank(kb, 0, 5 * n)
            key = [bank(kb, m, 5 * n - 4 + m, 5) if own else bank(kb, m * n, m * n + n) for m in range(5)]
            if own:
                mm(keys, v("KC", r=2), v("MCS", 0, 5 * n, r=2), True, False)
                parts = max(1, n // SUB)
                for x in range(parts):
                    p, q = a + x * n // parts, a + (x + 1) * n // parts
                    if q == b:
                        mm(keys, v("I"), nodes(a, b, 0, 5), False, False)
                    for k in range(16):
                        mm(bank(kb, 5 * (p - a), 5 * (q - a)), place(10240, k), s("A", 80 * p + k, 80 * q - 15 + k, 16), False, k == 15 and q == b)
                scan(s("KS", 5 * a, 5 * b), v("RS5", 0, 5 * n), keys, 0.0, Op.max, Op.min)
            else:
                least = [s("KS", 5 * a + m, 5 * b - 4 + m, 5) for m in range(5)]
                for m0, m1 in PIECES:
                    mm(bank(kb, m0 * n, m1 * n), v("KC", r=2), v("MCV%d" % n, m0 * n, m1 * n, r=2), True, False)
                    for x, src in ((-10240, "A"), (20480, "RL")):
                        for k in range(16):
                            mm(bank(kb, m0 * n, m1 * n), place(x, k), s(src, 16 * n * m0 + k, 16 * n * m1 - 15 + k, 16), False, False)
                    for m in range(m0, m1):
                        mm(key[m], v("I"), nodes(a, b, m, m + 1), False, m == m1 - 1)
                    for m in range(m0, m1):
                        if m:
                            tt(least[m], key[m], least[m - 1], Op.min)
                        else:
                            ts(least[0], key[0], float(KN), Op.min)
            eq = [s("EQm", 128 * (m - 1) + a, 128 * (m - 1) + b) for m in range(1, 5)]
            for m in range(1, 5):
                tt(eq[m - 1], key[m], s("KS", 5 * a + 4, 5 * b, 5), Op.is_equal)
            at = bank(kb, 328, 328 + n)
            mms(at, (v("c160" if own else "c1", r=1), v("b1", 0, n, r=1)), *[(times(m * (32 if own else n)), eq[m - 1]) for m in range(1, 5)])
            ts(s("pos", a, b), at, 0.5 if own else 16.0, Op.mult, v("kc"), Op.add)
            win, top = s("A", 80 * a, 80 * b), col("top%d" % h)

            def second(f, near):
                vgather(lambda: g.vector.tensor_scalar(near[0], win[0].indirect(f[0]), top[0], 2.0, Op.is_le, Op.mult), near, [win, f, top])
            mid = min(b, a + BYS) if a == sv else a
            if own:
                for x in range(a, mid, NS):
                    y = min(x + NS, mid)
                    actg(s("NR", 16 * x, 16 * y), win, s("pos", x, y), Act.Sign, top)
                    if (t, h) not in FREE:
                        inturn()
                for x in range(mid, b, NP):
                    y = min(x + NP, b)
                    second(s("pos", x, y), s("NR", 16 * x, 16 * y))
            else:
                actg(s("NA", 0, 16 * n), win, s("pos", a, b), Act.Abs)
                if (t, h) not in FREE:
                    inturn()
                ts(s("NR", 16 * a, 16 * b), s("NA", 0, 16 * n), top, Op.is_le, 2.0, Op.mult)
                mm(bank(0, 384, 512), v("I"), s4("F"), True, False)
            for x, y, name in ((a, mid, "c2k"), (mid, b, "c34k")):
                if x < y:
                    mm(bank(0, 384 + x, 384 + y), *const(name, y - x), False, False)
            join = JOIN and (t, h) not in FREE
            if own or not join:
                x = 0 if join and a == sv else a
                for k in range(16):
                    mm(bank(0, 384 + x, 384 + b), place(-2048, k), s("NR", 16 * x + k, 16 * b - 15 + k, 16), False, b == 128 and k == 15)

        def meeting():
            c = 64
            ts(s("Cc"), s("KS", 4, 640, 5), 2047, Op.bitwise_and)
            tt(s4("KI"), bank(0, 384, 512), s("Cc"), Op.max)
            for x in range(2):
                ts(s("SJi", x * c, x * c + c), s4("KI", which=x), 2047, Op.bitwise_and)
            ts(s("Hh"), s("SJi"), 0.125, Op.mult, 1279.5625, Op.add)
            gcp(s("SJ"), s("SJi"))
            S, J, HS, HJ = s("SJ", 0, c), s("SJ", c, 2 * c), s("Hh", 0, c), s("Hh", c, 2 * c)
            eq = [s("EQ2", l * c, l * c + c) for l in range(16)]
            for r in range(2):
                for l in range(8):
                    mms(bank(2 + r, l * c, l * c + c), (v("B%d" % (8 * r + l)), HS))
                for l in range(8):
                    tt(eq[8 * r + l], bank(2 + r, l * c, l * c + c), HJ, Op.is_equal)
            G, XP = (bank(0, c * i, c * i + c) for i in range(2))
            ML, JL, JH = (bank(1, c * i, c * i + c) for i in range(3))
            MT, S32, UJ = (bank(2, c * i, c * i + c) for i in (4, 5, 6))
            mms(S32, const("c32", c), (v("I"), S))
            mms(UJ, (s("W32"), s4("Z", which=1)))
            tt(s("JS"), S32, J, Op.mult)
            tt(s("JQ"), UJ, s("JS"), Op.add)
            ts(s("Jn"), s("JQ"), 5, Op.logical_shift_right, 2047, Op.bitwise_and)
            mms(G, *[(v("TRI"), eq[l]) for l in range(16)])
            mms(ML, *[(v("MS%d" % l), eq[l]) for l in range(16)])
            ts(s("mj"), G, 0.0, Op.is_gt)
            ts(s("ms"), ML, 0.0, Op.is_le)
            mms(XP, (v("BN"), s("mj")), (times(-1, "BD"), s("ms")))
            mms(JL, (v("I"), J), (times(-BIG), s("mj")))
            mms(JH, (v("I"), J), (times(BIG), s("mj")))
            ts(s("oha"), XP, v("kn"), Op.is_equal)
            ts(s("ohb"), XP, v("km"), Op.is_equal)
            tt(s("t1"), JL, s("Jn"), Op.max)
            tt(s4("FO", which=1), JH, s("t1"), Op.min)
            for x in range(4):
                mms(bank(2, x, 4 * c - 3 + x, 4), (v("PA%d" % x), s("oha")), (v("PA%d" % x), s("ohb")), (turn(4 * x), J))
            scan(s("T1"), v("RS4"), bank(2, 0, 4 * c), 0.0, Op.max, Op.min)
            if t < 3:
                mms(MT, (v("S15"), s("mj")))
                red(v("metc", 2 * t + h, 2 * t + h + 1), MT)
            mms(bank(3, 4, 6 * c - 1, 6), const("cBIG", c), (v("I"), S), (times(-BIG), s("ms")), (times(-BIG, "NOK"), s("oha")))
            PEN = [bank(3, 5, 6 * c, 6), bank(0, 6 * c, 7 * c)]
            for x in range(2):
                mms(PEN[x], const("cP", c, 2), (times(32768), s4("Hs", which=x)), (times(-2048, "BD"), s4("Z", which=x)))
            for x in range(4):
                mms(bank(3, x, 6 * c - 5 + x, 6), (times(BIG), s("ms")), (v("PN%d" % x), s("oha")), (v("PB%d" % x), s("ohb")),
                    (turn(x), s("T1", 3, 4 * c, 4)))
            tt(s("Fj"), PEN[1], s4("FO", which=1), Op.min)
            scan(s("T2"), v("RS6"), bank(3, 0, 6 * c), 0.0, Op.max, Op.min)
            gcp(s4("FO", which=0), s("T2", 4, 6 * c, 6))

        def send(what, a):
            dst = T.cores[(rank + NEXT) % nrank]
            rid, pid = topo.addr(dst, core)
            es = topo.engines(core, dst)[:8]
            name = "%s%d%d" % (what, h, t + 1)
            src, land = s4("FO", a, a + 128), v4("F%d%d" % (h, t + 1), t + 1, a, a + 128)

            def call():
                g.remote_dma(out_ap=land[0], in_ap=src[0], remote_sem=T.sem["r" + name], local_sem=T.sem["loc"],
                             pid=pid, routing_id=rid, dma_engine_mask=sum(1 << e for e in es))
            me = op("g", call, [], [src], 0.4, "loc", len(es))
            ops.append(["r", None, WIRE, {me: False}, "r" + name, len(topo.engines(T.cores[(rank - NEXT) % nrank], core)[:8])])
            mark(land, True, len(ops) - 1)

        def store(out, name, sem):
            for j in range(2):
                src = s(name, r=64 * j + 64, p=64 * j)
                dma(out[64 * h:64 * h + 64, 128 * j:128 * j + 128], src[0], [], [src], "%s%d" % (sem, h))

        def veins():
            OL = bank(1, 288, 296)
            terms = []
            for q in sorted(range(16), key=lambda q: -(q % w // (w // 2))):
                pair = q // w * (w // 2) + q % (w // 2)
                terms.append((place(1, q), s("Fj", pair, 64, 8) if q % w // (w // 2) else s("T2", 6 * pair + 5, 384, 48)))
            mms(OL, *terms)
            ts(s("Ol", 0, 8), OL, REST, Op.add)
            line("Of", s("Of"), OL, 1.0, REST)
            y, f, z = s("Y"), s("Ol", 0, 8), s("Z2")
            gcp(z, s4("Z"))
            vgather(lambda: g.vector.tensor_tensor(y[0], X[0].indirect(f[0]), z[0], Op.add), y, [X, f, z])
            ts(s4("FO", 128, 256), y, 0.5, Op.mult, 1279.75, Op.add)
            if t < 3:
                send("F", 0)
                send("Z", 128)
            else:
                ts(s("Zo"), s4("FO", 128, 256), -1280.0, Op.add)
                gcp(s("yo"), s4("FO"))
                store(T.yf, "yo", "oF")
                store(T.yz, "Zo", "oZ")

        def mining():
            ew = "EQW%d" % h
            RR, CN, OA = bank(1, 0, 256), bank(0, 256, 512), bank(1, 256, 280)
            line("zq", s("zq"), s4("Z"), -1.25, -1279.625)
            for x, src in ((1, ("Fj",)), (0, ("T2", 5, 384, 6))):
                for j in range(2):
                    mms(bank(0, 128 * x + 64 * j, 128 * x + 64 * j + 64), (v("BD%d" % j), s(*src)))
            for x in range(2):
                line("Er", s4("Er", 0, 256, x), bank(0, 128 * x, 128 * x + 128), -1.0, -REST)
            for j in range(2):
                mms(bank(1, 256 + 8 * j, 264 + 8 * j), (v("I%d" % j), s("Of")))
                mms(bank(1, 272 + 4 * j, 276 + 4 * j), *[(v("I%d%d" % (j, x)), s("Of", x, 7 + x, 2)) for x in range(2)])
            ts(s("LW", 77, 1184, 48), OA, -1.0, Op.mult)
            mm(CN, v("I"), v("THM"), True, False)
            for c in range(8):
                ts(vx(T[ew][:, c, 0:256 - 32 * c], ew, 256 * c, 256 * c + 256 - 32 * c, 256 - 32 * c), s4("Er", 32 * c, 256), s("LW", 845 + 48 * c, 846 + 48 * c), Op.is_equal)
                if c < 7:
                    mm(bank(0, 288 + 32 * c, 512), times(-1, "BD2"), vx(T[ew][:, c, 32:256 - 32 * c], ew, 256 * c + 32, 256 * c + 256, 224 - 32 * c), False, False)
                mm(bank(0, 256 + 32 * c, 288 + 32 * c), v("W4D"), vx(T[ew][:, c, 0:32], ew, 256 * c, 256 * c + 32, 32), False, c == 7)
            for j in range(2):
                mms(bank(1, 128 * j, 128 * j + 128), (v("I%d" % j), s("zq")), (v("I%d" % j), s("Y")))
            if t >= R2S:
                act(s("R2"), RR, Act.Relu, bias=1280.0)
            else:
                ts(s("R2"), RR, 1280.0, Op.add, 0.0, Op.max)
            scan(s("LW", 0, 768, 3), v("RS16"), CN, 0.0, Op.mult, Op.min)
            scan(s("LO"), v("RSL"), s("LW", 45, 800, 16), 0.0, Op.mult, Op.min)
            ts(s("Ls"), s("LO", 2, 48, 3), -1.0, Op.mult)
            XW, ls, r2 = s("X"), s("Ls"), s("R2")
            op("v", lambda: g.vector.tensor_copy(XW[0].indirect(ls[0]), r2[0]), [XW], [ls, r2], 0.05 + 256 * 3.8 * CYC)

        if lists is not None:
            prep(*PREP[lists])
            return
        if t == 0:
            visit(t, h, 0)
            visit(t, h, 1)
            if h == 0:
                x = len(ops)
                key_constants()
                due.update((i, SOON) for i in range(x, len(ops)))
                meeting_constants()
                mining_constants()
            cp(col("top%d" % h), col("limf%d" % h))
        else:
            if h == 0:
                red(v("mets"), v("metc", 2 * t - 2, 2 * t))
                cp(v("meti"), v("mets"))
                ts(v("mete"), v("meti"), 3, Op.bitwise_and)
            tt(col("top%d" % h), col("limf%d" % h), v("mete"), Op.add)
        for a, b, kb in chunks:
            gather(a, b)
        for ch in chunks:
            choose(*ch)
        meeting()
        veins()
        if t < 3:
            visit(t + 1, h, 0)
        mining()
        if t < 3:
            visit(t + 1, h, 1)
        else:
            src = s("X", 0, 2048, r=64)
            dma(T.yx[64 * h:64 * h + 64, :], src[0], [], [src], "oX%d" % h)
            due[len(ops) - 1] = 0.0 if h else AHEAD

    loads(0)
    loads(1)
    list_constants()
    for h in range(2):
        stream_constants(h)
    for t in range(4):
        for h in range(2):
            visit(t, h)

    every = list(range(len(ops)))
    hold = [{"r": 0.0, "y": 0.1}.get(o[0], o[2]) for o in ops]
    after, before = [[] for _ in ops], [[] for _ in ops]
    for j, o in enumerate(ops):
        for i, wait in o[3].items():
            lag = ops[i][2] + WAKE if wait else (ops[i][2] if o[0] == "r" else hold[i])
            after[i].append((j, lag))
            before[j].append((i, lag + hold[j] - hold[i]))

    def fit(key, follow, lead, early):
        left = [len(x) for x in lead]
        free = {o[0]: [] for o in ops}
        ready, at, turn = sorted(((key[i], i) for i in every if not left[i]), reverse=True), [0.0] * len(ops), []
        while ready:
            i = ready.pop()[1]
            start, taken = early[i], free[ops[i][0]]
            x = len(taken)
            while x and taken[x - 1][0] > start:
                x -= 1
            if x and taken[x - 1][1] > start:
                start = taken[x - 1][1]
            while x < len(taken) and start + hold[i] > taken[x][0] + SLACK:
                start = taken[x][1]
                x += 1
            if x and taken[x - 1][1] >= start:
                taken[x - 1][1] = start + hold[i]
            else:
                taken.insert(x, [start, start + hold[i]])
                x += 1
            if x < len(taken) and taken[x - 1][1] >= taken[x][0]:
                taken[x - 1][1] = max(taken[x - 1][1], taken[x][1])
                del taken[x]
            at[i] = start
            turn.append(i)
            for j, lag in follow[i]:
                left[j] -= 1
                if early[j] < start + lag:
                    early[j] = start + lag
                if not left[j]:
                    new, a, b = (key[j], j), 0, len(ready)
                    while a < b:
                        if ready[(a + b) // 2] > new:
                            a = (a + b) // 2 + 1
                        else:
                            b = (a + b) // 2
                    ready.insert(a, new)
        return at, turn

    def again(at):
        back, turn = fit([-at[i] - hold[i] for i in every], before, after, [o[2] - hold[i] + due.get(i, 0.0) for i, o in enumerate(ops)])
        at, turn = fit([-back[i] - hold[i] for i in every], after, before, [0.0] * len(ops))
        return at, sorted(turn, key=lambda i: at[i])

    def length(order):
        total = 0.0
        for (gath, fixed, wake, wire, slow), cost in zip(CASES, costs):
            now, done = {o[0]: 0.0 for o in ops}, [0.0] * len(ops)
            for i in order:
                q = ops[i][0]
                start = now[q]
                for j in waits[i]:
                    if done[j] > start:
                        start = done[j]
                done[i] = start + cost[i] + wake
                now[q] = start + cost[i] if q in semof else (start + 0.1 if q == "y" else 0.0)
            total += max(done)
        return total / len(CASES)

    if not ORDER:
        waits = [[j for j, wait in o[3].items() if wait or o[0] == "r"] for o in ops]
        costs = [[wire - wake if o[0] == "r" else fixed * o[2] + picks[i] * (gath - fixed * GATH) * CYC if i in picks else o[2] * slow.get(o[0], 1)
                  for i, o in enumerate(ops)] for gath, fixed, wake, wire, slow in CASES]
        way = [0.0] * len(ops)
        for i in every[::-1]:
            way[i] = max([ops[i][2] + due.get(i, 0.0)] + [lag + way[j] for j, lag in after[i]])
        at, turn = fit([-x for x in way], after, before, [0.0] * len(ops))
        best, seed = None, SEED
        for x in range(ROUNDS + TRIES):
            if x >= ROUNDS:
                at, seed = list(now[1]), (seed * 1103515245 + 12345) % (1 << 31)
                lo, size = seed % 1000 / 1000 * (max(at) + STRETCH) - STRETCH, SHAKE[x % len(SHAKE)]
                for i in every:
                    if lo < at[i] < lo + STRETCH:
                        seed = (seed * 1103515245 + 12345) % (1 << 31)
                        at[i] += size * ((seed >> 8) % 2001 / 1000 - 1)
            at, order = again(at)
            end = length(order)
            if best is None or end < now[0] + WORSE * (1 - x / (ROUNDS + TRIES)):
                now = (end, at, order)
            if best is None or end < best[0]:
                best = now
        ORDER.append(best)
    end, at, order = ORDER[0]

    count, know, value, clocks = {}, {o[0]: {} for o in ops}, {}, {}
    for i in order:
        q, call, cost, deps, sem, inc = ops[i]
        k = know[q]
        latest = {}
        for j, wait in deps.items():
            if wait and (ops[j][4] not in latest or value[latest[ops[j][4]]] < value[j]):
                latest[ops[j][4]] = j
        for j in sorted(latest.values(), key=lambda j: -len(clocks[j])):
            if k.get(ops[j][4], 0) < value[j]:
                eng[q].wait_ge(T.sem[ops[j][4]], value[j])
                for x, y in clocks[j].items():
                    if k.get(x, 0) < y:
                        k[x] = y
        count[sem] = value[i] = count.get(sem, 0) + inc
        clocks[i] = {sem: value[i]}
        if q != "r":
            r = call()
            if r is not None:
                r.then_inc(T.sem[sem], inc)
            clocks[i] = dict(k)
            clocks[i][sem] = value[i]
    for x in SEMAPHORES:
        if count.get(x):
            g.wait_ge(T.sem[x], count[x])
